import numpy as np
import ml_dtypes


def mxq(x, axis, fmt="e4m3"):
    dtype, down = {"e4m3": (ml_dtypes.float8_e4m3fn, 7), "e5m2": (ml_dtypes.float8_e5m2, 14)}[fmt]
    v = np.moveaxis(np.asarray(x, np.float32).astype(ml_dtypes.bfloat16).astype(np.float64), axis, -1)
    blocks = v.reshape(v.shape[:-1] + (-1, 32))
    amax = np.abs(blocks).max(-1, keepdims=True)
    byte = np.maximum(np.where(amax > 0, np.frexp(amax)[1] - 1 + 127, 0) - down, 1)
    scale = np.exp2(byte - 127.0)
    codes = (blocks / scale).astype(np.float32).astype(dtype).astype(np.float64)
    return np.moveaxis((codes * scale).reshape(v.shape), -1, axis)


WIDE = False


def mx_kscale(k):
    if not WIDE:
        return np.ones(k)
    levels = np.array([10, -10, 5, -5, 0])
    if k % 512:
        return np.exp2(np.random.permutation(np.resize(levels, k // 32))).repeat(32)
    a = np.empty((k // 512, 16))
    for p in range(k // 512):
        a[p, :8] = np.random.permutation(np.resize(levels, 8))
        for g in range(8):
            far = levels[np.abs(levels - a[p, g]) >= 10]
            a[p, g + 8] = far[np.random.randint(len(far))]
    return np.exp2(a.ravel()).repeat(32)


def f64(x):
    return np.asarray(x).astype(np.float64)


def striped(idx):
    return np.tile(idx.reshape(-1, 16).T, (8, 1)).astype(np.uint16)


def unstriped(offs):
    return offs[:16].T.reshape(-1).astype(np.int64)


E2M1 = np.array([0.0, 0.5, 1.0, 1.5, 2.0, 3.0, 4.0, 6.0, -0.0, -0.5, -1.0, -1.5, -2.0, -3.0, -4.0, -6.0])


def pack_weight(w, fmt):
    k, n = w.shape
    w = f64(np.asarray(w, np.float32).astype(ml_dtypes.bfloat16)).reshape(k // 32, 32, n)
    amax = np.abs(w).max(1)
    if fmt == "e4m3":
        byte = np.frexp(amax)[1] - 1 + 127 - 7
    else:
        mant, ex = np.frexp(amax / 6.0)
        byte = np.where(mant > 0.5, ex, ex - 1) + 127
    byte = np.clip(np.where(amax > 0, byte, 1), 1, 254)
    scaled = (w * np.exp2(127.0 - byte)[:, None, :]).reshape(k, n).astype(np.float32)
    by_word = np.ascontiguousarray(scaled.reshape(k // 512, 128, 4, n).transpose(0, 1, 3, 2))
    if fmt == "e4m3":
        words = by_word.astype(ml_dtypes.float8_e4m3fn).view(np.uint8)
    else:
        c = by_word.astype(ml_dtypes.float4_e2m1fn).view(np.uint8) & 0xF
        words = (c[..., 0::2] | (c[..., 1::2] << 4)).reshape(k // 512, 128, 2 * n)
    return np.ascontiguousarray(words), np.ascontiguousarray(byte.astype(np.uint8).reshape(k // 512, 16, n))


def unpack_weight(words, scales, fmt):
    g, _, n = scales.shape
    words = np.ascontiguousarray(words).reshape(g, 128, n, -1)
    if fmt == "e4m3":
        vals = words.view(ml_dtypes.float8_e4m3fn).astype(np.float64)
    else:
        nib = np.empty((g, 128, n, 4), np.uint8)
        nib[..., 0::2] = words & 0xF
        nib[..., 1::2] = words >> 4
        vals = E2M1[nib]
    vals = vals * np.repeat(np.exp2(scales.astype(np.float64) - 127.0), 8, axis=1)[..., None]
    return vals.transpose(0, 1, 3, 2).reshape(g * 512, n)


K, M, T, S = 1024, 1024, 4096, 1536


def setup_inputs():
    n = np.random.standard_normal
    s = mx_kscale(K)[:, None]
    u = mx_kscale(512)[:, None]
    v = pack_weight(n((K, T)) * s, "e4m3")
    p_w4 = pack_weight(n((K, M)) / np.sqrt(K) / s, "e2m1")
    return {
        "tab_words": v[0],
        "tab_scales": v[1],
        "w4_words": p_w4[0],
        "w4_scales": p_w4[1],
        "down": (n((K, 512)) / np.sqrt(K) / s * u.T).astype(np.float32),
        "up": (0.5 * n((512, M)) / np.sqrt(512) / u).astype(np.float32),
        "ts": np.tile(np.exp(0.5 * n(T)), (128, 1)).astype(np.float32),
        "b": (0.3 * n(1024)).astype(np.float32),
        "offs": striped(np.random.permutation(T)[:S]),
    }


def reference(tab_words, tab_scales, w4_words, w4_scales, down, up, ts, b, offs):
    tab_ = unpack_weight(tab_words, tab_scales, "e4m3")[:, unstriped(offs)]
    w4_ = unpack_weight(w4_words, w4_scales, "e2m1")
    down_ = mxq(f64(down), 0, "e4m3")
    up_ = mxq(f64(up), 0, "e4m3")
    h_ = mxq(down_.T @ tab_, 0, "e4m3")
    y = w4_.T @ tab_ + up_.T @ h_
    y = y * f64(ts)[0][unstriped(offs)]
    return y + f64(b)[:, None]

@@ -1,0 +1,272 @@
+from contextlib import ExitStack
+
+import concourse.mybir as mybir
+from concourse.masks import make_identity
+
+K, M, T, S, R = 1024, 1024, 4096, 1536, 512
+FLOPS = 2 * S * (K * M + K * R + R * M)
+
+F32 = mybir.dt.float32
+BF16 = mybir.dt.bfloat16
+I32 = mybir.dt.int32
+U32 = mybir.dt.uint32
+U16 = mybir.dt.uint16
+U8 = mybir.dt.uint8
+FP8X4 = mybir.dt.float8_e4m3fn_x4
+FP4X4 = mybir.dt.float4_e2m1fn_x4
+MULT = mybir.AluOpType.mult
+IDENT = mybir.ActivationFunctionType.Identity
+
+P = 128
+PACK = 4
+PASSES = K // (P * PACK)
+CHUNK = 512
+CHUNKS = S // CHUNK
+SUB = 128
+N_TILES = M // P
+BANKS = 8
+Y_BANKS = 5
+H_BANKS = BANKS - Y_BANKS
+UP_COLS = 512
+HALF = R // 2
+
+
+def tile_list_tabts_bias_kernel(
+    tc, tab_words, tab_scales, w4_words, w4_scales, down, up, ts, b, offs, out
+):
+    nc = tc.nc
+    with ExitStack() as ctx:
+        keep = ctx.enter_context(tc.tile_pool(name="keep", bufs=1))
+        stage = ctx.enter_context(tc.tile_pool(name="stage", bufs=6))
+        psum = ctx.enter_context(tc.psum_pool(name="psum", bufs=1))
+
+        offsets = keep.tile([P, S // 16], U16, name="offsets")
+        nc.sync.dma_start(offsets[:], offs)
+        w4 = keep.tile([P, PASSES, M // 2], I32, name="w4", align_bytes=64)
+        w4_src = w4_words.bitcast(I32).rearrange("a p w -> p a w")
+        early = Y_BANKS * P // 2
+        nc.sync.dma_start(w4[:, :, :early], w4_src[:, :, :early])
+
+        tab_plane = keep.tile([P, T // 4], I32, name="tab_plane", align_bytes=64)
+        nc.vector.memset(tab_plane[:], 0)
+        for q in range(4):
+            nc.sync.dma_start(
+                tab_plane[32 * q : 32 * q + 8, :],
+                tab_scales[:, 4 * q : 4 * q + 4, :].bitcast(I32),
+            )
+        ts_row = keep.tile([P, T // P], F32, name="ts_row")
+        nc.sync.dma_start(ts_row[:], ts[0].rearrange("(q c) -> q c", q=P))
+        identity = keep.tile([P, P], F32, name="identity")
+        make_identity(nc, identity[:])
+        w4_plane = keep.tile([P, PASSES, M // 4], I32, name="w4_plane", align_bytes=64)
+        nc.gpsimd.memset(w4_plane[:], 0)
+        moved = keep.tile([P, S // 4], I32, name="moved", align_bytes=64)
+        nc.gpsimd.memset(moved[:], 0)
+
+        tab = [keep.tile([P, T], I32, name="tab%d" % a, align_bytes=64) for a in range(PASSES)]
+
+        def load_tab(a):
+            nc.sync.dma_start(tab[a][:], tab_words[a].rearrange("p t i -> p (t i)").bitcast(I32))
+
+        load_tab(0)
+        for q in range(4):
+            nc.sync.dma_start(
+                w4_plane[32 * q : 32 * q + 4],
+                w4_scales[:, 4 * q : 4 * q + 4, :].bitcast(I32).rearrange("a r n -> r a n"),
+            )
+        load_tab(1)
+        picked = keep.tile([P, S], U8, name="picked", align_bytes=64)
+        nc.vector.tensor_copy(picked[:], tab_plane[:].bitcast(U8).indirect(offsets[:]))
+        for q in range(4):
+            nc.sync.dma_start(
+                moved[32 * q : 32 * q + 4, :], picked[32 * q + 4 : 32 * q + 8, :].bitcast(I32)
+            )
+        down_raw = {}
+        for a in range(PASSES):
+            for u in range(2):
+                raw = keep.tile([P, PACK, HALF], F32, name="down_raw%d%d" % (a, u))
+                rows = down[a * P * PACK : (a + 1) * P * PACK, u * HALF : (u + 1) * HALF]
+                nc.sync.dma_start(raw[:], rows.rearrange("(p j) r -> p j r", j=PACK))
+                down_raw[a, u] = raw
+        up_raw = []
+        for g in range(M // UP_COLS):
+            raw = keep.tile([P, PACK, UP_COLS], F32, name="up_raw%d" % g)
+            cols = up[:, g * UP_COLS : (g + 1) * UP_COLS]
+            for t in range(PACK):
+                nc.sync.dma_start(raw[:, t, :], cols.rearrange("(g t i) n -> t g i n", t=PACK, i=8)[t])
+            up_raw.append(raw)
+        nc.sync.dma_start(w4[:, :, early:], w4_src[:, :, early:])
+        bias = keep.tile([P, N_TILES], F32, name="bias")
+        with nc.allow_non_contiguous_dma(reason="one bias value to a partition"):
+            nc.sync.dma_start(bias[:], b.rearrange("(i p) -> p i", p=P))
+
+        ts_all = keep.tile([P, T], F32, name="ts_all")
+        ts_view = ts_all[:].rearrange("p (q c) -> p q c", q=P)
+        for c0 in range(0, T // P, 4):
+            bank = psum.tile([P, 4, P], F32, name="bank%d" % (c0 // 4))
+            for j in range(4):
+                column = ts_row[:, c0 + j : c0 + j + 1].to_broadcast([P, P])
+                nc.tensor.transpose(bank[:, j, :], column, identity[:])
+            nc.scalar.copy(ts_view[:, :, c0 : c0 + 4], bank[:].rearrange("p j q -> p q j"))
+
+        v_codes, v_scales, ts_cols = {}, {}, {}
+
+        def entries(c):
+            return offsets[:, c * CHUNK // 16 : (c + 1) * CHUNK // 16]
+
+        for c in range(CHUNKS):
+            v_scales[0, c] = picked[:, c * CHUNK : (c + 1) * CHUNK]
+            v_scales[1, c] = moved[:].bitcast(U8)[:, c * CHUNK : (c + 1) * CHUNK]
+
+        def gather_codes(a, c):
+            t = keep.tile([P, CHUNK], U32, name="v_codes%d%d" % (a, c), align_bytes=64)
+            nc.vector.tensor_copy(t[:], tab[a][:].bitcast(U32).indirect(entries(c)))
+            v_codes[a, c] = t
+
+        def gather_ts(c):
+            t = keep.tile([P, CHUNK], F32, name="ts_cols", bufs=2)
+            nc.vector.tensor_copy(t[:], ts_all[:].indirect(entries(c)))
+            ts_cols[c] = t
+
+        y_bank = {}
+
+        def w4_pass(i, c, a):
+            if a == 0:
+                y_bank[i, c] = psum.tile([P, CHUNK], F32, name="bank%d" % (len(y_bank) % BANKS))
+            nc.tensor.matmul_mx(
+                out=y_bank[i, c][:],
+                lhsT=w4[:, a, :].bitcast(U8)[:, 2 * P * i : 2 * P * (i + 1)].bitcast(FP4X4),
+                lhsT_scale=w4_plane[:, a, :].bitcast(U8)[:, P * i : P * (i + 1)],
+                rhs=v_codes[a, c][:].bitcast(FP8X4),
+                rhs_scale=v_scales[a, c],
+                start=(a == 0),
+                stop=False,
+            )
+
+        down_bf = [
+            keep.tile([P, PACK, P, PACK], BF16, name="down_bf%d" % a, align_bytes=64)
+            for a in range(PASSES)
+        ]
+        down_codes = keep.tile([P, PASSES, R], U32, name="down_codes", align_bytes=64)
+        down_scales = keep.tile([P, PASSES, R], U8, name="down_scales", align_bytes=64)
+
+        def round_down(copy, a, u, t0, t1):
+            src = down_raw[a, u][:].rearrange("p j (g t i) -> p t g i j", t=PACK, i=8)
+            for t in range(t0, t1):
+                dst = down_bf[a][:, t, u * P // 2 : (u + 1) * P // 2, :]
+                copy(dst.rearrange("p (g i) j -> p g i j", i=8), src[:, t])
+
+        def quantize_down(a, t0, t1):
+            nc.vector.quantize_mx(
+                out=down_codes[:, a, t0 * P : t1 * P].bitcast(FP8X4),
+                scales=down_scales[:, a, t0 * P : t1 * P],
+                in_=down_bf[a][:, t0:t1].rearrange("p t m j -> p (t m j)"),
+            )
+
+        up_bf = keep.tile([P, M, PACK], BF16, name="up_bf", align_bytes=64)
+        up_codes = keep.tile([P, M], U32, name="up_codes", align_bytes=64)
+        up_scales = keep.tile([P, M], U8, name="up_scales", align_bytes=64)
+
+        def round_up(g):
+            cols = slice(g * UP_COLS, (g + 1) * UP_COLS)
+            nc.vector.tensor_copy(up_bf[:, cols, :], up_raw[g][:].rearrange("p j n -> p n j"))
+
+        def quantize_up(g):
+            cols = slice(g * UP_COLS, (g + 1) * UP_COLS)
+            nc.vector.quantize_mx(
+                out=up_codes[:, cols].bitcast(FP8X4),
+                scales=up_scales[:, cols],
+                in_=up_bf[:, cols, :].rearrange("p n j -> p (n j)"),
+            )
+
+        h_bf = keep.tile([P, S, PACK], BF16, name="h_bf", align_bytes=64)
+        h_codes = keep.tile([P, S], U32, name="h_codes", align_bytes=64)
+        h_scales = keep.tile([P, S], U8, name="h_scales", align_bytes=64)
+
+        def make_h(c):
+            for s0 in range(0, CHUNK, SUB):
+                turn = (c * CHUNK + s0) // SUB % H_BANKS
+                bank = psum.tile([P, PACK, SUB], F32, name="bank%d" % (Y_BANKS + turn))
+                for t in range(PACK):
+                    for a in range(PASSES):
+                        nc.tensor.matmul_mx(
+                            out=bank[:, t, :],
+                            lhsT=down_codes[:, a, t * P : (t + 1) * P].bitcast(FP8X4),
+                            lhsT_scale=down_scales[:, a, t * P : (t + 1) * P],
+                            rhs=v_codes[a, c][:, s0 : s0 + SUB].bitcast(FP8X4),
+                            rhs_scale=v_scales[a, c][:, s0 : s0 + SUB],
+                            start=(a == 0),
+                            stop=(a == PASSES - 1),
+                        )
+                j0 = c * CHUNK + s0
+                nc.scalar.copy(h_bf[:, j0 : j0 + SUB, :], bank[:].rearrange("p t n -> p n t"))
+
+        def quantize_h(c):
+            cols = slice(c * CHUNK, (c + 1) * CHUNK)
+            nc.vector.quantize_mx(
+                out=h_codes[:, cols].bitcast(FP8X4),
+                scales=h_scales[:, cols],
+                in_=h_bf[:, cols, :].rearrange("p n t -> p (n t)"),
+            )
+
+        def finish(i, c):
+            cols = slice(c * CHUNK, (c + 1) * CHUNK)
+            rows = slice(i * P, (i + 1) * P)
+            nc.tensor.matmul_mx(
+                out=y_bank[i, c][:],
+                lhsT=up_codes[:, rows].bitcast(FP8X4),
+                lhsT_scale=up_scales[:, rows],
+                rhs=h_codes[:, cols].bitcast(FP8X4),
+                rhs_scale=h_scales[:, cols],
+                start=False,
+                stop=True,
+            )
+            scaled = stage.tile([P, CHUNK], F32, name="scaled")
+            result = stage.tile([P, CHUNK], F32, name="result")
+            width = CHUNK // 2 if (i, c) == (N_TILES - 1, CHUNKS - 1) else CHUNK
+            for j0 in range(0, CHUNK, width):
+                part = slice(j0, j0 + width)
+                nc.vector.tensor_tensor(scaled[:, part], y_bank[i, c][:, part], ts_cols[c][:, part], MULT)
+                nc.scalar.activation(result[:, part], scaled[:, part], IDENT, bias=bias[:, i : i + 1])
+                nc.sync.dma_start(out[rows, c * CHUNK + j0 : c * CHUNK + j0 + width], result[:, part])
+
+        gather_codes(0, 0)
+        for i in range(Y_BANKS):
+            w4_pass(i, 0, 0)
+        gather_codes(1, 0)
+        for i in range(Y_BANKS):
+            w4_pass(i, 0, 1)
+
+        round_down(nc.scalar.copy, 0, 0, 0, PACK)
+        round_down(nc.scalar.copy, 0, 1, 0, PACK)
+        quantize_down(0, 0, PACK)
+        for u in range(2):
+            round_down(nc.vector.tensor_copy, 1, u, 0, 2)
+            round_down(nc.scalar.copy, 1, u, 2, PACK)
+        for t in range(PACK):
+            quantize_down(1, t, t + 1)
+
+        make_h(0)
+        for c in range(1, CHUNKS):
+            for a in range(PASSES):
+                gather_codes(a, c)
+            make_h(c)
+        quantize_h(0)
+        round_up(0)
+        gather_ts(0)
+        quantize_up(0)
+        round_up(1)
+        quantize_h(1)
+        quantize_up(1)
+        for i in range(Y_BANKS):
+            finish(i, 0)
+        gather_ts(1)
+        quantize_h(2)
+        for c in range(CHUNKS):
+            if c == 1:
+                gather_ts(2)
+            for i in range(N_TILES):
+                if (i, c) not in y_bank:
+                    for a in range(PASSES):
+                        w4_pass(i, c, a)
+                    finish(i, c)

@@ -1,7 +1,6 @@
 from contextlib import ExitStack
 
 import concourse.mybir as mybir
-from concourse.masks import make_identity
 
 K, M, T, S, R = 1024, 1024, 4096, 1536, 512
 FLOPS = 2 * S * (K * M + K * R + R * M)
@@ -44,24 +43,20 @@ def tile_list_tabts_bias_kernel(
         nc.sync.dma_start(offsets[:], offs)
         w4 = keep.tile([P, PASSES, M // 2], I32, name="w4", align_bytes=64)
         w4_src = w4_words.bitcast(I32).rearrange("a p w -> p a w")
-        early = Y_BANKS * P // 2
+        early = UP_COLS // 2
         nc.sync.dma_start(w4[:, :, :early], w4_src[:, :, :early])
 
         tab_plane = keep.tile([P, T // 4], I32, name="tab_plane", align_bytes=64)
         nc.vector.memset(tab_plane[:], 0)
         for q in range(4):
             nc.sync.dma_start(
-                tab_plane[32 * q : 32 * q + 8, :],
-                tab_scales[:, 4 * q : 4 * q + 4, :].bitcast(I32),
+                tab_plane[32 * q : 32 * q + 4, :], tab_scales[0, 4 * q : 4 * q + 4, :].bitcast(I32)
             )
-        ts_row = keep.tile([P, T // P], F32, name="ts_row")
-        nc.sync.dma_start(ts_row[:], ts[0].rearrange("(q c) -> q c", q=P))
-        identity = keep.tile([P, P], F32, name="identity")
-        make_identity(nc, identity[:])
+        nc.sync.dma_start(tab_plane[4:P:8, :], tab_scales[1].bitcast(I32))
         w4_plane = keep.tile([P, PASSES, M // 4], I32, name="w4_plane", align_bytes=64)
-        nc.gpsimd.memset(w4_plane[:], 0)
+        nc.vector.memset(w4_plane[:], 0)
         moved = keep.tile([P, S // 4], I32, name="moved", align_bytes=64)
-        nc.gpsimd.memset(moved[:], 0)
+        nc.vector.memset(moved[:], 0)
 
         tab = [keep.tile([P, T], I32, name="tab%d" % a, align_bytes=64) for a in range(PASSES)]
 
@@ -79,7 +74,7 @@ def tile_list_tabts_bias_kernel(
         nc.vector.tensor_copy(picked[:], tab_plane[:].bitcast(U8).indirect(offsets[:]))
         for q in range(4):
             nc.sync.dma_start(
-                moved[32 * q : 32 * q + 4, :], picked[32 * q + 4 : 32 * q + 8, :].bitcast(I32)
+                moved[32 * q : 32 * q + 4, :], picked[32 * q + 4 : 32 * q + 32 : 8, :].bitcast(I32)
             )
         down_raw = {}
         for a in range(PASSES):
@@ -88,26 +83,23 @@ def tile_list_tabts_bias_kernel(
                 rows = down[a * P * PACK : (a + 1) * P * PACK, u * HALF : (u + 1) * HALF]
                 nc.sync.dma_start(raw[:], rows.rearrange("(p j) r -> p j r", j=PACK))
                 down_raw[a, u] = raw
-        up_raw = []
-        for g in range(M // UP_COLS):
+        up_raw = {}
+
+        def load_up(g):
             raw = keep.tile([P, PACK, UP_COLS], F32, name="up_raw%d" % g)
             cols = up[:, g * UP_COLS : (g + 1) * UP_COLS]
             for t in range(PACK):
                 nc.sync.dma_start(raw[:, t, :], cols.rearrange("(g t i) n -> t g i n", t=PACK, i=8)[t])
-            up_raw.append(raw)
-        nc.sync.dma_start(w4[:, :, early:], w4_src[:, :, early:])
+            up_raw[g] = raw
+
+        load_up(0)
+        ts_all = keep.tile([P, T], F32, name="ts_all")
+        nc.sync.dma_start(ts_all[:], ts)
         bias = keep.tile([P, N_TILES], F32, name="bias")
         with nc.allow_non_contiguous_dma(reason="one bias value to a partition"):
             nc.sync.dma_start(bias[:], b.rearrange("(i p) -> p i", p=P))
-
-        ts_all = keep.tile([P, T], F32, name="ts_all")
-        ts_view = ts_all[:].rearrange("p (q c) -> p q c", q=P)
-        for c0 in range(0, T // P, 4):
-            bank = psum.tile([P, 4, P], F32, name="bank%d" % (c0 // 4))
-            for j in range(4):
-                column = ts_row[:, c0 + j : c0 + j + 1].to_broadcast([P, P])
-                nc.tensor.transpose(bank[:, j, :], column, identity[:])
-            nc.scalar.copy(ts_view[:, :, c0 : c0 + 4], bank[:].rearrange("p j q -> p q j"))
+        nc.sync.dma_start(w4[:, :, early:], w4_src[:, :, early:])
+        load_up(1)
 
         v_codes, v_scales, ts_cols = {}, {}, {}
 
@@ -124,7 +116,7 @@ def tile_list_tabts_bias_kernel(
             v_codes[a, c] = t
 
         def gather_ts(c):
-            t = keep.tile([P, CHUNK], F32, name="ts_cols", bufs=2)
+            t = keep.tile([P, CHUNK], F32, name="ts_cols%d" % c)
             nc.vector.tensor_copy(t[:], ts_all[:].indirect(entries(c)))
             ts_cols[c] = t
 
@@ -167,9 +159,9 @@ def tile_list_tabts_bias_kernel(
         up_codes = keep.tile([P, M], U32, name="up_codes", align_bytes=64)
         up_scales = keep.tile([P, M], U8, name="up_scales", align_bytes=64)
 
-        def round_up(g):
+        def round_up(copy, g):
             cols = slice(g * UP_COLS, (g + 1) * UP_COLS)
-            nc.vector.tensor_copy(up_bf[:, cols, :], up_raw[g][:].rearrange("p j n -> p n j"))
+            copy(up_bf[:, cols, :], up_raw[g][:].rearrange("p j n -> p n j"))
 
         def quantize_up(g):
             cols = slice(g * UP_COLS, (g + 1) * UP_COLS)
@@ -230,43 +222,43 @@ def tile_list_tabts_bias_kernel(
                 nc.scalar.activation(result[:, part], scaled[:, part], IDENT, bias=bias[:, i : i + 1])
                 nc.sync.dma_start(out[rows, c * CHUNK + j0 : c * CHUNK + j0 + width], result[:, part])
 
-        gather_codes(0, 0)
-        for i in range(Y_BANKS):
-            w4_pass(i, 0, 0)
-        gather_codes(1, 0)
-        for i in range(Y_BANKS):
-            w4_pass(i, 0, 1)
+        half = N_TILES // 2
+        order = [(i, c) for i0 in (0, half) for c in range(CHUNKS) for i in range(i0, i0 + half)]
+        for a in range(PASSES):
+            gather_codes(a, 0)
+            gather_codes(a, 1)
+            for i, c in order[:Y_BANKS]:
+                w4_pass(i, c, a)
 
         round_down(nc.scalar.copy, 0, 0, 0, PACK)
-        round_down(nc.scalar.copy, 0, 1, 0, PACK)
+        round_down(nc.vector.tensor_copy, 0, 1, 0, 2)
+        round_down(nc.scalar.copy, 0, 1, 2, PACK)
+        round_down(nc.vector.tensor_copy, 1, 0, 0, 2)
+        round_down(nc.scalar.copy, 1, 0, 2, PACK)
         quantize_down(0, 0, PACK)
-        for u in range(2):
-            round_down(nc.vector.tensor_copy, 1, u, 0, 2)
-            round_down(nc.scalar.copy, 1, u, 2, PACK)
+        round_down(nc.vector.tensor_copy, 1, 1, 0, 3)
+        round_down(nc.scalar.copy, 1, 1, 3, PACK)
         for t in range(PACK):
             quantize_down(1, t, t + 1)
 
         make_h(0)
-        for c in range(1, CHUNKS):
-            for a in range(PASSES):
-                gather_codes(a, c)
-            make_h(c)
+        make_h(1)
+        for a in range(PASSES):
+            gather_codes(a, 2)
+        make_h(2)
+        round_up(nc.vector.tensor_copy, 0)
         quantize_h(0)
-        round_up(0)
-        gather_ts(0)
         quantize_up(0)
-        round_up(1)
         quantize_h(1)
-        quantize_up(1)
-        for i in range(Y_BANKS):
-            finish(i, 0)
+        gather_ts(0)
         gather_ts(1)
         quantize_h(2)
-        for c in range(CHUNKS):
-            if c == 1:
+        for n, (i, c) in enumerate(order):
+            if n == Y_BANKS:
                 gather_ts(2)
-            for i in range(N_TILES):
-                if (i, c) not in y_bank:
-                    for a in range(PASSES):
-                        w4_pass(i, c, a)
-                    finish(i, c)
+                round_up(nc.scalar.copy, 1)
+                quantize_up(1)
+            if n >= Y_BANKS:
+                for a in range(PASSES):
+                    w4_pass(i, c, a)
+            finish(i, c)

@@ -1,6 +1,7 @@
 from contextlib import ExitStack
 
 import concourse.mybir as mybir
+from concourse.masks import make_identity
 
 K, M, T, S, R = 1024, 1024, 4096, 1536, 512
 FLOPS = 2 * S * (K * M + K * R + R * M)
@@ -43,19 +44,20 @@ def tile_list_tabts_bias_kernel(
         nc.sync.dma_start(offsets[:], offs)
         w4 = keep.tile([P, PASSES, M // 2], I32, name="w4", align_bytes=64)
         w4_src = w4_words.bitcast(I32).rearrange("a p w -> p a w")
-        early = UP_COLS // 2
+        early = Y_BANKS * P // 2
         nc.sync.dma_start(w4[:, :, :early], w4_src[:, :, :early])
+
+        ts_row = keep.tile([P, T // P], F32, name="ts_row")
+        nc.gpsimd.dma_start(ts_row[:], ts[0].rearrange("(q c) -> q c", q=P))
+        identity = keep.tile([P, P], F32, name="identity")
+        make_identity(nc, identity[:])
 
         tab_plane = keep.tile([P, T // 4], I32, name="tab_plane", align_bytes=64)
         nc.vector.memset(tab_plane[:], 0)
-        for q in range(4):
-            nc.sync.dma_start(
-                tab_plane[32 * q : 32 * q + 4, :], tab_scales[0, 4 * q : 4 * q + 4, :].bitcast(I32)
-            )
-        nc.sync.dma_start(tab_plane[4:P:8, :], tab_scales[1].bitcast(I32))
+        nc.sync.dma_start(tab_plane[0:P:4, :], tab_scales.rearrange("a q t -> (a q) t").bitcast(I32))
         w4_plane = keep.tile([P, PASSES, M // 4], I32, name="w4_plane", align_bytes=64)
         nc.vector.memset(w4_plane[:], 0)
-        moved = keep.tile([P, S // 4], I32, name="moved", align_bytes=64)
+        moved = keep.tile([P, PASSES, S // 4], I32, name="moved", align_bytes=64)
         nc.vector.memset(moved[:], 0)
 
         tab = [keep.tile([P, T], I32, name="tab%d" % a, align_bytes=64) for a in range(PASSES)]
@@ -63,26 +65,39 @@ def tile_list_tabts_bias_kernel(
         def load_tab(a):
             nc.sync.dma_start(tab[a][:], tab_words[a].rearrange("p t i -> p (t i)").bitcast(I32))
 
+        def load_w4_scales(n0, n1):
+            for q in range(4):
+                nc.sync.dma_start(
+                    w4_plane[32 * q : 32 * q + 4, :, n0 // 4 : n1 // 4],
+                    w4_scales[:, 4 * q : 4 * q + 4, n0:n1].bitcast(I32).rearrange("a r n -> r a n"),
+                )
+
+        down_raw = {}
+
+        def load_down(a, r0, r1):
+            raw = keep.tile([P, PACK, r1 - r0], F32, name="down_raw%d_%d" % (a, r0), align_bytes=64)
+            rows = down[a * P * PACK : (a + 1) * P * PACK, r0:r1]
+            nc.sync.dma_start(raw[:], rows.rearrange("(p j) r -> p j r", j=PACK))
+            down_raw[a, r0, r1] = raw
+
         load_tab(0)
-        for q in range(4):
-            nc.sync.dma_start(
-                w4_plane[32 * q : 32 * q + 4],
-                w4_scales[:, 4 * q : 4 * q + 4, :].bitcast(I32).rearrange("a r n -> r a n"),
-            )
+        load_w4_scales(0, UP_COLS)
         load_tab(1)
         picked = keep.tile([P, S], U8, name="picked", align_bytes=64)
         nc.vector.tensor_copy(picked[:], tab_plane[:].bitcast(U8).indirect(offsets[:]))
-        for q in range(4):
-            nc.sync.dma_start(
-                moved[32 * q : 32 * q + 4, :], picked[32 * q + 4 : 32 * q + 32 : 8, :].bitcast(I32)
-            )
-        down_raw = {}
-        for a in range(PASSES):
-            for u in range(2):
-                raw = keep.tile([P, PACK, HALF], F32, name="down_raw%d%d" % (a, u))
-                rows = down[a * P * PACK : (a + 1) * P * PACK, u * HALF : (u + 1) * HALF]
-                nc.sync.dma_start(raw[:], rows.rearrange("(p j) r -> p j r", j=PACK))
-                down_raw[a, u] = raw
+
+        def place_scales(a):
+            for q in range(4):
+                first = 4 * (16 * a + 4 * q)
+                nc.sync.dma_start(
+                    moved[32 * q : 32 * q + 4, a, :], picked[first : first + 16 : 4, :].bitcast(I32)
+                )
+
+        place_scales(0)
+        load_down(0, 0, R)
+        load_down(1, 0, HALF)
+        place_scales(1)
+        load_down(1, HALF, R)
         up_raw = {}
 
         def load_up(g):
@@ -93,13 +108,22 @@ def tile_list_tabts_bias_kernel(
             up_raw[g] = raw
 
         load_up(0)
-        ts_all = keep.tile([P, T], F32, name="ts_all")
-        nc.sync.dma_start(ts_all[:], ts)
         bias = keep.tile([P, N_TILES], F32, name="bias")
         with nc.allow_non_contiguous_dma(reason="one bias value to a partition"):
             nc.sync.dma_start(bias[:], b.rearrange("(i p) -> p i", p=P))
         nc.sync.dma_start(w4[:, :, early:], w4_src[:, :, early:])
+        load_w4_scales(UP_COLS, M)
         load_up(1)
+
+        ts_all = keep.tile([P, T], F32, name="ts_all")
+        ts_view = ts_all[:].rearrange("p (q c) -> p q c", q=P)
+        for c0 in range(0, T // P, 4):
+            bank = psum.tile([P, 4, P], F32, name="bank%d" % (c0 // 4))
+            for j in range(4):
+                column = ts_row[:, c0 + j : c0 + j + 1].to_broadcast([P, P])
+                nc.tensor.transpose(bank[:, j, :], column, identity[:])
+            nc.scalar.copy(ts_view[:, :, c0 : c0 + 4], bank[:].rearrange("p j q -> p q j"))
+        ts_picked = keep.tile([P, 2 * CHUNK], F32, name="ts_picked")
 
         v_codes, v_scales, ts_cols = {}, {}, {}
 
@@ -107,17 +131,22 @@ def tile_list_tabts_bias_kernel(
             return offsets[:, c * CHUNK // 16 : (c + 1) * CHUNK // 16]
 
         for c in range(CHUNKS):
-            v_scales[0, c] = picked[:, c * CHUNK : (c + 1) * CHUNK]
-            v_scales[1, c] = moved[:].bitcast(U8)[:, c * CHUNK : (c + 1) * CHUNK]
+            for a in range(PASSES):
+                v_scales[a, c] = moved[:, a, :].bitcast(U8)[:, c * CHUNK : (c + 1) * CHUNK]
 
         def gather_codes(a, c):
-            t = keep.tile([P, CHUNK], U32, name="v_codes%d%d" % (a, c), align_bytes=64)
+            tag = "down_raw1_%d" % HALF if (a, c) == (1, 2) else "v_codes%d%d" % (a, c)
+            t = keep.tile([P, CHUNK], U32, name="v_codes%d%d" % (a, c), tag=tag, align_bytes=64)
             nc.vector.tensor_copy(t[:], tab[a][:].bitcast(U32).indirect(entries(c)))
             v_codes[a, c] = t
 
         def gather_ts(c):
-            t = keep.tile([P, CHUNK], F32, name="ts_cols%d" % c)
-            nc.vector.tensor_copy(t[:], ts_all[:].indirect(entries(c)))
+            if c < 2:
+                t = ts_picked[:, c * CHUNK : (c + 1) * CHUNK]
+            else:
+                last = keep.tile([P, CHUNK], F32, name="ts_last", tag="up_raw0")
+                t = last[:]
+            nc.vector.tensor_copy(t, ts_all[:].indirect(entries(c)))
             ts_cols[c] = t
 
         y_bank = {}
@@ -142,10 +171,10 @@ def tile_list_tabts_bias_kernel(
         down_codes = keep.tile([P, PASSES, R], U32, name="down_codes", align_bytes=64)
         down_scales = keep.tile([P, PASSES, R], U8, name="down_scales", align_bytes=64)
 
-        def round_down(copy, a, u, t0, t1):
-            src = down_raw[a, u][:].rearrange("p j (g t i) -> p t g i j", t=PACK, i=8)
+        def round_down(copy, a, r0, r1, t0, t1):
+            src = down_raw[a, r0, r1][:].rearrange("p j (g t i) -> p t g i j", t=PACK, i=8)
             for t in range(t0, t1):
-                dst = down_bf[a][:, t, u * P // 2 : (u + 1) * P // 2, :]
+                dst = down_bf[a][:, t, r0 // PACK : r1 // PACK, :]
                 copy(dst.rearrange("p (g i) j -> p g i j", i=8), src[:, t])
 
         def quantize_down(a, t0, t1):
@@ -230,14 +259,13 @@ def tile_list_tabts_bias_kernel(
             for i, c in order[:Y_BANKS]:
                 w4_pass(i, c, a)
 
-        round_down(nc.scalar.copy, 0, 0, 0, PACK)
-        round_down(nc.vector.tensor_copy, 0, 1, 0, 2)
-        round_down(nc.scalar.copy, 0, 1, 2, PACK)
-        round_down(nc.vector.tensor_copy, 1, 0, 0, 2)
-        round_down(nc.scalar.copy, 1, 0, 2, PACK)
+        round_down(nc.vector.tensor_copy, 0, 0, R, 0, 2)
+        round_down(nc.scalar.copy, 0, 0, R, 2, PACK)
+        round_down(nc.vector.tensor_copy, 1, 0, HALF, 0, 2)
+        round_down(nc.scalar.copy, 1, 0, HALF, 2, PACK)
         quantize_down(0, 0, PACK)
-        round_down(nc.vector.tensor_copy, 1, 1, 0, 3)
-        round_down(nc.scalar.copy, 1, 1, 3, PACK)
+        round_down(nc.vector.tensor_copy, 1, HALF, R, 0, 3)
+        round_down(nc.scalar.copy, 1, HALF, R, 3, PACK)
         for t in range(PACK):
             quantize_down(1, t, t + 1)
 
@@ -256,7 +284,7 @@ def tile_list_tabts_bias_kernel(
         for n, (i, c) in enumerate(order):
             if n == Y_BANKS:
                 gather_ts(2)
-                round_up(nc.scalar.copy, 1)
+                round_up(nc.vector.tensor_copy, 1)
                 quantize_up(1)
             if n >= Y_BANKS:
                 for a in range(PASSES):

@@ -37,16 +37,18 @@ def tile_list_tabts_bias_kernel(
     nc = tc.nc
     with ExitStack() as ctx:
         keep = ctx.enter_context(tc.tile_pool(name="keep", bufs=1))
-        stage = ctx.enter_context(tc.tile_pool(name="stage", bufs=6))
+        stage = ctx.enter_context(tc.tile_pool(name="stage", bufs=8))
         psum = ctx.enter_context(tc.psum_pool(name="psum", bufs=1))
 
         offsets = keep.tile([P, S // 16], U16, name="offsets")
         nc.sync.dma_start(offsets[:], offs)
-        w4 = keep.tile([P, PASSES, M // 2], I32, name="w4", align_bytes=64)
-        w4_src = w4_words.bitcast(I32).rearrange("a p w -> p a w")
-        early = Y_BANKS * P // 2
-        nc.sync.dma_start(w4[:, :, :early], w4_src[:, :, :early])
+        tab = [keep.tile([P, T], I32, name="tab%d" % a, align_bytes=64) for a in range(PASSES)]
 
+        def load_tab(a, t0, t1):
+            words = tab_words[a].rearrange("p t i -> p (t i)").bitcast(I32)
+            nc.sync.dma_start(tab[a][:, t0:t1], words[:, t0:t1])
+
+        load_tab(0, 0, T // 4)
         ts_row = keep.tile([P, T // P], F32, name="ts_row")
         nc.gpsimd.dma_start(ts_row[:], ts[0].rearrange("(q c) -> q c", q=P))
         identity = keep.tile([P, P], F32, name="identity")
@@ -60,14 +62,9 @@ def tile_list_tabts_bias_kernel(
         moved = keep.tile([P, PASSES, S // 4], I32, name="moved", align_bytes=64)
         nc.vector.memset(moved[:], 0)
 
-        tab = [keep.tile([P, T], I32, name="tab%d" % a, align_bytes=64) for a in range(PASSES)]
-
-        def load_tab(a):
-            nc.sync.dma_start(tab[a][:], tab_words[a].rearrange("p t i -> p (t i)").bitcast(I32))
-
-        def load_w4_scales(n0, n1):
+        def load_w4_scales(queue, n0, n1):
             for q in range(4):
-                nc.sync.dma_start(
+                queue.dma_start(
                     w4_plane[32 * q : 32 * q + 4, :, n0 // 4 : n1 // 4],
                     w4_scales[:, 4 * q : 4 * q + 4, n0:n1].bitcast(I32).rearrange("a r n -> r a n"),
                 )
@@ -80,16 +77,20 @@ def tile_list_tabts_bias_kernel(
             nc.sync.dma_start(raw[:], rows.rearrange("(p j) r -> p j r", j=PACK))
             down_raw[a, r0, r1] = raw
 
-        load_tab(0)
-        load_w4_scales(0, UP_COLS)
-        load_tab(1)
+        load_tab(0, T // 4, T)
+        w4 = keep.tile([P, PASSES, M // 2], I32, name="w4", align_bytes=64)
+        w4_src = w4_words.bitcast(I32).rearrange("a p w -> p a w")
+        early = UP_COLS // 2
+        load_w4_scales(nc.gpsimd, 0, UP_COLS)
+        load_tab(1, 0, T)
+        nc.sync.dma_start(w4[:, :, :early], w4_src[:, :, :early])
         picked = keep.tile([P, S], U8, name="picked", align_bytes=64)
         nc.vector.tensor_copy(picked[:], tab_plane[:].bitcast(U8).indirect(offsets[:]))
 
         def place_scales(a):
             for q in range(4):
                 first = 4 * (16 * a + 4 * q)
-                nc.sync.dma_start(
+                nc.gpsimd.dma_start(
                     moved[32 * q : 32 * q + 4, a, :], picked[first : first + 16 : 4, :].bitcast(I32)
                 )
 
@@ -112,7 +113,7 @@ def tile_list_tabts_bias_kernel(
         with nc.allow_non_contiguous_dma(reason="one bias value to a partition"):
             nc.sync.dma_start(bias[:], b.rearrange("(i p) -> p i", p=P))
         nc.sync.dma_start(w4[:, :, early:], w4_src[:, :, early:])
-        load_w4_scales(UP_COLS, M)
+        load_w4_scales(nc.sync, UP_COLS, M)
         load_up(1)
 
         ts_all = keep.tile([P, T], F32, name="ts_all")
@@ -123,7 +124,6 @@ def tile_list_tabts_bias_kernel(
                 column = ts_row[:, c0 + j : c0 + j + 1].to_broadcast([P, P])
                 nc.tensor.transpose(bank[:, j, :], column, identity[:])
             nc.scalar.copy(ts_view[:, :, c0 : c0 + 4], bank[:].rearrange("p j q -> p q j"))
-        ts_picked = keep.tile([P, 2 * CHUNK], F32, name="ts_picked")
 
         v_codes, v_scales, ts_cols = {}, {}, {}
 
@@ -141,11 +141,7 @@ def tile_list_tabts_bias_kernel(
             v_codes[a, c] = t
 
         def gather_ts(c):
-            if c < 2:
-                t = ts_picked[:, c * CHUNK : (c + 1) * CHUNK]
-            else:
-                last = keep.tile([P, CHUNK], F32, name="ts_last", tag="up_raw0")
-                t = last[:]
+            t = ts_last[:] if c == CHUNKS - 1 else ts_first[:, c * CHUNK : (c + 1) * CHUNK]
             nc.vector.tensor_copy(t, ts_all[:].indirect(entries(c)))
             ts_cols[c] = t
 
@@ -278,6 +274,8 @@ def tile_list_tabts_bias_kernel(
         quantize_h(0)
         quantize_up(0)
         quantize_h(1)
+        ts_first = keep.tile([P, S - CHUNK], F32, name="ts_first")
+        ts_last = keep.tile([P, CHUNK], F32, name="ts_last", tag="up_raw0")
         gather_ts(0)
         gather_ts(1)
         quantize_h(2)

@@ -28,7 +28,6 @@ BANKS = 8
 Y_BANKS = 5
 H_BANKS = BANKS - Y_BANKS
 UP_COLS = 512
-HALF = R // 2
 
 
 def tile_list_tabts_bias_kernel(
@@ -56,49 +55,42 @@ def tile_list_tabts_bias_kernel(
 
         tab_plane = keep.tile([P, T // 4], I32, name="tab_plane", align_bytes=64)
         nc.vector.memset(tab_plane[:], 0)
-        nc.sync.dma_start(tab_plane[0:P:4, :], tab_scales.rearrange("a q t -> (a q) t").bitcast(I32))
+        nc.sync.dma_start(tab_plane[0:P:4, :], tab_scales.rearrange("a s t -> s a t").bitcast(I32))
         w4_plane = keep.tile([P, PASSES, M // 4], I32, name="w4_plane", align_bytes=64)
         nc.vector.memset(w4_plane[:], 0)
         moved = keep.tile([P, PASSES, S // 4], I32, name="moved", align_bytes=64)
         nc.vector.memset(moved[:], 0)
+        for q in range(4):
+            nc.gpsimd.dma_start(
+                w4_plane[32 * q : 32 * q + 4, :, :],
+                w4_scales[:, 4 * q : 4 * q + 4, :].bitcast(I32).rearrange("a r n -> r a n"),
+            )
+        b_rows = keep.tile([P, P], F32, name="b_rows")
+        nc.gpsimd.memset(b_rows[:], 0.0)
+        nc.gpsimd.dma_start(b_rows[0:N_TILES, :], b.rearrange("(i p) -> i p", p=P))
 
-        def load_w4_scales(queue, n0, n1):
-            for q in range(4):
-                queue.dma_start(
-                    w4_plane[32 * q : 32 * q + 4, :, n0 // 4 : n1 // 4],
-                    w4_scales[:, 4 * q : 4 * q + 4, n0:n1].bitcast(I32).rearrange("a r n -> r a n"),
-                )
+        down_raw = []
 
-        down_raw = {}
-
-        def load_down(a, r0, r1):
-            raw = keep.tile([P, PACK, r1 - r0], F32, name="down_raw%d_%d" % (a, r0), align_bytes=64)
-            rows = down[a * P * PACK : (a + 1) * P * PACK, r0:r1]
+        def load_down(a):
+            raw = keep.tile([P, PACK, R], F32, name="down_raw%d" % a, align_bytes=64)
+            rows = down[a * P * PACK : (a + 1) * P * PACK, :]
             nc.sync.dma_start(raw[:], rows.rearrange("(p j) r -> p j r", j=PACK))
-            down_raw[a, r0, r1] = raw
+            down_raw.append(raw)
 
         load_tab(0, T // 4, T)
+        load_down(0)
         w4 = keep.tile([P, PASSES, M // 2], I32, name="w4", align_bytes=64)
         w4_src = w4_words.bitcast(I32).rearrange("a p w -> p a w")
         early = UP_COLS // 2
-        load_w4_scales(nc.gpsimd, 0, UP_COLS)
-        load_tab(1, 0, T)
         nc.sync.dma_start(w4[:, :, :early], w4_src[:, :, :early])
+        load_tab(1, 0, T)
+        load_down(1)
         picked = keep.tile([P, S], U8, name="picked", align_bytes=64)
         nc.vector.tensor_copy(picked[:], tab_plane[:].bitcast(U8).indirect(offsets[:]))
-
-        def place_scales(a):
-            for q in range(4):
-                first = 4 * (16 * a + 4 * q)
-                nc.gpsimd.dma_start(
-                    moved[32 * q : 32 * q + 4, a, :], picked[first : first + 16 : 4, :].bitcast(I32)
-                )
-
-        place_scales(0)
-        load_down(0, 0, R)
-        load_down(1, 0, HALF)
-        place_scales(1)
-        load_down(1, HALF, R)
+        for q in range(4):
+            nc.scalar.dma_start(
+                moved[32 * q : 32 * q + 4, :, :], picked[32 * q : 32 * q + 32 : 4, :].bitcast(I32)
+            )
         up_raw = {}
 
         def load_up(g):
@@ -109,11 +101,7 @@ def tile_list_tabts_bias_kernel(
             up_raw[g] = raw
 
         load_up(0)
-        bias = keep.tile([P, N_TILES], F32, name="bias")
-        with nc.allow_non_contiguous_dma(reason="one bias value to a partition"):
-            nc.sync.dma_start(bias[:], b.rearrange("(i p) -> p i", p=P))
         nc.sync.dma_start(w4[:, :, early:], w4_src[:, :, early:])
-        load_w4_scales(nc.sync, UP_COLS, M)
         load_up(1)
 
         ts_all = keep.tile([P, T], F32, name="ts_all")
@@ -124,37 +112,44 @@ def tile_list_tabts_bias_kernel(
                 column = ts_row[:, c0 + j : c0 + j + 1].to_broadcast([P, P])
                 nc.tensor.transpose(bank[:, j, :], column, identity[:])
             nc.scalar.copy(ts_view[:, :, c0 : c0 + 4], bank[:].rearrange("p j q -> p q j"))
+        bias = keep.tile([P, N_TILES], F32, name="bias")
+        bank = psum.tile([P, P], F32, name="bank0")
+        nc.tensor.transpose(bank[:], b_rows[:], identity[:])
+        nc.scalar.copy(bias[:], bank[:, 0:N_TILES])
 
         v_codes, v_scales, ts_cols = {}, {}, {}
 
-        def entries(c):
-            return offsets[:, c * CHUNK // 16 : (c + 1) * CHUNK // 16]
+        def entries(c0, c1):
+            return offsets[:, c0 * CHUNK // 16 : c1 * CHUNK // 16]
 
         for c in range(CHUNKS):
             for a in range(PASSES):
                 v_scales[a, c] = moved[:, a, :].bitcast(U8)[:, c * CHUNK : (c + 1) * CHUNK]
 
-        def gather_codes(a, c):
-            tag = "down_raw1_%d" % HALF if (a, c) == (1, 2) else "v_codes%d%d" % (a, c)
-            t = keep.tile([P, CHUNK], U32, name="v_codes%d%d" % (a, c), tag=tag, align_bytes=64)
-            nc.vector.tensor_copy(t[:], tab[a][:].bitcast(U32).indirect(entries(c)))
-            v_codes[a, c] = t
+        def gather_codes(a, c0, c1, tag):
+            t = keep.tile([P, (c1 - c0) * CHUNK], U32, name="v_codes", tag=tag, align_bytes=64)
+            nc.vector.tensor_copy(t[:], tab[a][:].bitcast(U32).indirect(entries(c0, c1)))
+            for c in range(c0, c1):
+                v_codes[a, c] = t[:, (c - c0) * CHUNK : (c - c0 + 1) * CHUNK]
 
-        def gather_ts(c):
-            t = ts_last[:] if c == CHUNKS - 1 else ts_first[:, c * CHUNK : (c + 1) * CHUNK]
-            nc.vector.tensor_copy(t, ts_all[:].indirect(entries(c)))
-            ts_cols[c] = t
+        def gather_ts(c0, c1, tag):
+            t = keep.tile([P, (c1 - c0) * CHUNK], F32, name="ts_cols", tag=tag, align_bytes=64)
+            nc.vector.tensor_copy(t[:], ts_all[:].indirect(entries(c0, c1)))
+            for c in range(c0, c1):
+                ts_cols[c] = t[:, (c - c0) * CHUNK : (c - c0 + 1) * CHUNK]
 
         y_bank = {}
 
         def w4_pass(i, c, a):
             if a == 0:
-                y_bank[i, c] = psum.tile([P, CHUNK], F32, name="bank%d" % (len(y_bank) % BANKS))
+                n = len(y_bank)
+                turn = n % Y_BANKS if n < 2 * Y_BANKS else (n - Y_BANKS) % BANKS
+                y_bank[i, c] = psum.tile([P, CHUNK], F32, name="bank%d" % turn)
             nc.tensor.matmul_mx(
                 out=y_bank[i, c][:],
                 lhsT=w4[:, a, :].bitcast(U8)[:, 2 * P * i : 2 * P * (i + 1)].bitcast(FP4X4),
                 lhsT_scale=w4_plane[:, a, :].bitcast(U8)[:, P * i : P * (i + 1)],
-                rhs=v_codes[a, c][:].bitcast(FP8X4),
+                rhs=v_codes[a, c].bitcast(FP8X4),
                 rhs_scale=v_scales[a, c],
                 start=(a == 0),
                 stop=False,
@@ -167,11 +162,10 @@ def tile_list_tabts_bias_kernel(
         down_codes = keep.tile([P, PASSES, R], U32, name="down_codes", align_bytes=64)
         down_scales = keep.tile([P, PASSES, R], U8, name="down_scales", align_bytes=64)
 
-        def round_down(copy, a, r0, r1, t0, t1):
-            src = down_raw[a, r0, r1][:].rearrange("p j (g t i) -> p t g i j", t=PACK, i=8)
+        def round_down(copy, a, t0, t1):
+            src = down_raw[a][:].rearrange("p j (g t i) -> p t g i j", t=PACK, i=8)
             for t in range(t0, t1):
-                dst = down_bf[a][:, t, r0 // PACK : r1 // PACK, :]
-                copy(dst.rearrange("p (g i) j -> p g i j", i=8), src[:, t])
+                copy(down_bf[a][:, t].rearrange("p (g i) j -> p g i j", i=8), src[:, t])
 
         def quantize_down(a, t0, t1):
             nc.vector.quantize_mx(
@@ -180,23 +174,28 @@ def tile_list_tabts_bias_kernel(
                 in_=down_bf[a][:, t0:t1].rearrange("p t m j -> p (t m j)"),
             )
 
-        up_bf = keep.tile([P, M, PACK], BF16, name="up_bf", align_bytes=64)
+        up_bf = {}
         up_codes = keep.tile([P, M], U32, name="up_codes", align_bytes=64)
         up_scales = keep.tile([P, M], U8, name="up_scales", align_bytes=64)
 
-        def round_up(copy, g):
-            cols = slice(g * UP_COLS, (g + 1) * UP_COLS)
-            copy(up_bf[:, cols, :], up_raw[g][:].rearrange("p j n -> p n j"))
+        def round_up(copy, g, width, tag):
+            up_bf[g] = keep.tile([P, UP_COLS, PACK], BF16, name="up_bf", tag=tag, align_bytes=64)
+            for n0 in range(0, UP_COLS, width):
+                cols = slice(n0, n0 + width)
+                copy(up_bf[g][:, cols, :], up_raw[g][:, :, cols].rearrange("p j n -> p n j"))
 
-        def quantize_up(g):
-            cols = slice(g * UP_COLS, (g + 1) * UP_COLS)
-            nc.vector.quantize_mx(
-                out=up_codes[:, cols].bitcast(FP8X4),
-                scales=up_scales[:, cols],
-                in_=up_bf[:, cols, :].rearrange("p n j -> p (n j)"),
-            )
+        def quantize_up(g, width):
+            for n0 in range(0, UP_COLS, width):
+                cols = slice(g * UP_COLS + n0, g * UP_COLS + n0 + width)
+                nc.vector.quantize_mx(
+                    out=up_codes[:, cols].bitcast(FP8X4),
+                    scales=up_scales[:, cols],
+                    in_=up_bf[g][:, n0 : n0 + width, :].rearrange("p n j -> p (n j)"),
+                )
 
-        h_bf = keep.tile([P, S, PACK], BF16, name="h_bf", align_bytes=64)
+        h_bf = [
+            keep.tile([P, CHUNK, PACK], BF16, name="h_bf%d" % c, align_bytes=64) for c in range(CHUNKS)
+        ]
         h_codes = keep.tile([P, S], U32, name="h_codes", align_bytes=64)
         h_scales = keep.tile([P, S], U8, name="h_scales", align_bytes=64)
 
@@ -204,26 +203,25 @@ def tile_list_tabts_bias_kernel(
             for s0 in range(0, CHUNK, SUB):
                 turn = (c * CHUNK + s0) // SUB % H_BANKS
                 bank = psum.tile([P, PACK, SUB], F32, name="bank%d" % (Y_BANKS + turn))
-                for t in range(PACK):
-                    for a in range(PASSES):
+                for a in range(PASSES):
+                    for t in range(PACK):
                         nc.tensor.matmul_mx(
                             out=bank[:, t, :],
                             lhsT=down_codes[:, a, t * P : (t + 1) * P].bitcast(FP8X4),
                             lhsT_scale=down_scales[:, a, t * P : (t + 1) * P],
                             rhs=v_codes[a, c][:, s0 : s0 + SUB].bitcast(FP8X4),
                             rhs_scale=v_scales[a, c][:, s0 : s0 + SUB],
-                            start=(a == 0),
-                            stop=(a == PASSES - 1),
+                            start=(a == 0 and t == 0),
+                            stop=(a == PASSES - 1 and t == PACK - 1),
                         )
-                j0 = c * CHUNK + s0
-                nc.scalar.copy(h_bf[:, j0 : j0 + SUB, :], bank[:].rearrange("p t n -> p n t"))
+                nc.scalar.copy(h_bf[c][:, s0 : s0 + SUB, :], bank[:].rearrange("p t n -> p n t"))
 
         def quantize_h(c):
             cols = slice(c * CHUNK, (c + 1) * CHUNK)
             nc.vector.quantize_mx(
                 out=h_codes[:, cols].bitcast(FP8X4),
                 scales=h_scales[:, cols],
-                in_=h_bf[:, cols, :].rearrange("p n t -> p (n t)"),
+                in_=h_bf[c][:].rearrange("p n t -> p (n t)"),
             )
 
         def finish(i, c):
@@ -249,41 +247,35 @@ def tile_list_tabts_bias_kernel(
 
         half = N_TILES // 2
         order = [(i, c) for i0 in (0, half) for c in range(CHUNKS) for i in range(i0, i0 + half)]
+        gather_codes(0, 0, CHUNKS, "v_codes0")
+        gather_ts(0, CHUNKS - 1, "tab0")
+        round_down(nc.scalar.copy, 0, 0, PACK)
+        quantize_down(0, 0, PACK)
+        gather_codes(1, 0, 1, "v_codes10")
+        gather_codes(1, 1, 2, "v_codes11")
         for a in range(PASSES):
-            gather_codes(a, 0)
-            gather_codes(a, 1)
             for i, c in order[:Y_BANKS]:
                 w4_pass(i, c, a)
 
-        round_down(nc.vector.tensor_copy, 0, 0, R, 0, 2)
-        round_down(nc.scalar.copy, 0, 0, R, 2, PACK)
-        round_down(nc.vector.tensor_copy, 1, 0, HALF, 0, 2)
-        round_down(nc.scalar.copy, 1, 0, HALF, 2, PACK)
-        quantize_down(0, 0, PACK)
-        round_down(nc.vector.tensor_copy, 1, HALF, R, 0, 3)
-        round_down(nc.scalar.copy, 1, HALF, R, 3, PACK)
+        round_down(nc.vector.tensor_copy, 1, 0, 2)
+        round_down(nc.scalar.copy, 1, 2, PACK)
         for t in range(PACK):
             quantize_down(1, t, t + 1)
+        gather_codes(1, 2, 3, "down_bf1")
 
         make_h(0)
         make_h(1)
-        for a in range(PASSES):
-            gather_codes(a, 2)
         make_h(2)
-        round_up(nc.vector.tensor_copy, 0)
+        round_up(nc.vector.tensor_copy, 0, UP_COLS // 2, "up_bf0")
         quantize_h(0)
-        quantize_up(0)
+        quantize_up(0, UP_COLS // 2)
         quantize_h(1)
-        ts_first = keep.tile([P, S - CHUNK], F32, name="ts_first")
-        ts_last = keep.tile([P, CHUNK], F32, name="ts_last", tag="up_raw0")
-        gather_ts(0)
-        gather_ts(1)
         quantize_h(2)
         for n, (i, c) in enumerate(order):
             if n == Y_BANKS:
-                gather_ts(2)
-                round_up(nc.vector.tensor_copy, 1)
-                quantize_up(1)
+                gather_ts(2, 3, "h_bf0")
+                round_up(nc.scalar.copy, 1, UP_COLS // 4, "h_bf1")
+                quantize_up(1, UP_COLS)
             if n >= Y_BANKS:
                 for a in range(PASSES):
                     w4_pass(i, c, a)

@@ -28,6 +28,7 @@ BANKS = 8
 Y_BANKS = 5
 H_BANKS = BANKS - Y_BANKS
 UP_COLS = 512
+ROUND = (7, 5, 6, 4, 0, 1, 2, 3)
 
 
 def tile_list_tabts_bias_kernel(
@@ -50,6 +51,9 @@ def tile_list_tabts_bias_kernel(
         load_tab(0, 0, T // 4)
         ts_row = keep.tile([P, T // P], F32, name="ts_row")
         nc.gpsimd.dma_start(ts_row[:], ts[0].rearrange("(q c) -> q c", q=P))
+        b_rows = keep.tile([P, P], F32, name="b_rows")
+        nc.gpsimd.memset(b_rows[:], 0.0)
+        nc.gpsimd.dma_start(b_rows[0:N_TILES, :], b.rearrange("(i p) -> i p", p=P))
         identity = keep.tile([P, P], F32, name="identity")
         make_identity(nc, identity[:])
 
@@ -61,13 +65,10 @@ def tile_list_tabts_bias_kernel(
         moved = keep.tile([P, PASSES, S // 4], I32, name="moved", align_bytes=64)
         nc.vector.memset(moved[:], 0)
         for q in range(4):
-            nc.gpsimd.dma_start(
+            nc.scalar.dma_start(
                 w4_plane[32 * q : 32 * q + 4, :, :],
                 w4_scales[:, 4 * q : 4 * q + 4, :].bitcast(I32).rearrange("a r n -> r a n"),
             )
-        b_rows = keep.tile([P, P], F32, name="b_rows")
-        nc.gpsimd.memset(b_rows[:], 0.0)
-        nc.gpsimd.dma_start(b_rows[0:N_TILES, :], b.rearrange("(i p) -> i p", p=P))
 
         down_raw = []
 
@@ -87,17 +88,12 @@ def tile_list_tabts_bias_kernel(
         load_down(1)
         picked = keep.tile([P, S], U8, name="picked", align_bytes=64)
         nc.vector.tensor_copy(picked[:], tab_plane[:].bitcast(U8).indirect(offsets[:]))
-        for q in range(4):
-            nc.scalar.dma_start(
-                moved[32 * q : 32 * q + 4, :, :], picked[32 * q : 32 * q + 32 : 4, :].bitcast(I32)
-            )
         up_raw = {}
 
         def load_up(g):
             raw = keep.tile([P, PACK, UP_COLS], F32, name="up_raw%d" % g)
             cols = up[:, g * UP_COLS : (g + 1) * UP_COLS]
-            for t in range(PACK):
-                nc.sync.dma_start(raw[:, t, :], cols.rearrange("(g t i) n -> t g i n", t=PACK, i=8)[t])
+            nc.sync.dma_start(raw[:], cols.rearrange("(p t) n -> p t n", t=PACK))
             up_raw[g] = raw
 
         load_up(0)
@@ -116,6 +112,11 @@ def tile_list_tabts_bias_kernel(
         bank = psum.tile([P, P], F32, name="bank0")
         nc.tensor.transpose(bank[:], b_rows[:], identity[:])
         nc.scalar.copy(bias[:], bank[:, 0:N_TILES])
+
+        for q in range(4):
+            nc.scalar.dma_start(
+                moved[32 * q : 32 * q + 4, :, :], picked[32 * q : 32 * q + 32 : 4, :].bitcast(I32)
+            )
 
         v_codes, v_scales, ts_cols = {}, {}, {}
 
@@ -143,7 +144,7 @@ def tile_list_tabts_bias_kernel(
         def w4_pass(i, c, a):
             if a == 0:
                 n = len(y_bank)
-                turn = n % Y_BANKS if n < 2 * Y_BANKS else (n - Y_BANKS) % BANKS
+                turn = n if n < Y_BANKS else ROUND[(n - Y_BANKS) % BANKS]
                 y_bank[i, c] = psum.tile([P, CHUNK], F32, name="bank%d" % turn)
             nc.tensor.matmul_mx(
                 out=y_bank[i, c][:],
@@ -162,10 +163,10 @@ def tile_list_tabts_bias_kernel(
         down_codes = keep.tile([P, PASSES, R], U32, name="down_codes", align_bytes=64)
         down_scales = keep.tile([P, PASSES, R], U8, name="down_scales", align_bytes=64)
 
-        def round_down(copy, a, t0, t1):
-            src = down_raw[a][:].rearrange("p j (g t i) -> p t g i j", t=PACK, i=8)
-            for t in range(t0, t1):
-                copy(down_bf[a][:, t].rearrange("p (g i) j -> p g i j", i=8), src[:, t])
+        def round_down(copy, a, m0, m1):
+            src = down_raw[a][:].rearrange("p j (m t) -> p m j t", t=PACK)
+            dst = down_bf[a][:].rearrange("p t m j -> p m j t")
+            copy(dst[:, m0:m1], src[:, m0:m1])
 
         def quantize_down(a, t0, t1):
             nc.vector.quantize_mx(
@@ -196,13 +197,13 @@ def tile_list_tabts_bias_kernel(
         h_bf = [
             keep.tile([P, CHUNK, PACK], BF16, name="h_bf%d" % c, align_bytes=64) for c in range(CHUNKS)
         ]
-        h_codes = keep.tile([P, S], U32, name="h_codes", align_bytes=64)
+        h_codes = {}
         h_scales = keep.tile([P, S], U8, name="h_scales", align_bytes=64)
 
         def make_h(c):
             for s0 in range(0, CHUNK, SUB):
-                turn = (c * CHUNK + s0) // SUB % H_BANKS
-                bank = psum.tile([P, PACK, SUB], F32, name="bank%d" % (Y_BANKS + turn))
+                turn = Y_BANKS + (c * CHUNK + s0) // SUB % H_BANKS if c < CHUNKS - 1 else s0 // SUB
+                bank = psum.tile([P, PACK, SUB], F32, name="bank%d" % turn)
                 for a in range(PASSES):
                     for t in range(PACK):
                         nc.tensor.matmul_mx(
@@ -216,13 +217,20 @@ def tile_list_tabts_bias_kernel(
                         )
                 nc.scalar.copy(h_bf[c][:, s0 : s0 + SUB, :], bank[:].rearrange("p t n -> p n t"))
 
-        def quantize_h(c):
+        def quantize_h(c, tag):
             cols = slice(c * CHUNK, (c + 1) * CHUNK)
+            h_codes[c] = keep.tile([P, CHUNK], U32, name="h_codes", tag=tag, align_bytes=64)
             nc.vector.quantize_mx(
-                out=h_codes[:, cols].bitcast(FP8X4),
+                out=h_codes[c][:].bitcast(FP8X4),
                 scales=h_scales[:, cols],
                 in_=h_bf[c][:].rearrange("p n t -> p (n t)"),
             )
+
+        scaled = {}
+
+        def parts(i, c):
+            width = CHUNK // 2 if (i, c) == (N_TILES - 1, CHUNKS - 1) else CHUNK
+            return [slice(j0, j0 + width) for j0 in range(0, CHUNK, width)]
 
         def finish(i, c):
             cols = slice(c * CHUNK, (c + 1) * CHUNK)
@@ -231,25 +239,27 @@ def tile_list_tabts_bias_kernel(
                 out=y_bank[i, c][:],
                 lhsT=up_codes[:, rows].bitcast(FP8X4),
                 lhsT_scale=up_scales[:, rows],
-                rhs=h_codes[:, cols].bitcast(FP8X4),
+                rhs=h_codes[c][:].bitcast(FP8X4),
                 rhs_scale=h_scales[:, cols],
                 start=False,
                 stop=True,
             )
-            scaled = stage.tile([P, CHUNK], F32, name="scaled")
+            scaled[i, c] = stage.tile([P, CHUNK], F32, name="scaled")
+            for part in parts(i, c):
+                nc.vector.tensor_tensor(scaled[i, c][:, part], y_bank[i, c][:, part], ts_cols[c][:, part], MULT)
+
+        def store(i, c):
             result = stage.tile([P, CHUNK], F32, name="result")
-            width = CHUNK // 2 if (i, c) == (N_TILES - 1, CHUNKS - 1) else CHUNK
-            for j0 in range(0, CHUNK, width):
-                part = slice(j0, j0 + width)
-                nc.vector.tensor_tensor(scaled[:, part], y_bank[i, c][:, part], ts_cols[c][:, part], MULT)
-                nc.scalar.activation(result[:, part], scaled[:, part], IDENT, bias=bias[:, i : i + 1])
-                nc.sync.dma_start(out[rows, c * CHUNK + j0 : c * CHUNK + j0 + width], result[:, part])
+            tile_out = out[i * P : (i + 1) * P, c * CHUNK : (c + 1) * CHUNK]
+            for part in parts(i, c):
+                nc.scalar.activation(result[:, part], scaled[i, c][:, part], IDENT, bias=bias[:, i : i + 1])
+                nc.sync.dma_start(tile_out[:, part], result[:, part])
 
         half = N_TILES // 2
         order = [(i, c) for i0 in (0, half) for c in range(CHUNKS) for i in range(i0, i0 + half)]
         gather_codes(0, 0, CHUNKS, "v_codes0")
-        gather_ts(0, CHUNKS - 1, "tab0")
-        round_down(nc.scalar.copy, 0, 0, PACK)
+        gather_ts(0, 1, "tab0")
+        round_down(nc.scalar.copy, 0, 0, P)
         quantize_down(0, 0, PACK)
         gather_codes(1, 0, 1, "v_codes10")
         gather_codes(1, 1, 2, "v_codes11")
@@ -257,26 +267,35 @@ def tile_list_tabts_bias_kernel(
             for i, c in order[:Y_BANKS]:
                 w4_pass(i, c, a)
 
-        round_down(nc.vector.tensor_copy, 1, 0, 2)
-        round_down(nc.scalar.copy, 1, 2, PACK)
+        round_down(nc.vector.tensor_copy, 1, 0, 88)
+        round_down(nc.scalar.copy, 1, 88, P)
         for t in range(PACK):
             quantize_down(1, t, t + 1)
         gather_codes(1, 2, 3, "down_bf1")
 
         make_h(0)
-        make_h(1)
-        make_h(2)
         round_up(nc.vector.tensor_copy, 0, UP_COLS // 2, "up_bf0")
-        quantize_h(0)
         quantize_up(0, UP_COLS // 2)
-        quantize_h(1)
-        quantize_h(2)
+        quantize_h(0, "up_bf0")
+        for i, c in order[:half]:
+            finish(i, c)
+        gather_ts(1, 2, "h_bf0")
+        make_h(1)
+        quantize_h(1, "h_codes1")
+        make_h(2)
+        for i, c in order[:half]:
+            store(i, c)
         for n, (i, c) in enumerate(order):
-            if n == Y_BANKS:
-                gather_ts(2, 3, "h_bf0")
-                round_up(nc.scalar.copy, 1, UP_COLS // 4, "h_bf1")
-                quantize_up(1, UP_COLS)
+            if n < half:
+                continue
+            if n == 2 * half:
+                quantize_h(2, "h_codes2")
+                gather_ts(2, 3, "h_bf1")
+            if n == 3 * half:
+                round_up(nc.vector.tensor_copy, 1, UP_COLS // 2, "h_bf2")
+                quantize_up(1, UP_COLS // 2)
             if n >= Y_BANKS:
                 for a in range(PASSES):
                     w4_pass(i, c, a)
             finish(i, c)
+            store(i, c)

@@ -84,10 +84,14 @@ def tile_list_tabts_bias_kernel(
         w4_src = w4_words.bitcast(I32).rearrange("a p w -> p a w")
         early = UP_COLS // 2
         nc.sync.dma_start(w4[:, :, :early], w4_src[:, :, :early])
-        load_tab(1, 0, T)
-        load_down(1)
         picked = keep.tile([P, S], U8, name="picked", align_bytes=64)
         nc.vector.tensor_copy(picked[:], tab_plane[:].bitcast(U8).indirect(offsets[:]))
+        for q in range(4):
+            nc.sync.dma_start(
+                moved[32 * q : 32 * q + 4, :, :], picked[32 * q : 32 * q + 32 : 4, :].bitcast(I32)
+            )
+        load_tab(1, 0, T)
+        load_down(1)
         up_raw = {}
 
         def load_up(g):
@@ -113,10 +117,6 @@ def tile_list_tabts_bias_kernel(
         nc.tensor.transpose(bank[:], b_rows[:], identity[:])
         nc.scalar.copy(bias[:], bank[:, 0:N_TILES])
 
-        for q in range(4):
-            nc.scalar.dma_start(
-                moved[32 * q : 32 * q + 4, :, :], picked[32 * q : 32 * q + 32 : 4, :].bitcast(I32)
-            )
 
         v_codes, v_scales, ts_cols = {}, {}, {}
 

@@ -48,27 +48,24 @@ def tile_list_tabts_bias_kernel(
             words = tab_words[a].rearrange("p t i -> p (t i)").bitcast(I32)
             nc.sync.dma_start(tab[a][:, t0:t1], words[:, t0:t1])
 
-        load_tab(0, 0, T // 4)
         ts_row = keep.tile([P, T // P], F32, name="ts_row")
-        nc.gpsimd.dma_start(ts_row[:], ts[0].rearrange("(q c) -> q c", q=P))
-        b_rows = keep.tile([P, P], F32, name="b_rows")
-        nc.gpsimd.memset(b_rows[:], 0.0)
-        nc.gpsimd.dma_start(b_rows[0:N_TILES, :], b.rearrange("(i p) -> i p", p=P))
-        identity = keep.tile([P, P], F32, name="identity")
-        make_identity(nc, identity[:])
-
+        nc.sync.dma_start(ts_row[:], ts[0].rearrange("(q c) -> q c", q=P))
+        load_tab(0, 0, T // 4)
         tab_plane = keep.tile([P, T // 4], I32, name="tab_plane", align_bytes=64)
         nc.vector.memset(tab_plane[:], 0)
         nc.sync.dma_start(tab_plane[0:P:4, :], tab_scales.rearrange("a s t -> s a t").bitcast(I32))
+        identity = keep.tile([P, P], F32, name="identity")
+        make_identity(nc, identity[:])
         w4_plane = keep.tile([P, PASSES, M // 4], I32, name="w4_plane", align_bytes=64)
-        nc.vector.memset(w4_plane[:], 0)
+        nc.gpsimd.memset(w4_plane[:], 0)
+        w4_rows = w4_scales.bitcast(I32).rearrange("a (q r) n -> r q a n", r=4)
+        for r in range(4):
+            nc.gpsimd.dma_start(w4_plane[r:P:32, :, :], w4_rows[r])
+        b_rows = keep.tile([P, P], F32, name="b_rows")
+        nc.vector.memset(b_rows[:], 0.0)
+        nc.scalar.dma_start(b_rows[0:N_TILES, :], b.rearrange("(i p) -> i p", p=P))
         moved = keep.tile([P, PASSES, S // 4], I32, name="moved", align_bytes=64)
         nc.vector.memset(moved[:], 0)
-        for q in range(4):
-            nc.scalar.dma_start(
-                w4_plane[32 * q : 32 * q + 4, :, :],
-                w4_scales[:, 4 * q : 4 * q + 4, :].bitcast(I32).rearrange("a r n -> r a n"),
-            )
 
         down_raw = []
 
@@ -80,13 +77,16 @@ def tile_list_tabts_bias_kernel(
 
         load_tab(0, T // 4, T)
         load_down(0)
-        w4 = keep.tile([P, PASSES, M // 2], I32, name="w4", align_bytes=64)
+        w4 = [
+            keep.tile([P, PASSES, UP_COLS // 2], I32, name="w4_%d" % g, align_bytes=64)
+            for g in range(M // UP_COLS)
+        ]
         w4_src = w4_words.bitcast(I32).rearrange("a p w -> p a w")
         early = UP_COLS // 2
-        nc.sync.dma_start(w4[:, :, :early], w4_src[:, :, :early])
+        nc.sync.dma_start(w4[0][:], w4_src[:, :, :early])
         picked = keep.tile([P, S], U8, name="picked", align_bytes=64)
         nc.vector.tensor_copy(picked[:], tab_plane[:].bitcast(U8).indirect(offsets[:]))
-        for q in range(4):
+        for q in (0, 2, 1, 3):
             nc.sync.dma_start(
                 moved[32 * q : 32 * q + 4, :, :], picked[32 * q : 32 * q + 32 : 4, :].bitcast(I32)
             )
@@ -101,7 +101,7 @@ def tile_list_tabts_bias_kernel(
             up_raw[g] = raw
 
         load_up(0)
-        nc.sync.dma_start(w4[:, :, early:], w4_src[:, :, early:])
+        nc.sync.dma_start(w4[1][:], w4_src[:, :, early:])
         load_up(1)
 
         ts_all = keep.tile([P, T], F32, name="ts_all")
@@ -146,9 +146,11 @@ def tile_list_tabts_bias_kernel(
                 n = len(y_bank)
                 turn = n if n < Y_BANKS else ROUND[(n - Y_BANKS) % BANKS]
                 y_bank[i, c] = psum.tile([P, CHUNK], F32, name="bank%d" % turn)
+            g, k = divmod(i, UP_COLS // P)
+            words = w4[g][:, a, :].bitcast(U8)
             nc.tensor.matmul_mx(
                 out=y_bank[i, c][:],
-                lhsT=w4[:, a, :].bitcast(U8)[:, 2 * P * i : 2 * P * (i + 1)].bitcast(FP4X4),
+                lhsT=words[:, 2 * P * k : 2 * P * (k + 1)].bitcast(FP4X4),
                 lhsT_scale=w4_plane[:, a, :].bitcast(U8)[:, P * i : P * (i + 1)],
                 rhs=v_codes[a, c].bitcast(FP8X4),
                 rhs_scale=v_scales[a, c],
@@ -258,7 +260,7 @@ def tile_list_tabts_bias_kernel(
         half = N_TILES // 2
         order = [(i, c) for i0 in (0, half) for c in range(CHUNKS) for i in range(i0, i0 + half)]
         gather_codes(0, 0, CHUNKS, "v_codes0")
-        gather_ts(0, 1, "tab0")
+        gather_ts(0, CHUNKS, "tab0")
         round_down(nc.scalar.copy, 0, 0, P)
         quantize_down(0, 0, PACK)
         gather_codes(1, 0, 1, "v_codes10")
@@ -279,7 +281,6 @@ def tile_list_tabts_bias_kernel(
         quantize_h(0, "up_bf0")
         for i, c in order[:half]:
             finish(i, c)
-        gather_ts(1, 2, "h_bf0")
         make_h(1)
         quantize_h(1, "h_codes1")
         make_h(2)
@@ -290,7 +291,6 @@ def tile_list_tabts_bias_kernel(
                 continue
             if n == 2 * half:
                 quantize_h(2, "h_codes2")
-                gather_ts(2, 3, "h_bf1")
             if n == 3 * half:
                 round_up(nc.vector.tensor_copy, 1, UP_COLS // 2, "h_bf2")
                 quantize_up(1, UP_COLS // 2)

@@ -97,7 +97,8 @@ def tile_list_tabts_bias_kernel(
         def load_up(g):
             raw = keep.tile([P, PACK, UP_COLS], F32, name="up_raw%d" % g)
             cols = up[:, g * UP_COLS : (g + 1) * UP_COLS]
-            nc.sync.dma_start(raw[:], cols.rearrange("(p t) n -> p t n", t=PACK))
+            for t in range(PACK):
+                nc.sync.dma_start(raw[:, t, :], cols.rearrange("(g t i) n -> t g i n", t=PACK, i=8)[t])
             up_raw[g] = raw
 
         load_up(0)
@@ -165,10 +166,10 @@ def tile_list_tabts_bias_kernel(
         down_codes = keep.tile([P, PASSES, R], U32, name="down_codes", align_bytes=64)
         down_scales = keep.tile([P, PASSES, R], U8, name="down_scales", align_bytes=64)
 
-        def round_down(copy, a, m0, m1):
-            src = down_raw[a][:].rearrange("p j (m t) -> p m j t", t=PACK)
-            dst = down_bf[a][:].rearrange("p t m j -> p m j t")
-            copy(dst[:, m0:m1], src[:, m0:m1])
+        def round_down(copy, a, t0, t1):
+            src = down_raw[a][:].rearrange("p j (g t i) -> p t g i j", t=PACK, i=8)
+            for t in range(t0, t1):
+                copy(down_bf[a][:, t].rearrange("p (g i) j -> p g i j", i=8), src[:, t])
 
         def quantize_down(a, t0, t1):
             nc.vector.quantize_mx(
@@ -261,7 +262,7 @@ def tile_list_tabts_bias_kernel(
         order = [(i, c) for i0 in (0, half) for c in range(CHUNKS) for i in range(i0, i0 + half)]
         gather_codes(0, 0, CHUNKS, "v_codes0")
         gather_ts(0, CHUNKS, "tab0")
-        round_down(nc.scalar.copy, 0, 0, P)
+        round_down(nc.scalar.copy, 0, 0, PACK)
         quantize_down(0, 0, PACK)
         gather_codes(1, 0, 1, "v_codes10")
         gather_codes(1, 1, 2, "v_codes11")
@@ -269,8 +270,8 @@ def tile_list_tabts_bias_kernel(
             for i, c in order[:Y_BANKS]:
                 w4_pass(i, c, a)
 
-        round_down(nc.vector.tensor_copy, 1, 0, 88)
-        round_down(nc.scalar.copy, 1, 88, P)
+        round_down(nc.vector.tensor_copy, 1, 0, 2)
+        round_down(nc.scalar.copy, 1, 2, PACK)
         for t in range(PACK):
             quantize_down(1, t, t + 1)
         gather_codes(1, 2, 3, "down_bf1")

@@ -56,16 +56,24 @@ def tile_list_tabts_bias_kernel(
         nc.sync.dma_start(tab_plane[0:P:4, :], tab_scales.rearrange("a s t -> s a t").bitcast(I32))
         identity = keep.tile([P, P], F32, name="identity")
         make_identity(nc, identity[:])
-        w4_plane = keep.tile([P, PASSES, M // 4], I32, name="w4_plane", align_bytes=64)
-        nc.gpsimd.memset(w4_plane[:], 0)
-        w4_rows = w4_scales.bitcast(I32).rearrange("a (q r) n -> r q a n", r=4)
-        for r in range(4):
-            nc.gpsimd.dma_start(w4_plane[r:P:32, :, :], w4_rows[r])
+        w4_plane = [
+            keep.tile([P, PASSES, UP_COLS // 4], I32, name="w4_plane%d" % g, align_bytes=64)
+            for g in range(M // UP_COLS)
+        ]
+
+        def load_w4_scales(queue, g):
+            cols = w4_scales[:, :, g * UP_COLS : (g + 1) * UP_COLS].bitcast(I32)
+            for r in range(4):
+                queue.dma_start(w4_plane[g][r:P:32, :, :], cols.rearrange("a (q r) n -> r q a n", r=4)[r])
+
+        nc.gpsimd.memset(w4_plane[0][:], 0)
+        load_w4_scales(nc.gpsimd, 0)
         b_rows = keep.tile([P, P], F32, name="b_rows")
         nc.vector.memset(b_rows[:], 0.0)
         nc.scalar.dma_start(b_rows[0:N_TILES, :], b.rearrange("(i p) -> i p", p=P))
         moved = keep.tile([P, PASSES, S // 4], I32, name="moved", align_bytes=64)
         nc.vector.memset(moved[:], 0)
+        nc.vector.memset(w4_plane[1][:], 0)
 
         down_raw = []
 
@@ -97,12 +105,12 @@ def tile_list_tabts_bias_kernel(
         def load_up(g):
             raw = keep.tile([P, PACK, UP_COLS], F32, name="up_raw%d" % g)
             cols = up[:, g * UP_COLS : (g + 1) * UP_COLS]
-            for t in range(PACK):
-                nc.sync.dma_start(raw[:, t, :], cols.rearrange("(g t i) n -> t g i n", t=PACK, i=8)[t])
+            nc.sync.dma_start(raw[:], cols.rearrange("(p t) n -> p t n", t=PACK))
             up_raw[g] = raw
 
         load_up(0)
         nc.sync.dma_start(w4[1][:], w4_src[:, :, early:])
+        load_w4_scales(nc.sync, 1)
         load_up(1)
 
         ts_all = keep.tile([P, T], F32, name="ts_all")
@@ -142,19 +150,24 @@ def tile_list_tabts_bias_kernel(
 
         y_bank = {}
 
-        def w4_pass(i, c, a):
+        def parts(i, c):
+            width = SUB if (i, c) == (N_TILES - 1, CHUNKS - 1) else CHUNK
+            return [slice(j0, j0 + width) for j0 in range(0, CHUNK, width)]
+
+        def w4_pass(i, c, part, a):
             if a == 0:
                 n = len(y_bank)
                 turn = n if n < Y_BANKS else ROUND[(n - Y_BANKS) % BANKS]
-                y_bank[i, c] = psum.tile([P, CHUNK], F32, name="bank%d" % turn)
+                width = part.stop - part.start
+                y_bank[i, c, part.start] = psum.tile([P, width], F32, name="bank%d" % turn)
             g, k = divmod(i, UP_COLS // P)
             words = w4[g][:, a, :].bitcast(U8)
             nc.tensor.matmul_mx(
-                out=y_bank[i, c][:],
+                out=y_bank[i, c, part.start][:],
                 lhsT=words[:, 2 * P * k : 2 * P * (k + 1)].bitcast(FP4X4),
-                lhsT_scale=w4_plane[:, a, :].bitcast(U8)[:, P * i : P * (i + 1)],
-                rhs=v_codes[a, c].bitcast(FP8X4),
-                rhs_scale=v_scales[a, c],
+                lhsT_scale=w4_plane[g][:, a, :].bitcast(U8)[:, P * k : P * (k + 1)],
+                rhs=v_codes[a, c][:, part].bitcast(FP8X4),
+                rhs_scale=v_scales[a, c][:, part],
                 start=(a == 0),
                 stop=False,
             )
@@ -167,9 +180,9 @@ def tile_list_tabts_bias_kernel(
         down_scales = keep.tile([P, PASSES, R], U8, name="down_scales", align_bytes=64)
 
         def round_down(copy, a, t0, t1):
-            src = down_raw[a][:].rearrange("p j (g t i) -> p t g i j", t=PACK, i=8)
-            for t in range(t0, t1):
-                copy(down_bf[a][:, t].rearrange("p (g i) j -> p g i j", i=8), src[:, t])
+            src = down_raw[a][:].rearrange("p j (m t) -> p m j t", t=PACK)
+            dst = down_bf[a][:].rearrange("p t m j -> p m j t")
+            copy(dst[:, :, :, t0:t1], src[:, :, :, t0:t1])
 
         def quantize_down(a, t0, t1):
             nc.vector.quantize_mx(
@@ -229,37 +242,30 @@ def tile_list_tabts_bias_kernel(
                 in_=h_bf[c][:].rearrange("p n t -> p (n t)"),
             )
 
-        scaled = {}
-
-        def parts(i, c):
-            width = CHUNK // 2 if (i, c) == (N_TILES - 1, CHUNKS - 1) else CHUNK
-            return [slice(j0, j0 + width) for j0 in range(0, CHUNK, width)]
-
-        def finish(i, c):
-            cols = slice(c * CHUNK, (c + 1) * CHUNK)
+        def finish(i, c, part):
             rows = slice(i * P, (i + 1) * P)
+            bank = y_bank[i, c, part.start]
             nc.tensor.matmul_mx(
-                out=y_bank[i, c][:],
+                out=bank[:],
                 lhsT=up_codes[:, rows].bitcast(FP8X4),
                 lhsT_scale=up_scales[:, rows],
-                rhs=h_codes[c][:].bitcast(FP8X4),
-                rhs_scale=h_scales[:, cols],
+                rhs=h_codes[c][:, part].bitcast(FP8X4),
+                rhs_scale=h_scales[:, c * CHUNK : (c + 1) * CHUNK][:, part],
                 start=False,
                 stop=True,
             )
-            scaled[i, c] = stage.tile([P, CHUNK], F32, name="scaled")
-            for part in parts(i, c):
-                nc.vector.tensor_tensor(scaled[i, c][:, part], y_bank[i, c][:, part], ts_cols[c][:, part], MULT)
+            scaled = stage.tile([P, part.stop - part.start], F32, name="scaled")
+            nc.vector.tensor_tensor(scaled[:], bank[:], ts_cols[c][:, part], MULT)
+            return scaled
 
-        def store(i, c):
-            result = stage.tile([P, CHUNK], F32, name="result")
-            tile_out = out[i * P : (i + 1) * P, c * CHUNK : (c + 1) * CHUNK]
-            for part in parts(i, c):
-                nc.scalar.activation(result[:, part], scaled[i, c][:, part], IDENT, bias=bias[:, i : i + 1])
-                nc.sync.dma_start(tile_out[:, part], result[:, part])
+        def store(i, c, part, scaled):
+            result = stage.tile([P, part.stop - part.start], F32, name="result")
+            nc.scalar.activation(result[:], scaled[:], IDENT, bias=bias[:, i : i + 1])
+            nc.sync.dma_start(out[i * P : (i + 1) * P, c * CHUNK : (c + 1) * CHUNK][:, part], result[:])
 
         half = N_TILES // 2
         order = [(i, c) for i0 in (0, half) for c in range(CHUNKS) for i in range(i0, i0 + half)]
+        whole = slice(0, CHUNK)
         gather_codes(0, 0, CHUNKS, "v_codes0")
         gather_ts(0, CHUNKS, "tab0")
         round_down(nc.scalar.copy, 0, 0, PACK)
@@ -268,7 +274,7 @@ def tile_list_tabts_bias_kernel(
         gather_codes(1, 1, 2, "v_codes11")
         for a in range(PASSES):
             for i, c in order[:Y_BANKS]:
-                w4_pass(i, c, a)
+                w4_pass(i, c, whole, a)
 
         round_down(nc.vector.tensor_copy, 1, 0, 2)
         round_down(nc.scalar.copy, 1, 2, PACK)
@@ -280,23 +286,21 @@ def tile_list_tabts_bias_kernel(
         round_up(nc.vector.tensor_copy, 0, UP_COLS // 2, "up_bf0")
         quantize_up(0, UP_COLS // 2)
         quantize_h(0, "up_bf0")
-        for i, c in order[:half]:
-            finish(i, c)
+        first = [finish(i, c, whole) for i, c in order[:half]]
         make_h(1)
         quantize_h(1, "h_codes1")
         make_h(2)
-        for i, c in order[:half]:
-            store(i, c)
+        quantize_h(2, "h_codes2")
+        for (i, c), scaled in zip(order, first):
+            store(i, c, whole, scaled)
         for n, (i, c) in enumerate(order):
             if n < half:
                 continue
             if n == 2 * half:
-                quantize_h(2, "h_codes2")
-            if n == 3 * half:
-                round_up(nc.vector.tensor_copy, 1, UP_COLS // 2, "h_bf2")
+                round_up(nc.vector.tensor_copy, 1, UP_COLS // 2, "h_bf1")
                 quantize_up(1, UP_COLS // 2)
-            if n >= Y_BANKS:
-                for a in range(PASSES):
-                    w4_pass(i, c, a)
-            finish(i, c)
-            store(i, c)
+            for part in parts(i, c):
+                if n >= Y_BANKS:
+                    for a in range(PASSES):
+                        w4_pass(i, c, part, a)
+                store(i, c, part, finish(i, c, part))

@@ -25,10 +25,8 @@ CHUNKS = S // CHUNK
 SUB = 128
 N_TILES = M // P
 BANKS = 8
-Y_BANKS = 5
-H_BANKS = BANKS - Y_BANKS
+Y_BANKS = 4
 UP_COLS = 512
-ROUND = (7, 5, 6, 4, 0, 1, 2, 3)
 
 
 def tile_list_tabts_bias_kernel(
@@ -50,9 +48,9 @@ def tile_list_tabts_bias_kernel(
 
         ts_row = keep.tile([P, T // P], F32, name="ts_row")
         nc.sync.dma_start(ts_row[:], ts[0].rearrange("(q c) -> q c", q=P))
-        load_tab(0, 0, T // 4)
         tab_plane = keep.tile([P, T // 4], I32, name="tab_plane", align_bytes=64)
-        nc.vector.memset(tab_plane[:], 0)
+        nc.gpsimd.memset(tab_plane[:, : T // 8], 0)
+        nc.vector.memset(tab_plane[:, T // 8 :], 0)
         nc.sync.dma_start(tab_plane[0:P:4, :], tab_scales.rearrange("a s t -> s a t").bitcast(I32))
         identity = keep.tile([P, P], F32, name="identity")
         make_identity(nc, identity[:])
@@ -71,8 +69,11 @@ def tile_list_tabts_bias_kernel(
         b_rows = keep.tile([P, P], F32, name="b_rows")
         nc.vector.memset(b_rows[:], 0.0)
         nc.scalar.dma_start(b_rows[0:N_TILES, :], b.rearrange("(i p) -> i p", p=P))
-        moved = keep.tile([P, PASSES, S // 4], I32, name="moved", align_bytes=64)
-        nc.vector.memset(moved[:], 0)
+        moved = [
+            keep.tile([P, PASSES, CHUNK // 4], I32, name="moved%d" % c, align_bytes=64) for c in range(CHUNKS)
+        ]
+        for c in range(CHUNKS):
+            nc.vector.memset(moved[c][:], 0)
         nc.vector.memset(w4_plane[1][:], 0)
 
         down_raw = []
@@ -83,7 +84,28 @@ def tile_list_tabts_bias_kernel(
             nc.sync.dma_start(raw[:], rows.rearrange("(p j) r -> p j r", j=PACK))
             down_raw.append(raw)
 
-        load_tab(0, T // 4, T)
+        def entries(c0, c1):
+            return offsets[:, c0 * CHUNK // 16 : c1 * CHUNK // 16]
+
+        picked = {}
+
+        def gather_scales(c0, c1):
+            t = keep.tile([P, (c1 - c0) * CHUNK], U8, name="picked%d" % c0, align_bytes=64)
+            nc.vector.tensor_copy(t[:], tab_plane[:].bitcast(U8).indirect(entries(c0, c1)))
+            for c in range(c0, c1):
+                picked[c] = t, slice((c - c0) * CHUNK, (c - c0 + 1) * CHUNK)
+
+        def move_scales(c):
+            t, cols = picked[c]
+            for q in (0, 2, 1, 3):
+                nc.sync.dma_start(
+                    moved[c][32 * q : 32 * q + 4, :, :], t[32 * q : 32 * q + 32 : 4, cols].bitcast(I32)
+                )
+
+        load_tab(0, 0, T)
+        gather_scales(0, 1)
+        gather_scales(1, CHUNKS)
+        move_scales(0)
         load_down(0)
         w4 = [
             keep.tile([P, PASSES, UP_COLS // 2], I32, name="w4_%d" % g, align_bytes=64)
@@ -92,14 +114,9 @@ def tile_list_tabts_bias_kernel(
         w4_src = w4_words.bitcast(I32).rearrange("a p w -> p a w")
         early = UP_COLS // 2
         nc.sync.dma_start(w4[0][:], w4_src[:, :, :early])
-        picked = keep.tile([P, S], U8, name="picked", align_bytes=64)
-        nc.vector.tensor_copy(picked[:], tab_plane[:].bitcast(U8).indirect(offsets[:]))
-        for q in (0, 2, 1, 3):
-            nc.sync.dma_start(
-                moved[32 * q : 32 * q + 4, :, :], picked[32 * q : 32 * q + 32 : 4, :].bitcast(I32)
-            )
         load_tab(1, 0, T)
         load_down(1)
+        move_scales(1)
         up_raw = {}
 
         def load_up(g):
@@ -109,9 +126,10 @@ def tile_list_tabts_bias_kernel(
             up_raw[g] = raw
 
         load_up(0)
+        move_scales(2)
+        load_up(1)
         nc.sync.dma_start(w4[1][:], w4_src[:, :, early:])
         load_w4_scales(nc.sync, 1)
-        load_up(1)
 
         ts_all = keep.tile([P, T], F32, name="ts_all")
         ts_view = ts_all[:].rearrange("p (q c) -> p q c", q=P)
@@ -129,12 +147,9 @@ def tile_list_tabts_bias_kernel(
 
         v_codes, v_scales, ts_cols = {}, {}, {}
 
-        def entries(c0, c1):
-            return offsets[:, c0 * CHUNK // 16 : c1 * CHUNK // 16]
-
         for c in range(CHUNKS):
             for a in range(PASSES):
-                v_scales[a, c] = moved[:, a, :].bitcast(U8)[:, c * CHUNK : (c + 1) * CHUNK]
+                v_scales[a, c] = moved[c][:, a, :].bitcast(U8)
 
         def gather_codes(a, c0, c1, tag):
             t = keep.tile([P, (c1 - c0) * CHUNK], U32, name="v_codes", tag=tag, align_bytes=64)
@@ -157,7 +172,7 @@ def tile_list_tabts_bias_kernel(
         def w4_pass(i, c, part, a):
             if a == 0:
                 n = len(y_bank)
-                turn = n if n < Y_BANKS else ROUND[(n - Y_BANKS) % BANKS]
+                turn = n % BANKS
                 width = part.stop - part.start
                 y_bank[i, c, part.start] = psum.tile([P, width], F32, name="bank%d" % turn)
             g, k = divmod(i, UP_COLS // P)
@@ -195,20 +210,17 @@ def tile_list_tabts_bias_kernel(
         up_codes = keep.tile([P, M], U32, name="up_codes", align_bytes=64)
         up_scales = keep.tile([P, M], U8, name="up_scales", align_bytes=64)
 
-        def round_up(copy, g, width, tag):
-            up_bf[g] = keep.tile([P, UP_COLS, PACK], BF16, name="up_bf", tag=tag, align_bytes=64)
-            for n0 in range(0, UP_COLS, width):
-                cols = slice(n0, n0 + width)
-                copy(up_bf[g][:, cols, :], up_raw[g][:, :, cols].rearrange("p j n -> p n j"))
+        def round_up(copy, n0, n1, tag):
+            up_bf[n0] = keep.tile([P, n1 - n0, PACK], BF16, name="up_bf", tag=tag, align_bytes=64)
+            g, m0 = divmod(n0, UP_COLS)
+            copy(up_bf[n0][:], up_raw[g][:, :, m0 : m0 + n1 - n0].rearrange("p j n -> p n j"))
 
-        def quantize_up(g, width):
-            for n0 in range(0, UP_COLS, width):
-                cols = slice(g * UP_COLS + n0, g * UP_COLS + n0 + width)
-                nc.vector.quantize_mx(
-                    out=up_codes[:, cols].bitcast(FP8X4),
-                    scales=up_scales[:, cols],
-                    in_=up_bf[g][:, n0 : n0 + width, :].rearrange("p n j -> p (n j)"),
-                )
+        def quantize_up(n0, n1):
+            nc.vector.quantize_mx(
+                out=up_codes[:, n0:n1].bitcast(FP8X4),
+                scales=up_scales[:, n0:n1],
+                in_=up_bf[n0][:].rearrange("p n j -> p (n j)"),
+            )
 
         h_bf = [
             keep.tile([P, CHUNK, PACK], BF16, name="h_bf%d" % c, align_bytes=64) for c in range(CHUNKS)
@@ -216,22 +228,31 @@ def tile_list_tabts_bias_kernel(
         h_codes = {}
         h_scales = keep.tile([P, S], U8, name="h_scales", align_bytes=64)
 
+        h_bank = {}
+
+        def h_pass(c, s, a, t):
+            if (a, t) == (0, 0):
+                h_bank[c, s] = psum.tile([P, PACK, SUB], F32, name="bank%d" % (Y_BANKS + s))
+            cols = slice(s * SUB, (s + 1) * SUB)
+            nc.tensor.matmul_mx(
+                out=h_bank[c, s][:, t, :],
+                lhsT=down_codes[:, a, t * P : (t + 1) * P].bitcast(FP8X4),
+                lhsT_scale=down_scales[:, a, t * P : (t + 1) * P],
+                rhs=v_codes[a, c][:, cols].bitcast(FP8X4),
+                rhs_scale=v_scales[a, c][:, cols],
+                start=(a, t) == (0, 0),
+                stop=(a, t) == (PASSES - 1, PACK - 1),
+            )
+
+        def round_h(c, s):
+            nc.scalar.copy(h_bf[c][:, s * SUB : (s + 1) * SUB, :], h_bank[c, s][:].rearrange("p t n -> p n t"))
+
         def make_h(c):
-            for s0 in range(0, CHUNK, SUB):
-                turn = Y_BANKS + (c * CHUNK + s0) // SUB % H_BANKS if c < CHUNKS - 1 else s0 // SUB
-                bank = psum.tile([P, PACK, SUB], F32, name="bank%d" % turn)
+            for s in range(CHUNK // SUB):
                 for a in range(PASSES):
                     for t in range(PACK):
-                        nc.tensor.matmul_mx(
-                            out=bank[:, t, :],
-                            lhsT=down_codes[:, a, t * P : (t + 1) * P].bitcast(FP8X4),
-                            lhsT_scale=down_scales[:, a, t * P : (t + 1) * P],
-                            rhs=v_codes[a, c][:, s0 : s0 + SUB].bitcast(FP8X4),
-                            rhs_scale=v_scales[a, c][:, s0 : s0 + SUB],
-                            start=(a == 0 and t == 0),
-                            stop=(a == PASSES - 1 and t == PACK - 1),
-                        )
-                nc.scalar.copy(h_bf[c][:, s0 : s0 + SUB, :], bank[:].rearrange("p t n -> p n t"))
+                        h_pass(c, s, a, t)
+                round_h(c, s)
 
         def quantize_h(c, tag):
             cols = slice(c * CHUNK, (c + 1) * CHUNK)
@@ -266,41 +287,54 @@ def tile_list_tabts_bias_kernel(
         half = N_TILES // 2
         order = [(i, c) for i0 in (0, half) for c in range(CHUNKS) for i in range(i0, i0 + half)]
         whole = slice(0, CHUNK)
+        quarter = UP_COLS // 2
+        subs = range(CHUNK // SUB)
         gather_codes(0, 0, CHUNKS, "v_codes0")
-        gather_ts(0, CHUNKS, "tab0")
+        gather_ts(0, 2, "tab0")
+        for i, c in order[:Y_BANKS]:
+            w4_pass(i, c, whole, 0)
         round_down(nc.scalar.copy, 0, 0, PACK)
         quantize_down(0, 0, PACK)
+        for s in subs:
+            for t in range(PACK):
+                h_pass(0, s, 0, t)
         gather_codes(1, 0, 1, "v_codes10")
         gather_codes(1, 1, 2, "v_codes11")
-        for a in range(PASSES):
-            for i, c in order[:Y_BANKS]:
-                w4_pass(i, c, whole, a)
+        for i, c in order[:Y_BANKS]:
+            w4_pass(i, c, whole, 1)
 
         round_down(nc.vector.tensor_copy, 1, 0, 2)
         round_down(nc.scalar.copy, 1, 2, PACK)
         for t in range(PACK):
             quantize_down(1, t, t + 1)
+            for s in subs:
+                h_pass(0, s, 1, t)
+        for s in subs:
+            round_h(0, s)
         gather_codes(1, 2, 3, "down_bf1")
 
-        make_h(0)
-        round_up(nc.vector.tensor_copy, 0, UP_COLS // 2, "up_bf0")
-        quantize_up(0, UP_COLS // 2)
+        round_up(nc.vector.tensor_copy, 0, quarter, "up_bf0")
+        quantize_up(0, quarter)
         quantize_h(0, "up_bf0")
-        first = [finish(i, c, whole) for i, c in order[:half]]
+        round_up(nc.vector.tensor_copy, quarter, UP_COLS, "h_bf0")
+        quantize_up(quarter, UP_COLS)
         make_h(1)
-        quantize_h(1, "h_codes1")
+        quantize_h(1, "h_bf0")
+        gather_ts(2, 3, "h_bf1")
         make_h(2)
+        first = [finish(i, c, whole) for i, c in order[:2]]
         quantize_h(2, "h_codes2")
-        for (i, c), scaled in zip(order, first):
-            store(i, c, whole, scaled)
+        first = first + [finish(i, c, whole) for i, c in order[2:half]]
+        late_up = list(range(UP_COLS, M, P))
         for n, (i, c) in enumerate(order):
             if n < half:
-                continue
-            if n == 2 * half:
-                round_up(nc.vector.tensor_copy, 1, UP_COLS // 2, "h_bf1")
-                quantize_up(1, UP_COLS // 2)
-            for part in parts(i, c):
-                if n >= Y_BANKS:
+                store(i, c, whole, first[n])
+            else:
+                for part in parts(i, c):
                     for a in range(PASSES):
                         w4_pass(i, c, part, a)
-                store(i, c, part, finish(i, c, part))
+                    store(i, c, part, finish(i, c, part))
+            if 2 <= n < 2 + len(late_up):
+                n0 = late_up[n - 2]
+                round_up(nc.scalar.copy, n0, n0 + P, "up_bf%d" % n0)
+                quantize_up(n0, n0 + P)

@@ -48,9 +48,9 @@ def tile_list_tabts_bias_kernel(
 
         ts_row = keep.tile([P, T // P], F32, name="ts_row")
         nc.sync.dma_start(ts_row[:], ts[0].rearrange("(q c) -> q c", q=P))
+        load_tab(0, 0, T // 8)
         tab_plane = keep.tile([P, T // 4], I32, name="tab_plane", align_bytes=64)
-        nc.gpsimd.memset(tab_plane[:, : T // 8], 0)
-        nc.vector.memset(tab_plane[:, T // 8 :], 0)
+        nc.vector.memset(tab_plane[:], 0)
         nc.sync.dma_start(tab_plane[0:P:4, :], tab_scales.rearrange("a s t -> s a t").bitcast(I32))
         identity = keep.tile([P, P], F32, name="identity")
         make_identity(nc, identity[:])
@@ -102,7 +102,7 @@ def tile_list_tabts_bias_kernel(
                     moved[c][32 * q : 32 * q + 4, :, :], t[32 * q : 32 * q + 32 : 4, cols].bitcast(I32)
                 )
 
-        load_tab(0, 0, T)
+        load_tab(0, T // 8, T)
         gather_scales(0, 1)
         gather_scales(1, CHUNKS)
         move_scales(0)
@@ -165,8 +165,8 @@ def tile_list_tabts_bias_kernel(
 
         y_bank = {}
 
-        def parts(i, c):
-            width = SUB if (i, c) == (N_TILES - 1, CHUNKS - 1) else CHUNK
+        def pieces(i, c):
+            width = {len(order) - 2: 256, len(order) - 1: 256}.get(order.index((i, c)), CHUNK)
             return [slice(j0, j0 + width) for j0 in range(0, CHUNK, width)]
 
         def w4_pass(i, c, part, a):
@@ -263,7 +263,7 @@ def tile_list_tabts_bias_kernel(
                 in_=h_bf[c][:].rearrange("p n t -> p (n t)"),
             )
 
-        def finish(i, c, part):
+        def finish(i, c, part, piece=slice(0, CHUNK)):
             rows = slice(i * P, (i + 1) * P)
             bank = y_bank[i, c, part.start]
             nc.tensor.matmul_mx(
@@ -275,8 +275,11 @@ def tile_list_tabts_bias_kernel(
                 start=False,
                 stop=True,
             )
-            scaled = stage.tile([P, part.stop - part.start], F32, name="scaled")
-            nc.vector.tensor_tensor(scaled[:], bank[:], ts_cols[c][:, part], MULT)
+            return scale(i, c, piece)
+
+        def scale(i, c, piece):
+            scaled = stage.tile([P, piece.stop - piece.start], F32, name="scaled")
+            nc.vector.tensor_tensor(scaled[:], y_bank[i, c, 0][:, piece], ts_cols[c][:, piece], MULT)
             return scaled
 
         def store(i, c, part, scaled):
@@ -330,10 +333,12 @@ def tile_list_tabts_bias_kernel(
             if n < half:
                 store(i, c, whole, first[n])
             else:
-                for part in parts(i, c):
-                    for a in range(PASSES):
-                        w4_pass(i, c, part, a)
-                    store(i, c, part, finish(i, c, part))
+                for a in range(PASSES):
+                    w4_pass(i, c, whole, a)
+                cut = pieces(i, c)
+                store(i, c, cut[0], finish(i, c, whole, cut[0]))
+                for piece in cut[1:]:
+                    store(i, c, piece, scale(i, c, piece))
             if 2 <= n < 2 + len(late_up):
                 n0 = late_up[n - 2]
                 round_up(nc.scalar.copy, n0, n0 + P, "up_bf%d" % n0)

@@ -1,3 +1,4 @@
+import math
 from contextlib import ExitStack
 
 import concourse.mybir as mybir
@@ -27,6 +28,7 @@ N_TILES = M // P
 BANKS = 8
 Y_BANKS = 4
 UP_COLS = 512
+LEAD = 32
 
 
 def tile_list_tabts_bias_kernel(
@@ -40,7 +42,12 @@ def tile_list_tabts_bias_kernel(
 
         offsets = keep.tile([P, S // 16], U16, name="offsets")
         nc.sync.dma_start(offsets[:], offs)
-        tab = [keep.tile([P, T], I32, name="tab%d" % a, align_bytes=64) for a in range(PASSES)]
+        tab = [keep.tile([P, T], I32, name="tab%d" % a, align_bytes=256) for a in range(PASSES)]
+
+        def stationary(shape, dtype, name):
+            words = math.prod(shape)
+            t = keep.tile([P, LEAD + words], dtype, name=name, align_bytes=256)
+            return t[:, LEAD:].rearrange("p (a w) -> p a w", a=shape[0])
 
         def load_tab(a, t0, t1):
             words = tab_words[a].rearrange("p t i -> p (t i)").bitcast(I32)
@@ -49,13 +56,13 @@ def tile_list_tabts_bias_kernel(
         ts_row = keep.tile([P, T // P], F32, name="ts_row")
         nc.sync.dma_start(ts_row[:], ts[0].rearrange("(q c) -> q c", q=P))
         load_tab(0, 0, T // 8)
-        tab_plane = keep.tile([P, T // 4], I32, name="tab_plane", align_bytes=64)
+        tab_plane = keep.tile([P, T // 4], I32, name="tab_plane", align_bytes=256)
         nc.vector.memset(tab_plane[:], 0)
         nc.sync.dma_start(tab_plane[0:P:4, :], tab_scales.rearrange("a s t -> s a t").bitcast(I32))
         identity = keep.tile([P, P], F32, name="identity")
         make_identity(nc, identity[:])
         w4_plane = [
-            keep.tile([P, PASSES, UP_COLS // 4], I32, name="w4_plane%d" % g, align_bytes=64)
+            keep.tile([P, PASSES, UP_COLS // 4], I32, name="w4_plane%d" % g, align_bytes=256)
             for g in range(M // UP_COLS)
         ]
 
@@ -70,7 +77,7 @@ def tile_list_tabts_bias_kernel(
         nc.vector.memset(b_rows[:], 0.0)
         nc.scalar.dma_start(b_rows[0:N_TILES, :], b.rearrange("(i p) -> i p", p=P))
         moved = [
-            keep.tile([P, PASSES, CHUNK // 4], I32, name="moved%d" % c, align_bytes=64) for c in range(CHUNKS)
+            keep.tile([P, PASSES, CHUNK // 4], I32, name="moved%d" % c, align_bytes=256) for c in range(CHUNKS)
         ]
         for c in range(CHUNKS):
             nc.vector.memset(moved[c][:], 0)
@@ -79,7 +86,7 @@ def tile_list_tabts_bias_kernel(
         down_raw = []
 
         def load_down(a):
-            raw = keep.tile([P, PACK, R], F32, name="down_raw%d" % a, align_bytes=64)
+            raw = keep.tile([P, PACK, R], F32, name="down_raw%d" % a, align_bytes=256)
             rows = down[a * P * PACK : (a + 1) * P * PACK, :]
             nc.sync.dma_start(raw[:], rows.rearrange("(p j) r -> p j r", j=PACK))
             down_raw.append(raw)
@@ -90,7 +97,7 @@ def tile_list_tabts_bias_kernel(
         picked = {}
 
         def gather_scales(c0, c1):
-            t = keep.tile([P, (c1 - c0) * CHUNK], U8, name="picked%d" % c0, align_bytes=64)
+            t = keep.tile([P, (c1 - c0) * CHUNK], U8, name="picked%d" % c0, align_bytes=256)
             nc.vector.tensor_copy(t[:], tab_plane[:].bitcast(U8).indirect(entries(c0, c1)))
             for c in range(c0, c1):
                 picked[c] = t, slice((c - c0) * CHUNK, (c - c0 + 1) * CHUNK)
@@ -107,13 +114,10 @@ def tile_list_tabts_bias_kernel(
         gather_scales(1, CHUNKS)
         move_scales(0)
         load_down(0)
-        w4 = [
-            keep.tile([P, PASSES, UP_COLS // 2], I32, name="w4_%d" % g, align_bytes=64)
-            for g in range(M // UP_COLS)
-        ]
+        w4 = [stationary([PASSES, UP_COLS // 2], I32, "w4_%d" % g) for g in range(M // UP_COLS)]
         w4_src = w4_words.bitcast(I32).rearrange("a p w -> p a w")
         early = UP_COLS // 2
-        nc.sync.dma_start(w4[0][:], w4_src[:, :, :early])
+        nc.sync.dma_start(w4[0], w4_src[:, :, :early])
         load_tab(1, 0, T)
         load_down(1)
         move_scales(1)
@@ -128,7 +132,7 @@ def tile_list_tabts_bias_kernel(
         load_up(0)
         move_scales(2)
         load_up(1)
-        nc.sync.dma_start(w4[1][:], w4_src[:, :, early:])
+        nc.sync.dma_start(w4[1], w4_src[:, :, early:])
         load_w4_scales(nc.sync, 1)
 
         ts_all = keep.tile([P, T], F32, name="ts_all")
@@ -152,13 +156,13 @@ def tile_list_tabts_bias_kernel(
                 v_scales[a, c] = moved[c][:, a, :].bitcast(U8)
 
         def gather_codes(a, c0, c1, tag):
-            t = keep.tile([P, (c1 - c0) * CHUNK], U32, name="v_codes", tag=tag, align_bytes=64)
+            t = keep.tile([P, (c1 - c0) * CHUNK], U32, name="v_codes", tag=tag, align_bytes=256)
             nc.vector.tensor_copy(t[:], tab[a][:].bitcast(U32).indirect(entries(c0, c1)))
             for c in range(c0, c1):
                 v_codes[a, c] = t[:, (c - c0) * CHUNK : (c - c0 + 1) * CHUNK]
 
         def gather_ts(c0, c1, tag):
-            t = keep.tile([P, (c1 - c0) * CHUNK], F32, name="ts_cols", tag=tag, align_bytes=64)
+            t = keep.tile([P, (c1 - c0) * CHUNK], F32, name="ts_cols", tag=tag, align_bytes=256)
             nc.vector.tensor_copy(t[:], ts_all[:].indirect(entries(c0, c1)))
             for c in range(c0, c1):
                 ts_cols[c] = t[:, (c - c0) * CHUNK : (c - c0 + 1) * CHUNK]
@@ -188,11 +192,11 @@ def tile_list_tabts_bias_kernel(
             )
 
         down_bf = [
-            keep.tile([P, PACK, P, PACK], BF16, name="down_bf%d" % a, align_bytes=64)
+            keep.tile([P, PACK, P, PACK], BF16, name="down_bf%d" % a, align_bytes=256)
             for a in range(PASSES)
         ]
-        down_codes = keep.tile([P, PASSES, R], U32, name="down_codes", align_bytes=64)
-        down_scales = keep.tile([P, PASSES, R], U8, name="down_scales", align_bytes=64)
+        down_codes = stationary([PASSES, R], U32, "down_codes")
+        down_scales = keep.tile([P, PASSES, R], U8, name="down_scales", align_bytes=256)
 
         def round_down(copy, a, t0, t1):
             src = down_raw[a][:].rearrange("p j (m t) -> p m j t", t=PACK)
@@ -207,11 +211,11 @@ def tile_list_tabts_bias_kernel(
             )
 
         up_bf = {}
-        up_codes = keep.tile([P, M], U32, name="up_codes", align_bytes=64)
-        up_scales = keep.tile([P, M], U8, name="up_scales", align_bytes=64)
+        up_codes = stationary([1, M], U32, "up_codes")[:, 0, :]
+        up_scales = keep.tile([P, M], U8, name="up_scales", align_bytes=256)
 
         def round_up(copy, n0, n1, tag):
-            up_bf[n0] = keep.tile([P, n1 - n0, PACK], BF16, name="up_bf", tag=tag, align_bytes=64)
+            up_bf[n0] = keep.tile([P, n1 - n0, PACK], BF16, name="up_bf", tag=tag, align_bytes=256)
             g, m0 = divmod(n0, UP_COLS)
             copy(up_bf[n0][:], up_raw[g][:, :, m0 : m0 + n1 - n0].rearrange("p j n -> p n j"))
 
@@ -223,10 +227,10 @@ def tile_list_tabts_bias_kernel(
             )
 
         h_bf = [
-            keep.tile([P, CHUNK, PACK], BF16, name="h_bf%d" % c, align_bytes=64) for c in range(CHUNKS)
+            keep.tile([P, CHUNK, PACK], BF16, name="h_bf%d" % c, align_bytes=256) for c in range(CHUNKS)
         ]
         h_codes = {}
-        h_scales = keep.tile([P, S], U8, name="h_scales", align_bytes=64)
+        h_scales = keep.tile([P, S], U8, name="h_scales", align_bytes=256)
 
         h_bank = {}
 
@@ -256,7 +260,7 @@ def tile_list_tabts_bias_kernel(
 
         def quantize_h(c, tag):
             cols = slice(c * CHUNK, (c + 1) * CHUNK)
-            h_codes[c] = keep.tile([P, CHUNK], U32, name="h_codes", tag=tag, align_bytes=64)
+            h_codes[c] = keep.tile([P, CHUNK], U32, name="h_codes", tag=tag, align_bytes=256)
             nc.vector.quantize_mx(
                 out=h_codes[c][:].bitcast(FP8X4),
                 scales=h_scales[:, cols],

@@ -21,14 +21,21 @@ IDENT = mybir.ActivationFunctionType.Identity
 P = 128
 PACK = 4
 PASSES = K // (P * PACK)
+GROUP = 16
+QUADRANT = 32
 CHUNK = 512
 CHUNKS = S // CHUNK
 SUB = 128
+SUBS = CHUNK // SUB
 N_TILES = M // P
 BANKS = 8
-Y_BANKS = 4
-UP_COLS = 512
-LEAD = 32
+EARLY = BANKS - SUBS
+HALF = M // 2
+HEAD = T // 8
+STAGE = 8
+ALIGN = 256
+WORD_LEAD = ALIGN // 2
+SCALE_LEAD = ALIGN // 4
 
 
 def tile_list_tabts_bias_kernel(
@@ -37,17 +44,16 @@ def tile_list_tabts_bias_kernel(
     nc = tc.nc
     with ExitStack() as ctx:
         keep = ctx.enter_context(tc.tile_pool(name="keep", bufs=1))
-        stage = ctx.enter_context(tc.tile_pool(name="stage", bufs=8))
+        stage = ctx.enter_context(tc.tile_pool(name="stage", bufs=STAGE))
         psum = ctx.enter_context(tc.psum_pool(name="psum", bufs=1))
 
-        offsets = keep.tile([P, S // 16], U16, name="offsets")
-        nc.sync.dma_start(offsets[:], offs)
-        tab = [keep.tile([P, T], I32, name="tab%d" % a, align_bytes=256) for a in range(PASSES)]
+        def stationary(shape, dtype, name, lead):
+            padded = keep.tile([P, lead + math.prod(shape)], dtype, name=name, align_bytes=ALIGN)
+            return padded[:, lead:].rearrange("p (a w) -> p a w", a=shape[0])
 
-        def stationary(shape, dtype, name):
-            words = math.prod(shape)
-            t = keep.tile([P, LEAD + words], dtype, name=name, align_bytes=256)
-            return t[:, LEAD:].rearrange("p (a w) -> p a w", a=shape[0])
+        offsets = keep.tile([P, S // GROUP], U16, name="offsets")
+        nc.sync.dma_start(offsets[:], offs)
+        tab = [keep.tile([P, T], I32, name="tab%d" % a, align_bytes=ALIGN) for a in range(PASSES)]
 
         def load_tab(a, t0, t1):
             words = tab_words[a].rearrange("p t i -> p (t i)").bitcast(I32)
@@ -55,87 +61,85 @@ def tile_list_tabts_bias_kernel(
 
         ts_row = keep.tile([P, T // P], F32, name="ts_row")
         nc.sync.dma_start(ts_row[:], ts[0].rearrange("(q c) -> q c", q=P))
-        load_tab(0, 0, T // 8)
-        tab_plane = keep.tile([P, T // 4], I32, name="tab_plane", align_bytes=256)
-        nc.vector.memset(tab_plane[:], 0)
-        nc.sync.dma_start(tab_plane[0:P:4, :], tab_scales.rearrange("a s t -> s a t").bitcast(I32))
+        load_tab(0, 0, HEAD)
+        tab_rows = keep.tile([P, T // 4], I32, name="tab_rows", align_bytes=ALIGN)
+        nc.vector.memset(tab_rows[:], 0)
+        nc.sync.dma_start(tab_rows[0:P:4, :], tab_scales.rearrange("a s t -> s a t").bitcast(I32))
         identity = keep.tile([P, P], F32, name="identity")
         make_identity(nc, identity[:])
         w4_plane = [
-            keep.tile([P, PASSES, UP_COLS // 4], I32, name="w4_plane%d" % g, align_bytes=256)
-            for g in range(M // UP_COLS)
+            stationary([PASSES, HALF // 4], I32, "w4_plane%d" % g, SCALE_LEAD // 4) for g in range(M // HALF)
         ]
 
         def load_w4_scales(queue, g):
-            cols = w4_scales[:, :, g * UP_COLS : (g + 1) * UP_COLS].bitcast(I32)
+            cols = w4_scales[:, :, g * HALF : (g + 1) * HALF].bitcast(I32)
             for r in range(4):
-                queue.dma_start(w4_plane[g][r:P:32, :, :], cols.rearrange("a (q r) n -> r q a n", r=4)[r])
+                queue.dma_start(w4_plane[g][r:P:QUADRANT, :, :], cols.rearrange("a (q r) n -> r q a n", r=4)[r])
 
         nc.gpsimd.memset(w4_plane[0][:], 0)
         load_w4_scales(nc.gpsimd, 0)
         b_rows = keep.tile([P, P], F32, name="b_rows")
         nc.vector.memset(b_rows[:], 0.0)
         nc.scalar.dma_start(b_rows[0:N_TILES, :], b.rearrange("(i p) -> i p", p=P))
-        moved = [
-            keep.tile([P, PASSES, CHUNK // 4], I32, name="moved%d" % c, align_bytes=256) for c in range(CHUNKS)
+        v_plane = [
+            keep.tile([P, PASSES, CHUNK // 4], I32, name="v_plane%d" % c, align_bytes=ALIGN) for c in range(CHUNKS)
         ]
         for c in range(CHUNKS):
-            nc.vector.memset(moved[c][:], 0)
+            nc.vector.memset(v_plane[c][:], 0)
         nc.vector.memset(w4_plane[1][:], 0)
 
         down_raw = []
 
         def load_down(a):
-            raw = keep.tile([P, PACK, R], F32, name="down_raw%d" % a, align_bytes=256)
+            raw = keep.tile([P, PACK, R], F32, name="down_raw%d" % a, align_bytes=ALIGN)
             rows = down[a * P * PACK : (a + 1) * P * PACK, :]
             nc.sync.dma_start(raw[:], rows.rearrange("(p j) r -> p j r", j=PACK))
             down_raw.append(raw)
 
         def entries(c0, c1):
-            return offsets[:, c0 * CHUNK // 16 : c1 * CHUNK // 16]
+            return offsets[:, c0 * CHUNK // GROUP : c1 * CHUNK // GROUP]
 
         picked = {}
 
         def gather_scales(c0, c1):
-            t = keep.tile([P, (c1 - c0) * CHUNK], U8, name="picked%d" % c0, align_bytes=256)
-            nc.vector.tensor_copy(t[:], tab_plane[:].bitcast(U8).indirect(entries(c0, c1)))
+            rows = keep.tile([P, (c1 - c0) * CHUNK], U8, name="picked%d" % c0, align_bytes=ALIGN)
+            nc.vector.tensor_copy(rows[:], tab_rows[:].bitcast(U8).indirect(entries(c0, c1)))
             for c in range(c0, c1):
-                picked[c] = t, slice((c - c0) * CHUNK, (c - c0 + 1) * CHUNK)
+                picked[c] = rows[:, (c - c0) * CHUNK : (c - c0 + 1) * CHUNK]
 
         def move_scales(c):
-            t, cols = picked[c]
             for q in (0, 2, 1, 3):
-                nc.sync.dma_start(
-                    moved[c][32 * q : 32 * q + 4, :, :], t[32 * q : 32 * q + 32 : 4, cols].bitcast(I32)
-                )
+                p0 = QUADRANT * q
+                nc.sync.dma_start(v_plane[c][p0 : p0 + 4, :, :], picked[c][p0 : p0 + QUADRANT : 4, :].bitcast(I32))
 
-        load_tab(0, T // 8, T)
+        load_tab(0, HEAD, T)
         gather_scales(0, 1)
         gather_scales(1, CHUNKS)
         move_scales(0)
         load_down(0)
-        w4 = [stationary([PASSES, UP_COLS // 2], I32, "w4_%d" % g) for g in range(M // UP_COLS)]
-        w4_src = w4_words.bitcast(I32).rearrange("a p w -> p a w")
-        early = UP_COLS // 2
-        nc.sync.dma_start(w4[0], w4_src[:, :, :early])
+        w4_early = [stationary([1, HALF // 2], I32, "w4_early%d" % a, WORD_LEAD // 4) for a in range(PASSES)]
+        w4_late = stationary([PASSES, HALF // 2], I32, "w4_late", WORD_LEAD // 4)
+        w4_pairs = w4_words.bitcast(I32).rearrange("a p w -> p a w")
+        nc.sync.dma_start(w4_early[0][:, 0, :], w4_pairs[:, 0, : HALF // 2])
         load_tab(1, 0, T)
+        nc.sync.dma_start(w4_early[1][:, 0, :], w4_pairs[:, 1, : HALF // 2])
         load_down(1)
         move_scales(1)
         up_raw = {}
 
         def load_up(g):
-            raw = keep.tile([P, PACK, UP_COLS], F32, name="up_raw%d" % g)
-            cols = up[:, g * UP_COLS : (g + 1) * UP_COLS]
+            raw = keep.tile([P, PACK, HALF], F32, name="up_raw%d" % g, align_bytes=ALIGN)
+            cols = up[:, g * HALF : (g + 1) * HALF]
             nc.sync.dma_start(raw[:], cols.rearrange("(p t) n -> p t n", t=PACK))
             up_raw[g] = raw
 
         load_up(0)
         move_scales(2)
         load_up(1)
-        nc.sync.dma_start(w4[1], w4_src[:, :, early:])
+        nc.sync.dma_start(w4_late, w4_pairs[:, :, HALF // 2 :])
         load_w4_scales(nc.sync, 1)
 
-        ts_all = keep.tile([P, T], F32, name="ts_all")
+        ts_all = keep.tile([P, T], F32, name="ts_all", align_bytes=ALIGN)
         ts_view = ts_all[:].rearrange("p (q c) -> p q c", q=P)
         for c0 in range(0, T // P, 4):
             bank = psum.tile([P, 4, P], F32, name="bank%d" % (c0 // 4))
@@ -148,55 +152,45 @@ def tile_list_tabts_bias_kernel(
         nc.tensor.transpose(bank[:], b_rows[:], identity[:])
         nc.scalar.copy(bias[:], bank[:, 0:N_TILES])
 
+        v_codes, ts_cols = {}, {}
 
-        v_codes, v_scales, ts_cols = {}, {}, {}
-
-        for c in range(CHUNKS):
-            for a in range(PASSES):
-                v_scales[a, c] = moved[c][:, a, :].bitcast(U8)
+        def v_scales(a, c):
+            return v_plane[c][:, a, :].bitcast(U8)
 
         def gather_codes(a, c0, c1, tag):
-            t = keep.tile([P, (c1 - c0) * CHUNK], U32, name="v_codes", tag=tag, align_bytes=256)
-            nc.vector.tensor_copy(t[:], tab[a][:].bitcast(U32).indirect(entries(c0, c1)))
+            words = keep.tile([P, (c1 - c0) * CHUNK], U32, name="v_codes", tag=tag, align_bytes=ALIGN)
+            nc.vector.tensor_copy(words[:], tab[a][:].bitcast(U32).indirect(entries(c0, c1)))
             for c in range(c0, c1):
-                v_codes[a, c] = t[:, (c - c0) * CHUNK : (c - c0 + 1) * CHUNK]
+                v_codes[a, c] = words[:, (c - c0) * CHUNK : (c - c0 + 1) * CHUNK]
 
         def gather_ts(c0, c1, tag):
-            t = keep.tile([P, (c1 - c0) * CHUNK], F32, name="ts_cols", tag=tag, align_bytes=256)
-            nc.vector.tensor_copy(t[:], ts_all[:].indirect(entries(c0, c1)))
+            cols = keep.tile([P, (c1 - c0) * CHUNK], F32, name="ts_cols", tag=tag, align_bytes=ALIGN)
+            nc.vector.tensor_copy(cols[:], ts_all[:].indirect(entries(c0, c1)))
             for c in range(c0, c1):
-                ts_cols[c] = t[:, (c - c0) * CHUNK : (c - c0 + 1) * CHUNK]
+                ts_cols[c] = cols[:, (c - c0) * CHUNK : (c - c0 + 1) * CHUNK]
 
         y_bank = {}
 
-        def pieces(i, c):
-            width = {len(order) - 2: 256, len(order) - 1: 256}.get(order.index((i, c)), CHUNK)
-            return [slice(j0, j0 + width) for j0 in range(0, CHUNK, width)]
-
-        def w4_pass(i, c, part, a):
+        def w4_pass(i, c, a):
             if a == 0:
-                n = len(y_bank)
-                turn = n % BANKS
-                width = part.stop - part.start
-                y_bank[i, c, part.start] = psum.tile([P, width], F32, name="bank%d" % turn)
-            g, k = divmod(i, UP_COLS // P)
-            words = w4[g][:, a, :].bitcast(U8)
+                y_bank[i, c] = psum.tile([P, CHUNK], F32, name="bank%d" % (len(y_bank) % BANKS))
+            g, n = divmod(i * P, HALF)
+            words = (w4_early[a][:, 0, :] if g == 0 else w4_late[:, a, :]).bitcast(U8)
             nc.tensor.matmul_mx(
-                out=y_bank[i, c, part.start][:],
-                lhsT=words[:, 2 * P * k : 2 * P * (k + 1)].bitcast(FP4X4),
-                lhsT_scale=w4_plane[g][:, a, :].bitcast(U8)[:, P * k : P * (k + 1)],
-                rhs=v_codes[a, c][:, part].bitcast(FP8X4),
-                rhs_scale=v_scales[a, c][:, part],
+                out=y_bank[i, c][:],
+                lhsT=words[:, 2 * n : 2 * (n + P)].bitcast(FP4X4),
+                lhsT_scale=w4_plane[g][:, a, :].bitcast(U8)[:, n : n + P],
+                rhs=v_codes[a, c].bitcast(FP8X4),
+                rhs_scale=v_scales(a, c),
                 start=(a == 0),
                 stop=False,
             )
 
         down_bf = [
-            keep.tile([P, PACK, P, PACK], BF16, name="down_bf%d" % a, align_bytes=256)
-            for a in range(PASSES)
+            keep.tile([P, PACK, P, PACK], BF16, name="down_bf%d" % a, align_bytes=ALIGN) for a in range(PASSES)
         ]
-        down_codes = stationary([PASSES, R], U32, "down_codes")
-        down_scales = keep.tile([P, PASSES, R], U8, name="down_scales", align_bytes=256)
+        down_codes = stationary([PASSES, R], U32, "down_codes", WORD_LEAD // 4)
+        down_scales = stationary([PASSES, R], U8, "down_scales", SCALE_LEAD)
 
         def round_down(copy, a, t0, t1):
             src = down_raw[a][:].rearrange("p j (m t) -> p m j t", t=PACK)
@@ -211,39 +205,35 @@ def tile_list_tabts_bias_kernel(
             )
 
         up_bf = {}
-        up_codes = stationary([1, M], U32, "up_codes")[:, 0, :]
-        up_scales = keep.tile([P, M], U8, name="up_scales", align_bytes=256)
+        up_codes = stationary([1, M], U32, "up_codes", WORD_LEAD // 4)[:, 0, :]
+        up_scales = stationary([1, M], U8, "up_scales", SCALE_LEAD)[:, 0, :]
 
         def round_up(copy, n0, n1, tag):
-            up_bf[n0] = keep.tile([P, n1 - n0, PACK], BF16, name="up_bf", tag=tag, align_bytes=256)
-            g, m0 = divmod(n0, UP_COLS)
-            copy(up_bf[n0][:], up_raw[g][:, :, m0 : m0 + n1 - n0].rearrange("p j n -> p n j"))
+            up_bf[n0] = keep.tile([P, n1 - n0, PACK], BF16, name="up_bf", tag=tag, align_bytes=ALIGN)
+            g, n = divmod(n0, HALF)
+            copy(up_bf[n0][:], up_raw[g][:, :, n : n + n1 - n0].rearrange("p t n -> p n t"))
 
         def quantize_up(n0, n1):
             nc.vector.quantize_mx(
                 out=up_codes[:, n0:n1].bitcast(FP8X4),
                 scales=up_scales[:, n0:n1],
-                in_=up_bf[n0][:].rearrange("p n j -> p (n j)"),
+                in_=up_bf[n0][:].rearrange("p n t -> p (n t)"),
             )
 
-        h_bf = [
-            keep.tile([P, CHUNK, PACK], BF16, name="h_bf%d" % c, align_bytes=256) for c in range(CHUNKS)
-        ]
-        h_codes = {}
-        h_scales = keep.tile([P, S], U8, name="h_scales", align_bytes=256)
-
-        h_bank = {}
+        h_bf = [keep.tile([P, CHUNK, PACK], BF16, name="h_bf%d" % c, align_bytes=ALIGN) for c in range(CHUNKS)]
+        h_codes, h_bank = {}, {}
+        h_scales = keep.tile([P, S], U8, name="h_scales", align_bytes=ALIGN)
 
         def h_pass(c, s, a, t):
             if (a, t) == (0, 0):
-                h_bank[c, s] = psum.tile([P, PACK, SUB], F32, name="bank%d" % (Y_BANKS + s))
+                h_bank[c, s] = psum.tile([P, PACK, SUB], F32, name="bank%d" % (EARLY + s))
             cols = slice(s * SUB, (s + 1) * SUB)
             nc.tensor.matmul_mx(
                 out=h_bank[c, s][:, t, :],
                 lhsT=down_codes[:, a, t * P : (t + 1) * P].bitcast(FP8X4),
                 lhsT_scale=down_scales[:, a, t * P : (t + 1) * P],
                 rhs=v_codes[a, c][:, cols].bitcast(FP8X4),
-                rhs_scale=v_scales[a, c][:, cols],
+                rhs_scale=v_scales(a, c)[:, cols],
                 start=(a, t) == (0, 0),
                 stop=(a, t) == (PASSES - 1, PACK - 1),
             )
@@ -252,98 +242,103 @@ def tile_list_tabts_bias_kernel(
             nc.scalar.copy(h_bf[c][:, s * SUB : (s + 1) * SUB, :], h_bank[c, s][:].rearrange("p t n -> p n t"))
 
         def make_h(c):
-            for s in range(CHUNK // SUB):
+            for s in range(SUBS):
                 for a in range(PASSES):
                     for t in range(PACK):
                         h_pass(c, s, a, t)
                 round_h(c, s)
 
         def quantize_h(c, tag):
-            cols = slice(c * CHUNK, (c + 1) * CHUNK)
-            h_codes[c] = keep.tile([P, CHUNK], U32, name="h_codes", tag=tag, align_bytes=256)
+            h_codes[c] = keep.tile([P, CHUNK], U32, name="h_codes", tag=tag, align_bytes=ALIGN)
             nc.vector.quantize_mx(
                 out=h_codes[c][:].bitcast(FP8X4),
-                scales=h_scales[:, cols],
+                scales=h_scales[:, c * CHUNK : (c + 1) * CHUNK],
                 in_=h_bf[c][:].rearrange("p n t -> p (n t)"),
             )
 
-        def finish(i, c, part, piece=slice(0, CHUNK)):
+        def up_pass(i, c):
             rows = slice(i * P, (i + 1) * P)
-            bank = y_bank[i, c, part.start]
             nc.tensor.matmul_mx(
-                out=bank[:],
+                out=y_bank[i, c][:],
                 lhsT=up_codes[:, rows].bitcast(FP8X4),
                 lhsT_scale=up_scales[:, rows],
-                rhs=h_codes[c][:, part].bitcast(FP8X4),
-                rhs_scale=h_scales[:, c * CHUNK : (c + 1) * CHUNK][:, part],
+                rhs=h_codes[c][:].bitcast(FP8X4),
+                rhs_scale=h_scales[:, c * CHUNK : (c + 1) * CHUNK],
                 start=False,
                 stop=True,
             )
-            return scale(i, c, piece)
 
-        def scale(i, c, piece):
-            scaled = stage.tile([P, piece.stop - piece.start], F32, name="scaled")
-            nc.vector.tensor_tensor(scaled[:], y_bank[i, c, 0][:, piece], ts_cols[c][:, piece], MULT)
+        def scale(i, c, cols):
+            scaled = stage.tile([P, cols.stop - cols.start], F32, name="scaled", align_bytes=ALIGN)
+            nc.vector.tensor_tensor(scaled[:], y_bank[i, c][:, cols], ts_cols[c][:, cols], MULT)
             return scaled
 
-        def store(i, c, part, scaled):
-            result = stage.tile([P, part.stop - part.start], F32, name="result")
+        def store(i, c, cols, scaled):
+            result = stage.tile([P, cols.stop - cols.start], F32, name="result", align_bytes=ALIGN)
             nc.scalar.activation(result[:], scaled[:], IDENT, bias=bias[:, i : i + 1])
-            nc.sync.dma_start(out[i * P : (i + 1) * P, c * CHUNK : (c + 1) * CHUNK][:, part], result[:])
+            nc.sync.dma_start(out[i * P : (i + 1) * P, c * CHUNK : (c + 1) * CHUNK][:, cols], result[:])
 
-        half = N_TILES // 2
-        order = [(i, c) for i0 in (0, half) for c in range(CHUNKS) for i in range(i0, i0 + half)]
+        order = [(i, c) for i0 in (0, HALF // P) for c in range(CHUNKS) for i in range(i0, i0 + HALF // P)]
         whole = slice(0, CHUNK)
-        quarter = UP_COLS // 2
-        subs = range(CHUNK // SUB)
+
         gather_codes(0, 0, CHUNKS, "v_codes0")
         gather_ts(0, 2, "tab0")
-        for i, c in order[:Y_BANKS]:
-            w4_pass(i, c, whole, 0)
+        for i, c in order[:EARLY]:
+            w4_pass(i, c, 0)
         round_down(nc.scalar.copy, 0, 0, PACK)
         quantize_down(0, 0, PACK)
-        for s in subs:
+        for s in range(SUBS):
             for t in range(PACK):
                 h_pass(0, s, 0, t)
         gather_codes(1, 0, 1, "v_codes10")
         gather_codes(1, 1, 2, "v_codes11")
-        for i, c in order[:Y_BANKS]:
-            w4_pass(i, c, whole, 1)
+        for i, c in order[:EARLY]:
+            w4_pass(i, c, 1)
 
-        round_down(nc.vector.tensor_copy, 1, 0, 2)
-        round_down(nc.scalar.copy, 1, 2, PACK)
+        round_down(nc.vector.tensor_copy, 1, 0, PACK // 2)
+        round_down(nc.scalar.copy, 1, PACK // 2, PACK)
         for t in range(PACK):
             quantize_down(1, t, t + 1)
-            for s in subs:
+            for s in range(SUBS):
                 h_pass(0, s, 1, t)
-        for s in subs:
+        for s in range(SUBS):
             round_h(0, s)
-        gather_codes(1, 2, 3, "down_bf1")
+        gather_codes(1, 2, CHUNKS, "down_bf1")
 
-        round_up(nc.vector.tensor_copy, 0, quarter, "up_bf0")
-        quantize_up(0, quarter)
+        round_up(nc.vector.tensor_copy, 0, HALF // 2, "up_bf0")
+        quantize_up(0, HALF // 2)
         quantize_h(0, "up_bf0")
-        round_up(nc.vector.tensor_copy, quarter, UP_COLS, "h_bf0")
-        quantize_up(quarter, UP_COLS)
+        round_up(nc.vector.tensor_copy, HALF // 2, HALF, "h_bf0")
+        quantize_up(HALF // 2, HALF)
         make_h(1)
         quantize_h(1, "h_bf0")
-        gather_ts(2, 3, "h_bf1")
+        gather_ts(2, CHUNKS, "h_bf1")
         make_h(2)
-        first = [finish(i, c, whole) for i, c in order[:2]]
+
+        def close_early(tiles):
+            scaled = []
+            for i, c in tiles:
+                up_pass(i, c)
+                scaled.append(scale(i, c, whole))
+            return scaled
+
+        early_scaled = close_early(order[: EARLY // 2])
         quantize_h(2, "h_codes2")
-        first = first + [finish(i, c, whole) for i, c in order[2:half]]
-        late_up = list(range(UP_COLS, M, P))
+        early_scaled = early_scaled + close_early(order[EARLY // 2 : EARLY])
+
+        late_up = {EARLY // 2 + piece: n0 for piece, n0 in enumerate(range(HALF, M, P))}
         for n, (i, c) in enumerate(order):
-            if n < half:
-                store(i, c, whole, first[n])
+            if n < EARLY:
+                store(i, c, whole, early_scaled[n])
             else:
                 for a in range(PASSES):
-                    w4_pass(i, c, whole, a)
-                cut = pieces(i, c)
-                store(i, c, cut[0], finish(i, c, whole, cut[0]))
-                for piece in cut[1:]:
-                    store(i, c, piece, scale(i, c, piece))
-            if 2 <= n < 2 + len(late_up):
-                n0 = late_up[n - 2]
+                    w4_pass(i, c, a)
+                up_pass(i, c)
+                width = CHUNK // 2 if n >= len(order) - 2 else CHUNK
+                for j0 in range(0, CHUNK, width):
+                    cols = slice(j0, j0 + width)
+                    store(i, c, cols, scale(i, c, cols))
+            if n in late_up:
+                n0 = late_up[n]
                 round_up(nc.scalar.copy, n0, n0 + P, "up_bf%d" % n0)
                 quantize_up(n0, n0 + P)

@@ -31,7 +31,7 @@ N_TILES = M // P
 BANKS = 8
 EARLY = BANKS - SUBS
 HALF = M // 2
-HEAD = T // 8
+HEAD = T // 4
 STAGE = 8
 ALIGN = 256
 WORD_LEAD = ALIGN // 2
@@ -52,7 +52,6 @@ def tile_list_tabts_bias_kernel(
             return padded[:, lead:].rearrange("p (a w) -> p a w", a=shape[0])
 
         offsets = keep.tile([P, S // GROUP], U16, name="offsets")
-        nc.sync.dma_start(offsets[:], offs)
         tab = [keep.tile([P, T], I32, name="tab%d" % a, align_bytes=ALIGN) for a in range(PASSES)]
 
         def load_tab(a, t0, t1):
@@ -60,8 +59,9 @@ def tile_list_tabts_bias_kernel(
             nc.sync.dma_start(tab[a][:, t0:t1], words[:, t0:t1])
 
         ts_row = keep.tile([P, T // P], F32, name="ts_row")
-        nc.sync.dma_start(ts_row[:], ts[0].rearrange("(q c) -> q c", q=P))
         load_tab(0, 0, HEAD)
+        nc.sync.dma_start(offsets[:], offs)
+        nc.sync.dma_start(ts_row[:], ts[0].rearrange("(q c) -> q c", q=P))
         tab_rows = keep.tile([P, T // 4], I32, name="tab_rows", align_bytes=ALIGN)
         nc.vector.memset(tab_rows[:], 0)
         nc.sync.dma_start(tab_rows[0:P:4, :], tab_scales.rearrange("a s t -> s a t").bitcast(I32))
@@ -88,13 +88,13 @@ def tile_list_tabts_bias_kernel(
             nc.vector.memset(v_plane[c][:], 0)
         nc.vector.memset(w4_plane[1][:], 0)
 
-        down_raw = []
+        down_raw = {}
 
-        def load_down(a):
-            raw = keep.tile([P, PACK, R], F32, name="down_raw%d" % a, align_bytes=ALIGN)
-            rows = down[a * P * PACK : (a + 1) * P * PACK, :]
+        def load_down(a, m0, m1):
+            raw = keep.tile([P, PACK, PACK * (m1 - m0)], F32, name="down_raw%d_%d" % (a, m0), align_bytes=ALIGN)
+            rows = down[a * P * PACK : (a + 1) * P * PACK, PACK * m0 : PACK * m1]
             nc.sync.dma_start(raw[:], rows.rearrange("(p j) r -> p j r", j=PACK))
-            down_raw.append(raw)
+            down_raw[a, m0] = raw
 
         def entries(c0, c1):
             return offsets[:, c0 * CHUNK // GROUP : c1 * CHUNK // GROUP]
@@ -115,15 +115,16 @@ def tile_list_tabts_bias_kernel(
         load_tab(0, HEAD, T)
         gather_scales(0, 1)
         gather_scales(1, CHUNKS)
+        load_down(0, 0, P)
         move_scales(0)
-        load_down(0)
         w4_early = [stationary([1, HALF // 2], I32, "w4_early%d" % a, WORD_LEAD // 4) for a in range(PASSES)]
         w4_late = stationary([PASSES, HALF // 2], I32, "w4_late", WORD_LEAD // 4)
         w4_pairs = w4_words.bitcast(I32).rearrange("a p w -> p a w")
         nc.sync.dma_start(w4_early[0][:, 0, :], w4_pairs[:, 0, : HALF // 2])
         load_tab(1, 0, T)
         nc.sync.dma_start(w4_early[1][:, 0, :], w4_pairs[:, 1, : HALF // 2])
-        load_down(1)
+        load_down(1, 0, P // 2)
+        load_down(1, P // 2, P)
         move_scales(1)
         up_raw = {}
 
@@ -192,10 +193,10 @@ def tile_list_tabts_bias_kernel(
         down_codes = stationary([PASSES, R], U32, "down_codes", WORD_LEAD // 4)
         down_scales = stationary([PASSES, R], U8, "down_scales", SCALE_LEAD)
 
-        def round_down(copy, a, t0, t1):
-            src = down_raw[a][:].rearrange("p j (m t) -> p m j t", t=PACK)
+        def round_down(copy, a, m0, m1, t0, t1):
+            src = down_raw[a, m0][:].rearrange("p j (m t) -> p m j t", t=PACK)
             dst = down_bf[a][:].rearrange("p t m j -> p m j t")
-            copy(dst[:, :, :, t0:t1], src[:, :, :, t0:t1])
+            copy(dst[:, m0:m1, :, t0:t1], src[:, :, :, t0:t1])
 
         def quantize_down(a, t0, t1):
             nc.vector.quantize_mx(
@@ -285,7 +286,7 @@ def tile_list_tabts_bias_kernel(
         gather_ts(0, 2, "tab0")
         for i, c in order[:EARLY]:
             w4_pass(i, c, 0)
-        round_down(nc.scalar.copy, 0, 0, PACK)
+        round_down(nc.scalar.copy, 0, 0, P, 0, PACK)
         quantize_down(0, 0, PACK)
         for s in range(SUBS):
             for t in range(PACK):
@@ -295,11 +296,16 @@ def tile_list_tabts_bias_kernel(
         for i, c in order[:EARLY]:
             w4_pass(i, c, 1)
 
-        round_down(nc.vector.tensor_copy, 1, 0, PACK // 2)
-        round_down(nc.scalar.copy, 1, PACK // 2, PACK)
+        round_down(nc.scalar.copy, 1, 0, P // 2, 0, PACK)
+        round_down(nc.vector.tensor_copy, 1, P // 2, P, 0, PACK // 2)
+        round_down(nc.scalar.copy, 1, P // 2, P, PACK // 2, PACK)
         for t in range(PACK):
             quantize_down(1, t, t + 1)
-            for s in range(SUBS):
+        for t in range(PACK):
+            for s in range(SUBS // 2):
+                h_pass(0, s, 1, t)
+        for s in range(SUBS // 2, SUBS):
+            for t in range(PACK):
                 h_pass(0, s, 1, t)
         for s in range(SUBS):
             round_h(0, s)

@@ -16,6 +16,7 @@ U8 = mybir.dt.uint8
 FP8X4 = mybir.dt.float8_e4m3fn_x4
 FP4X4 = mybir.dt.float4_e2m1fn_x4
 MULT = mybir.AluOpType.mult
+ADD = mybir.AluOpType.add
 IDENT = mybir.ActivationFunctionType.Identity
 
 P = 128
@@ -27,11 +28,15 @@ CHUNK = 512
 CHUNKS = S // CHUNK
 SUB = 128
 SUBS = CHUNK // SUB
-N_TILES = M // P
+ROWS = M // P
 BANKS = 8
-EARLY = BANKS - SUBS
+EARLY_ROWS = 2
+EARLY_CHUNKS = 2
+EARLY_COLS = EARLY_ROWS * P
 HALF = M // 2
 HEAD = T // 4
+SINGLE_ROWS = 4
+WIDE_STAGE = 2
 STAGE = 8
 ALIGN = 256
 WORD_LEAD = ALIGN // 2
@@ -44,6 +49,7 @@ def tile_list_tabts_bias_kernel(
     nc = tc.nc
     with ExitStack() as ctx:
         keep = ctx.enter_context(tc.tile_pool(name="keep", bufs=1))
+        wide = ctx.enter_context(tc.tile_pool(name="wide", bufs=WIDE_STAGE))
         stage = ctx.enter_context(tc.tile_pool(name="stage", bufs=STAGE))
         psum = ctx.enter_context(tc.psum_pool(name="psum", bufs=1))
 
@@ -67,25 +73,37 @@ def tile_list_tabts_bias_kernel(
         nc.sync.dma_start(tab_rows[0:P:4, :], tab_scales.rearrange("a s t -> s a t").bitcast(I32))
         identity = keep.tile([P, P], F32, name="identity")
         make_identity(nc, identity[:])
+        w4_cols = [(0, EARLY_COLS), (EARLY_COLS, M)]
         w4_plane = [
-            stationary([PASSES, HALF // 4], I32, "w4_plane%d" % g, SCALE_LEAD // 4) for g in range(M // HALF)
+            stationary([PASSES, (n1 - n0) // 4], I32, "w4_plane%d" % n0, SCALE_LEAD // 4) for n0, n1 in w4_cols
         ]
+        w4_codes = [
+            stationary([PASSES, (n1 - n0) // 2], I32, "w4_codes%d" % n0, WORD_LEAD // 4) for n0, n1 in w4_cols
+        ]
+        w4_pairs = w4_words.bitcast(I32).rearrange("a p w -> p a w")
 
         def load_w4_scales(queue, g):
-            cols = w4_scales[:, :, g * HALF : (g + 1) * HALF].bitcast(I32)
+            n0, n1 = w4_cols[g]
+            cols = w4_scales[:, :, n0:n1].bitcast(I32)
             for r in range(4):
                 queue.dma_start(w4_plane[g][r:P:QUADRANT, :, :], cols.rearrange("a (q r) n -> r q a n", r=4)[r])
+
+        def load_w4_words(g):
+            n0, n1 = w4_cols[g]
+            nc.sync.dma_start(w4_codes[g], w4_pairs[:, :, n0 // 2 : n1 // 2])
 
         nc.gpsimd.memset(w4_plane[0][:], 0)
         load_w4_scales(nc.gpsimd, 0)
         b_rows = keep.tile([P, P], F32, name="b_rows")
         nc.vector.memset(b_rows[:], 0.0)
-        nc.scalar.dma_start(b_rows[0:N_TILES, :], b.rearrange("(i p) -> i p", p=P))
+        nc.scalar.dma_start(b_rows[0:ROWS, :], b.rearrange("(i p) -> i p", p=P))
+        runs = [(0, EARLY_CHUNKS), (EARLY_CHUNKS, CHUNKS)]
         v_plane = [
-            keep.tile([P, PASSES, CHUNK // 4], I32, name="v_plane%d" % c, align_bytes=ALIGN) for c in range(CHUNKS)
+            keep.tile([P, PASSES, (c1 - c0) * CHUNK // 4], I32, name="v_plane%d" % c0, align_bytes=ALIGN)
+            for c0, c1 in runs
         ]
-        for c in range(CHUNKS):
-            nc.vector.memset(v_plane[c][:], 0)
+        for plane in v_plane:
+            nc.vector.memset(plane[:], 0)
         nc.vector.memset(w4_plane[1][:], 0)
 
         down_raw = {}
@@ -101,31 +119,16 @@ def tile_list_tabts_bias_kernel(
 
         picked = {}
 
-        def gather_scales(c0, c1):
-            rows = keep.tile([P, (c1 - c0) * CHUNK], U8, name="picked%d" % c0, align_bytes=ALIGN)
-            nc.vector.tensor_copy(rows[:], tab_rows[:].bitcast(U8).indirect(entries(c0, c1)))
-            for c in range(c0, c1):
-                picked[c] = rows[:, (c - c0) * CHUNK : (c - c0 + 1) * CHUNK]
+        def gather_scales(g):
+            c0, c1 = runs[g]
+            picked[g] = keep.tile([P, (c1 - c0) * CHUNK], U8, name="picked%d" % g, align_bytes=ALIGN)
+            nc.vector.tensor_copy(picked[g][:], tab_rows[:].bitcast(U8).indirect(entries(c0, c1)))
 
-        def move_scales(c):
+        def move_scales(g):
             for q in (0, 2, 1, 3):
                 p0 = QUADRANT * q
-                nc.sync.dma_start(v_plane[c][p0 : p0 + 4, :, :], picked[c][p0 : p0 + QUADRANT : 4, :].bitcast(I32))
+                nc.sync.dma_start(v_plane[g][p0 : p0 + 4, :, :], picked[g][p0 : p0 + QUADRANT : 4, :].bitcast(I32))
 
-        load_tab(0, HEAD, T)
-        gather_scales(0, 1)
-        gather_scales(1, CHUNKS)
-        load_down(0, 0, P)
-        move_scales(0)
-        w4_early = [stationary([1, HALF // 2], I32, "w4_early%d" % a, WORD_LEAD // 4) for a in range(PASSES)]
-        w4_late = stationary([PASSES, HALF // 2], I32, "w4_late", WORD_LEAD // 4)
-        w4_pairs = w4_words.bitcast(I32).rearrange("a p w -> p a w")
-        nc.sync.dma_start(w4_early[0][:, 0, :], w4_pairs[:, 0, : HALF // 2])
-        load_tab(1, 0, T)
-        nc.sync.dma_start(w4_early[1][:, 0, :], w4_pairs[:, 1, : HALF // 2])
-        load_down(1, 0, P // 2)
-        load_down(1, P // 2, P)
-        move_scales(1)
         up_raw = {}
 
         def load_up(g):
@@ -134,11 +137,20 @@ def tile_list_tabts_bias_kernel(
             nc.sync.dma_start(raw[:], cols.rearrange("(p t) n -> p t n", t=PACK))
             up_raw[g] = raw
 
+        load_tab(0, HEAD, T)
+        gather_scales(0)
+        gather_scales(1)
+        load_down(0, 0, P)
+        move_scales(0)
+        load_w4_words(0)
+        load_tab(1, 0, T)
+        load_down(1, 0, P // 2)
+        load_down(1, P // 2, P)
         load_up(0)
-        move_scales(2)
-        load_up(1)
-        nc.sync.dma_start(w4_late, w4_pairs[:, :, HALF // 2 :])
+        move_scales(1)
+        load_w4_words(1)
         load_w4_scales(nc.sync, 1)
+        load_up(1)
 
         ts_all = keep.tile([P, T], F32, name="ts_all", align_bytes=ALIGN)
         ts_view = ts_all[:].rearrange("p (q c) -> p q c", q=P)
@@ -148,15 +160,17 @@ def tile_list_tabts_bias_kernel(
                 column = ts_row[:, c0 + j : c0 + j + 1].to_broadcast([P, P])
                 nc.tensor.transpose(bank[:, j, :], column, identity[:])
             nc.scalar.copy(ts_view[:, :, c0 : c0 + 4], bank[:].rearrange("p j q -> p q j"))
-        bias = keep.tile([P, N_TILES], F32, name="bias")
+        bias = keep.tile([P, ROWS], F32, name="bias")
         bank = psum.tile([P, P], F32, name="bank0")
         nc.tensor.transpose(bank[:], b_rows[:], identity[:])
-        nc.scalar.copy(bias[:], bank[:, 0:N_TILES])
+        nc.scalar.copy(bias[:], bank[:, 0:ROWS])
 
         v_codes, ts_cols = {}, {}
 
         def v_scales(a, c):
-            return v_plane[c][:, a, :].bitcast(U8)
+            g = 0 if c < EARLY_CHUNKS else 1
+            j0 = (c - runs[g][0]) * CHUNK
+            return v_plane[g][:, a, :].bitcast(U8)[:, j0 : j0 + CHUNK]
 
         def gather_codes(a, c0, c1, tag):
             words = keep.tile([P, (c1 - c0) * CHUNK], U32, name="v_codes", tag=tag, align_bytes=ALIGN)
@@ -171,15 +185,21 @@ def tile_list_tabts_bias_kernel(
                 ts_cols[c] = cols[:, (c - c0) * CHUNK : (c - c0 + 1) * CHUNK]
 
         y_bank = {}
+        turn = (4, 5, 6, 7, 0, 1, 2, 3)
+
+        def bank_of(n):
+            return n if n < len(early) else turn[(n - len(early)) % BANKS]
+
+        early = [(i, c) for c in range(EARLY_CHUNKS) for i in range(EARLY_ROWS)]
 
         def w4_pass(i, c, a):
             if a == 0:
-                y_bank[i, c] = psum.tile([P, CHUNK], F32, name="bank%d" % (len(y_bank) % BANKS))
-            g, n = divmod(i * P, HALF)
-            words = (w4_early[a][:, 0, :] if g == 0 else w4_late[:, a, :]).bitcast(U8)
+                y_bank[i, c] = psum.tile([P, CHUNK], F32, name="bank%d" % bank_of(len(y_bank)))
+            g = 0 if i < EARLY_ROWS else 1
+            n = i * P - w4_cols[g][0]
             nc.tensor.matmul_mx(
                 out=y_bank[i, c][:],
-                lhsT=words[:, 2 * n : 2 * (n + P)].bitcast(FP4X4),
+                lhsT=w4_codes[g][:, a, :].bitcast(U8)[:, 2 * n : 2 * (n + P)].bitcast(FP4X4),
                 lhsT_scale=w4_plane[g][:, a, :].bitcast(U8)[:, n : n + P],
                 rhs=v_codes[a, c].bitcast(FP8X4),
                 rhs_scale=v_scales(a, c),
@@ -209,25 +229,29 @@ def tile_list_tabts_bias_kernel(
         up_codes = stationary([1, M], U32, "up_codes", WORD_LEAD // 4)[:, 0, :]
         up_scales = stationary([1, M], U8, "up_scales", SCALE_LEAD)[:, 0, :]
 
-        def round_up(copy, n0, n1, tag):
-            up_bf[n0] = keep.tile([P, n1 - n0, PACK], BF16, name="up_bf", tag=tag, align_bytes=ALIGN)
-            g, n = divmod(n0, HALF)
-            copy(up_bf[n0][:], up_raw[g][:, :, n : n + n1 - n0].rearrange("p t n -> p n t"))
+        def round_up(copy, i0, i1, tag):
+            up_bf[i0] = keep.tile([P, (i1 - i0) * P, PACK], BF16, name="up_bf", tag=tag, align_bytes=ALIGN)
+            g, n = divmod(i0 * P, HALF)
+            copy(up_bf[i0][:], up_raw[g][:, :, n : n + (i1 - i0) * P].rearrange("p t n -> p n t"))
 
-        def quantize_up(n0, n1):
+        def gpsimd_round(dst, src):
+            nc.gpsimd.tensor_scalar(dst, src, 1.0, 0.0, MULT, ADD)
+
+        def quantize_up(i0, i1):
             nc.vector.quantize_mx(
-                out=up_codes[:, n0:n1].bitcast(FP8X4),
-                scales=up_scales[:, n0:n1],
-                in_=up_bf[n0][:].rearrange("p n t -> p (n t)"),
+                out=up_codes[:, i0 * P : i1 * P].bitcast(FP8X4),
+                scales=up_scales[:, i0 * P : i1 * P],
+                in_=up_bf[i0][:].rearrange("p n t -> p (n t)"),
             )
 
         h_bf = [keep.tile([P, CHUNK, PACK], BF16, name="h_bf%d" % c, align_bytes=ALIGN) for c in range(CHUNKS)]
-        h_codes, h_bank = {}, {}
+        h_codes = keep.tile([P, S], U32, name="h_codes", align_bytes=ALIGN)
         h_scales = keep.tile([P, S], U8, name="h_scales", align_bytes=ALIGN)
+        h_bank = {}
 
         def h_pass(c, s, a, t):
             if (a, t) == (0, 0):
-                h_bank[c, s] = psum.tile([P, PACK, SUB], F32, name="bank%d" % (EARLY + s))
+                h_bank[c, s] = psum.tile([P, PACK, SUB], F32, name="bank%d" % (BANKS - SUBS + s))
             cols = slice(s * SUB, (s + 1) * SUB)
             nc.tensor.matmul_mx(
                 out=h_bank[c, s][:, t, :],
@@ -242,17 +266,16 @@ def tile_list_tabts_bias_kernel(
         def round_h(c, s):
             nc.scalar.copy(h_bf[c][:, s * SUB : (s + 1) * SUB, :], h_bank[c, s][:].rearrange("p t n -> p n t"))
 
-        def make_h(c):
-            for s in range(SUBS):
+        def make_h(c, s0, s1):
+            for s in range(s0, s1):
                 for a in range(PASSES):
                     for t in range(PACK):
                         h_pass(c, s, a, t)
                 round_h(c, s)
 
-        def quantize_h(c, tag):
-            h_codes[c] = keep.tile([P, CHUNK], U32, name="h_codes", tag=tag, align_bytes=ALIGN)
+        def quantize_h(c):
             nc.vector.quantize_mx(
-                out=h_codes[c][:].bitcast(FP8X4),
+                out=h_codes[:, c * CHUNK : (c + 1) * CHUNK].bitcast(FP8X4),
                 scales=h_scales[:, c * CHUNK : (c + 1) * CHUNK],
                 in_=h_bf[c][:].rearrange("p n t -> p (n t)"),
             )
@@ -263,37 +286,40 @@ def tile_list_tabts_bias_kernel(
                 out=y_bank[i, c][:],
                 lhsT=up_codes[:, rows].bitcast(FP8X4),
                 lhsT_scale=up_scales[:, rows],
-                rhs=h_codes[c][:].bitcast(FP8X4),
+                rhs=h_codes[:, c * CHUNK : (c + 1) * CHUNK].bitcast(FP8X4),
                 rhs_scale=h_scales[:, c * CHUNK : (c + 1) * CHUNK],
                 start=False,
                 stop=True,
             )
 
-        def scale(i, c, cols):
-            scaled = stage.tile([P, cols.stop - cols.start], F32, name="scaled", align_bytes=ALIGN)
-            nc.vector.tensor_tensor(scaled[:], y_bank[i, c][:, cols], ts_cols[c][:, cols], MULT)
-            return scaled
+        def staged(name, width):
+            pool = wide if width > CHUNK else stage
+            return pool.tile([P, width], F32, name=name, align_bytes=ALIGN)
 
-        def store(i, c, cols, scaled):
-            result = stage.tile([P, cols.stop - cols.start], F32, name="result", align_bytes=ALIGN)
+        def scale(i, j0, j1, scaled):
+            c, j = divmod(j0, CHUNK)
+            cols = slice(j, j + j1 - j0)
+            nc.vector.tensor_tensor(scaled, y_bank[i, c][:, cols], ts_cols[c][:, cols], MULT)
+
+        def store(i, j0, scaled):
+            width = scaled.shape[1]
+            result = staged("result", width)
             nc.scalar.activation(result[:], scaled[:], IDENT, bias=bias[:, i : i + 1])
-            nc.sync.dma_start(out[i * P : (i + 1) * P, c * CHUNK : (c + 1) * CHUNK][:, cols], result[:])
-
-        order = [(i, c) for i0 in (0, HALF // P) for c in range(CHUNKS) for i in range(i0, i0 + HALF // P)]
-        whole = slice(0, CHUNK)
+            nc.sync.dma_start(out[i * P : (i + 1) * P, j0 : j0 + width], result[:])
 
         gather_codes(0, 0, CHUNKS, "v_codes0")
-        gather_ts(0, 2, "tab0")
-        for i, c in order[:EARLY]:
-            w4_pass(i, c, 0)
+        gather_ts(0, 1, "tab0")
         round_down(nc.scalar.copy, 0, 0, P, 0, PACK)
         quantize_down(0, 0, PACK)
+        gather_ts(1, EARLY_CHUNKS, "down_bf0")
+        for i, c in early:
+            w4_pass(i, c, 0)
         for s in range(SUBS):
             for t in range(PACK):
                 h_pass(0, s, 0, t)
-        gather_codes(1, 0, 1, "v_codes10")
-        gather_codes(1, 1, 2, "v_codes11")
-        for i, c in order[:EARLY]:
+        for c in range(EARLY_CHUNKS):
+            gather_codes(1, c, c + 1, "v_codes1%d" % c)
+        for i, c in early:
             w4_pass(i, c, 1)
 
         round_down(nc.scalar.copy, 1, 0, P // 2, 0, PACK)
@@ -309,42 +335,62 @@ def tile_list_tabts_bias_kernel(
                 h_pass(0, s, 1, t)
         for s in range(SUBS):
             round_h(0, s)
-        gather_codes(1, 2, CHUNKS, "down_bf1")
+        gather_codes(1, EARLY_CHUNKS, CHUNKS, "down_bf1")
 
-        round_up(nc.vector.tensor_copy, 0, HALF // 2, "up_bf0")
-        quantize_up(0, HALF // 2)
-        quantize_h(0, "up_bf0")
-        round_up(nc.vector.tensor_copy, HALF // 2, HALF, "h_bf0")
-        quantize_up(HALF // 2, HALF)
-        make_h(1)
-        quantize_h(1, "h_bf0")
-        gather_ts(2, CHUNKS, "h_bf1")
-        make_h(2)
+        last = CHUNKS - 1
+        round_up(nc.vector.tensor_copy, 0, EARLY_ROWS, "up_bf0")
+        quantize_up(0, EARLY_ROWS)
+        quantize_h(0)
+        gather_ts(EARLY_CHUNKS, CHUNKS, "h_bf0")
+        make_h(1, 0, SUBS)
+        early_scaled = [staged("scaled", EARLY_CHUNKS * CHUNK) for i in range(EARLY_ROWS)]
 
-        def close_early(tiles):
-            scaled = []
-            for i, c in tiles:
+        def close_early(c):
+            for i in range(EARLY_ROWS):
                 up_pass(i, c)
-                scaled.append(scale(i, c, whole))
-            return scaled
+                scale(i, c * CHUNK, (c + 1) * CHUNK, early_scaled[i][:, c * CHUNK : (c + 1) * CHUNK])
 
-        early_scaled = close_early(order[: EARLY // 2])
-        quantize_h(2, "h_codes2")
-        early_scaled = early_scaled + close_early(order[EARLY // 2 : EARLY])
+        quantize_h(1)
+        make_h(last, 0, SUBS)
+        quantize_h(last)
+        close_early(0)
+        close_early(1)
+        for i in range(EARLY_ROWS):
+            for a in range(PASSES):
+                w4_pass(i, last, a)
 
-        late_up = {EARLY // 2 + piece: n0 for piece, n0 in enumerate(range(HALF, M, P))}
-        for n, (i, c) in enumerate(order):
-            if n < EARLY:
-                store(i, c, whole, early_scaled[n])
-            else:
-                for a in range(PASSES):
-                    w4_pass(i, c, a)
+        round_up(nc.scalar.copy, EARLY_ROWS, EARLY_ROWS + 1, "h_bf1")
+        quantize_up(EARLY_ROWS, EARLY_ROWS + 1)
+        for i in range(EARLY_ROWS):
+            store(i, 0, early_scaled[i])
+        for c in range(EARLY_CHUNKS):
+            for a in range(PASSES):
+                w4_pass(EARLY_ROWS, c, a)
+        for i in range(EARLY_ROWS):
+            up_pass(i, last)
+            scaled = staged("scaled", CHUNK)
+            scale(i, S - CHUNK, S, scaled[:])
+            store(i, S - CHUNK, scaled)
+
+        for i in range(EARLY_ROWS, ROWS):
+            whole = i < ROWS - SINGLE_ROWS
+            if i + 1 < ROWS:
+                round_up(gpsimd_round, i + 1, i + 2, "h_bf2")
+                quantize_up(i + 1, i + 2)
+            if whole:
+                scaled = staged("scaled", S)
+            for c in range(CHUNKS):
+                if (i, c) not in y_bank:
+                    for a in range(PASSES):
+                        w4_pass(i, c, a)
                 up_pass(i, c)
-                width = CHUNK // 2 if n >= len(order) - 2 else CHUNK
-                for j0 in range(0, CHUNK, width):
-                    cols = slice(j0, j0 + width)
-                    store(i, c, cols, scale(i, c, cols))
-            if n in late_up:
-                n0 = late_up[n]
-                round_up(nc.scalar.copy, n0, n0 + P, "up_bf%d" % n0)
-                quantize_up(n0, n0 + P)
+                if whole:
+                    scale(i, c * CHUNK, (c + 1) * CHUNK, scaled[:, c * CHUNK : (c + 1) * CHUNK])
+                else:
+                    width = CHUNK // 2 if i == ROWS - 1 and c >= CHUNKS - 2 else CHUNK
+                    for j0 in range(c * CHUNK, (c + 1) * CHUNK, width):
+                        scaled = staged("scaled", width)
+                        scale(i, j0, j0 + width, scaled[:])
+                        store(i, j0, scaled)
+            if whole:
+                store(i, 0, scaled)

@@ -35,7 +35,7 @@ EARLY_CHUNKS = 2
 EARLY_COLS = EARLY_ROWS * P
 HALF = M // 2
 HEAD = T // 4
-SINGLE_ROWS = 4
+SINGLE_ROWS = 5
 WIDE_STAGE = 2
 STAGE = 8
 ALIGN = 256
@@ -124,10 +124,12 @@ def tile_list_tabts_bias_kernel(
             picked[g] = keep.tile([P, (c1 - c0) * CHUNK], U8, name="picked%d" % g, align_bytes=ALIGN)
             nc.vector.tensor_copy(picked[g][:], tab_rows[:].bitcast(U8).indirect(entries(c0, c1)))
 
-        def move_scales(g):
+        def move_scales(g, a0, a1):
             for q in (0, 2, 1, 3):
                 p0 = QUADRANT * q
-                nc.sync.dma_start(v_plane[g][p0 : p0 + 4, :, :], picked[g][p0 : p0 + QUADRANT : 4, :].bitcast(I32))
+                step = 4 * PASSES // (a1 - a0)
+                rows = picked[g][p0 + 4 * a0 : p0 + QUADRANT : step, :].bitcast(I32)
+                nc.sync.dma_start(v_plane[g][p0 : p0 + 4, a0:a1, :], rows)
 
         up_raw = {}
 
@@ -141,13 +143,14 @@ def tile_list_tabts_bias_kernel(
         gather_scales(0)
         gather_scales(1)
         load_down(0, 0, P)
-        move_scales(0)
-        load_w4_words(0)
+        move_scales(0, 0, 1)
         load_tab(1, 0, T)
+        load_w4_words(0)
+        move_scales(0, 1, PASSES)
         load_down(1, 0, P // 2)
         load_down(1, P // 2, P)
         load_up(0)
-        move_scales(1)
+        move_scales(1, 0, PASSES)
         load_w4_words(1)
         load_w4_scales(nc.sync, 1)
         load_up(1)
@@ -192,20 +195,32 @@ def tile_list_tabts_bias_kernel(
 
         early = [(i, c) for c in range(EARLY_CHUNKS) for i in range(EARLY_ROWS)]
 
-        def w4_pass(i, c, a):
+        def span(c):
+            return c * CHUNK, (c + 1) * CHUNK
+
+        def in_chunk(j0, j1):
+            c, j = divmod(j0, CHUNK)
+            return c, slice(j, j + j1 - j0)
+
+        def w4_pass(i, j0, j1, a):
             if a == 0:
-                y_bank[i, c] = psum.tile([P, CHUNK], F32, name="bank%d" % bank_of(len(y_bank)))
+                y_bank[i, j0] = psum.tile([P, j1 - j0], F32, name="bank%d" % bank_of(len(y_bank)))
+            c, cols = in_chunk(j0, j1)
             g = 0 if i < EARLY_ROWS else 1
             n = i * P - w4_cols[g][0]
             nc.tensor.matmul_mx(
-                out=y_bank[i, c][:],
+                out=y_bank[i, j0][:],
                 lhsT=w4_codes[g][:, a, :].bitcast(U8)[:, 2 * n : 2 * (n + P)].bitcast(FP4X4),
                 lhsT_scale=w4_plane[g][:, a, :].bitcast(U8)[:, n : n + P],
-                rhs=v_codes[a, c].bitcast(FP8X4),
-                rhs_scale=v_scales(a, c),
+                rhs=v_codes[a, c][:, cols].bitcast(FP8X4),
+                rhs_scale=v_scales(a, c)[:, cols],
                 start=(a == 0),
                 stop=False,
             )
+
+        def w4_passes(i, j0, j1):
+            for a in range(PASSES):
+                w4_pass(i, j0, j1, a)
 
         down_bf = [
             keep.tile([P, PACK, P, PACK], BF16, name="down_bf%d" % a, align_bytes=ALIGN) for a in range(PASSES)
@@ -226,22 +241,31 @@ def tile_list_tabts_bias_kernel(
             )
 
         up_bf = {}
-        up_codes = stationary([1, M], U32, "up_codes", WORD_LEAD // 4)[:, 0, :]
-        up_scales = stationary([1, M], U8, "up_scales", SCALE_LEAD)[:, 0, :]
+        up_codes = stationary([1, HALF], U32, "up_codes", WORD_LEAD // 4)[:, 0, :]
+        up_scales = stationary([1, HALF], U8, "up_scales", SCALE_LEAD)[:, 0, :]
+
+        def up_cols(i0, i1):
+            while i1 * P > HALF:
+                i0, i1 = i0 - 2, i1 - 2
+            return slice(i0 * P, i1 * P)
 
         def round_up(copy, i0, i1, tag):
-            up_bf[i0] = keep.tile([P, (i1 - i0) * P, PACK], BF16, name="up_bf", tag=tag, align_bytes=ALIGN)
+            rounded = keep.tile([P, (i1 - i0) * P, PACK], BF16, name="up_bf", tag=tag, align_bytes=ALIGN)
+            round_up_into(copy, i0, i1, rounded[:])
+
+        def round_up_into(copy, i0, i1, rounded):
+            up_bf[i0] = rounded
             g, n = divmod(i0 * P, HALF)
-            copy(up_bf[i0][:], up_raw[g][:, :, n : n + (i1 - i0) * P].rearrange("p t n -> p n t"))
+            copy(rounded, up_raw[g][:, :, n : n + (i1 - i0) * P].rearrange("p t n -> p n t"))
 
         def gpsimd_round(dst, src):
             nc.gpsimd.tensor_scalar(dst, src, 1.0, 0.0, MULT, ADD)
 
         def quantize_up(i0, i1):
             nc.vector.quantize_mx(
-                out=up_codes[:, i0 * P : i1 * P].bitcast(FP8X4),
-                scales=up_scales[:, i0 * P : i1 * P],
-                in_=up_bf[i0][:].rearrange("p n t -> p (n t)"),
+                out=up_codes[:, up_cols(i0, i1)].bitcast(FP8X4),
+                scales=up_scales[:, up_cols(i0, i1)],
+                in_=up_bf[i0].rearrange("p n t -> p (n t)"),
             )
 
         h_bf = [keep.tile([P, CHUNK, PACK], BF16, name="h_bf%d" % c, align_bytes=ALIGN) for c in range(CHUNKS)]
@@ -280,14 +304,14 @@ def tile_list_tabts_bias_kernel(
                 in_=h_bf[c][:].rearrange("p n t -> p (n t)"),
             )
 
-        def up_pass(i, c):
-            rows = slice(i * P, (i + 1) * P)
+        def up_pass(i, j0, j1):
+            rows = up_cols(i, i + 1)
             nc.tensor.matmul_mx(
-                out=y_bank[i, c][:],
+                out=y_bank[i, j0][:],
                 lhsT=up_codes[:, rows].bitcast(FP8X4),
                 lhsT_scale=up_scales[:, rows],
-                rhs=h_codes[:, c * CHUNK : (c + 1) * CHUNK].bitcast(FP8X4),
-                rhs_scale=h_scales[:, c * CHUNK : (c + 1) * CHUNK],
+                rhs=h_codes[:, j0:j1].bitcast(FP8X4),
+                rhs_scale=h_scales[:, j0:j1],
                 start=False,
                 stop=True,
             )
@@ -297,9 +321,8 @@ def tile_list_tabts_bias_kernel(
             return pool.tile([P, width], F32, name=name, align_bytes=ALIGN)
 
         def scale(i, j0, j1, scaled):
-            c, j = divmod(j0, CHUNK)
-            cols = slice(j, j + j1 - j0)
-            nc.vector.tensor_tensor(scaled, y_bank[i, c][:, cols], ts_cols[c][:, cols], MULT)
+            c, cols = in_chunk(j0, j1)
+            nc.vector.tensor_tensor(scaled, y_bank[i, j0][:], ts_cols[c][:, cols], MULT)
 
         def store(i, j0, scaled):
             width = scaled.shape[1]
@@ -308,19 +331,18 @@ def tile_list_tabts_bias_kernel(
             nc.sync.dma_start(out[i * P : (i + 1) * P, j0 : j0 + width], result[:])
 
         gather_codes(0, 0, CHUNKS, "v_codes0")
-        gather_ts(0, 1, "tab0")
         round_down(nc.scalar.copy, 0, 0, P, 0, PACK)
         quantize_down(0, 0, PACK)
-        gather_ts(1, EARLY_CHUNKS, "down_bf0")
+        gather_ts(0, 1, "down_bf0")
         for i, c in early:
-            w4_pass(i, c, 0)
+            w4_pass(i, *span(c), 0)
         for s in range(SUBS):
             for t in range(PACK):
                 h_pass(0, s, 0, t)
         for c in range(EARLY_CHUNKS):
             gather_codes(1, c, c + 1, "v_codes1%d" % c)
         for i, c in early:
-            w4_pass(i, c, 1)
+            w4_pass(i, *span(c), 1)
 
         round_down(nc.scalar.copy, 1, 0, P // 2, 0, PACK)
         round_down(nc.vector.tensor_copy, 1, P // 2, P, 0, PACK // 2)
@@ -341,54 +363,57 @@ def tile_list_tabts_bias_kernel(
         round_up(nc.vector.tensor_copy, 0, EARLY_ROWS, "up_bf0")
         quantize_up(0, EARLY_ROWS)
         quantize_h(0)
-        gather_ts(EARLY_CHUNKS, CHUNKS, "h_bf0")
+        gather_ts(1, EARLY_CHUNKS, "h_bf0")
         make_h(1, 0, SUBS)
-        early_scaled = [staged("scaled", EARLY_CHUNKS * CHUNK) for i in range(EARLY_ROWS)]
+        early_scaled = {}
 
-        def close_early(c):
+        def close_early(c, tag):
+            both = keep.tile([P, EARLY_ROWS, CHUNK], F32, name="early_scaled", tag=tag, align_bytes=ALIGN)
             for i in range(EARLY_ROWS):
-                up_pass(i, c)
-                scale(i, c * CHUNK, (c + 1) * CHUNK, early_scaled[i][:, c * CHUNK : (c + 1) * CHUNK])
+                up_pass(i, *span(c))
+                scale(i, *span(c), both[:, i, :])
+                early_scaled[i, c] = both[:, i, :]
 
         quantize_h(1)
+        spent = keep.tile([P, 2, CHUNK], F32, name="spent", tag="h_bf1", align_bytes=ALIGN)
+        ts_cols[last] = spent[:, 0, :]
+        nc.vector.tensor_copy(ts_cols[last], ts_all[:].indirect(entries(last, CHUNKS)))
         make_h(last, 0, SUBS)
         quantize_h(last)
-        close_early(0)
-        close_early(1)
+        close_early(0, "early_scaled")
+        rounded = spent[:, 1, :].bitcast(BF16).rearrange("p (n t) -> p n t", t=PACK)
+        round_up_into(nc.scalar.copy, EARLY_ROWS, 2 * EARLY_ROWS, rounded)
+        quantize_up(EARLY_ROWS, 2 * EARLY_ROWS)
+        close_early(1, "h_bf2")
         for i in range(EARLY_ROWS):
-            for a in range(PASSES):
-                w4_pass(i, last, a)
+            w4_passes(i, *span(last))
 
-        round_up(nc.scalar.copy, EARLY_ROWS, EARLY_ROWS + 1, "h_bf1")
-        quantize_up(EARLY_ROWS, EARLY_ROWS + 1)
-        for i in range(EARLY_ROWS):
-            store(i, 0, early_scaled[i])
+        for i, c in early:
+            store(i, c * CHUNK, early_scaled[i, c])
         for c in range(EARLY_CHUNKS):
-            for a in range(PASSES):
-                w4_pass(EARLY_ROWS, c, a)
+            w4_passes(EARLY_ROWS, *span(c))
         for i in range(EARLY_ROWS):
-            up_pass(i, last)
+            up_pass(i, *span(last))
             scaled = staged("scaled", CHUNK)
-            scale(i, S - CHUNK, S, scaled[:])
+            scale(i, *span(last), scaled[:])
             store(i, S - CHUNK, scaled)
 
         for i in range(EARLY_ROWS, ROWS):
             whole = i < ROWS - SINGLE_ROWS
-            if i + 1 < ROWS:
-                round_up(gpsimd_round, i + 1, i + 2, "h_bf2")
+            if EARLY_ROWS < i < ROWS - 1:
+                round_up_into(gpsimd_round, i + 1, i + 2, rounded[:, 0:P, :])
                 quantize_up(i + 1, i + 2)
             if whole:
                 scaled = staged("scaled", S)
             for c in range(CHUNKS):
-                if (i, c) not in y_bank:
-                    for a in range(PASSES):
-                        w4_pass(i, c, a)
-                up_pass(i, c)
-                if whole:
-                    scale(i, c * CHUNK, (c + 1) * CHUNK, scaled[:, c * CHUNK : (c + 1) * CHUNK])
-                else:
-                    width = CHUNK // 2 if i == ROWS - 1 and c >= CHUNKS - 2 else CHUNK
-                    for j0 in range(c * CHUNK, (c + 1) * CHUNK, width):
+                width = CHUNK // 2 if i == ROWS - 1 and c >= CHUNKS - 2 else CHUNK
+                for j0 in range(*span(c), width):
+                    if (i, j0) not in y_bank:
+                        w4_passes(i, j0, j0 + width)
+                    up_pass(i, j0, j0 + width)
+                    if whole:
+                        scale(i, j0, j0 + width, scaled[:, j0 : j0 + width])
+                    else:
                         scaled = staged("scaled", width)
                         scale(i, j0, j0 + width, scaled[:])
                         store(i, j0, scaled)

@@ -35,7 +35,6 @@ EARLY_CHUNKS = 2
 EARLY_COLS = EARLY_ROWS * P
 HALF = M // 2
 HEAD = T // 4
-SINGLE_ROWS = 5
 WIDE_STAGE = 2
 STAGE = 8
 ALIGN = 256
@@ -241,13 +240,12 @@ def tile_list_tabts_bias_kernel(
             )
 
         up_bf = {}
-        up_codes = stationary([1, HALF], U32, "up_codes", WORD_LEAD // 4)[:, 0, :]
-        up_scales = stationary([1, HALF], U8, "up_scales", SCALE_LEAD)[:, 0, :]
+        up_codes = stationary([1, M], U32, "up_codes", WORD_LEAD // 4)[:, 0, :]
+        up_scales = stationary([1, M], U8, "up_scales", SCALE_LEAD)[:, 0, :]
 
         def up_cols(i0, i1):
-            while i1 * P > HALF:
-                i0, i1 = i0 - 2, i1 - 2
-            return slice(i0 * P, i1 * P)
+            place = (5, 6, 0, 7, 0, 1, 2, 3)
+            return slice(place[i0] * P, (place[i0] + i1 - i0) * P)
 
         def round_up(copy, i0, i1, tag):
             rounded = keep.tile([P, (i1 - i0) * P, PACK], BF16, name="up_bf", tag=tag, align_bytes=ALIGN)
@@ -261,11 +259,11 @@ def tile_list_tabts_bias_kernel(
         def gpsimd_round(dst, src):
             nc.gpsimd.tensor_scalar(dst, src, 1.0, 0.0, MULT, ADD)
 
-        def quantize_up(i0, i1):
+        def quantize_up(i0, i1, part=None):
             nc.vector.quantize_mx(
                 out=up_codes[:, up_cols(i0, i1)].bitcast(FP8X4),
                 scales=up_scales[:, up_cols(i0, i1)],
-                in_=up_bf[i0].rearrange("p n t -> p (n t)"),
+                in_=(up_bf[i0] if part is None else part).rearrange("p n t -> p (n t)"),
             )
 
         h_bf = [keep.tile([P, CHUNK, PACK], BF16, name="h_bf%d" % c, align_bytes=ALIGN) for c in range(CHUNKS)]
@@ -375,7 +373,7 @@ def tile_list_tabts_bias_kernel(
                 early_scaled[i, c] = both[:, i, :]
 
         quantize_h(1)
-        spent = keep.tile([P, 2, CHUNK], F32, name="spent", tag="h_bf1", align_bytes=ALIGN)
+        spent = keep.tile([P, 3, CHUNK], F32, name="spent", tag="h_bf1", align_bytes=ALIGN)
         ts_cols[last] = spent[:, 0, :]
         nc.vector.tensor_copy(ts_cols[last], ts_all[:].indirect(entries(last, CHUNKS)))
         make_h(last, 0, SUBS)
@@ -383,7 +381,8 @@ def tile_list_tabts_bias_kernel(
         close_early(0, "early_scaled")
         rounded = spent[:, 1, :].bitcast(BF16).rearrange("p (n t) -> p n t", t=PACK)
         round_up_into(nc.scalar.copy, EARLY_ROWS, 2 * EARLY_ROWS, rounded)
-        quantize_up(EARLY_ROWS, 2 * EARLY_ROWS)
+        for i in (2, 3):
+            quantize_up(i, i + 1, rounded[:, (i - 2) * P : (i - 1) * P, :])
         close_early(1, "h_bf2")
         for i in range(EARLY_ROWS):
             w4_passes(i, *span(last))
@@ -398,24 +397,42 @@ def tile_list_tabts_bias_kernel(
             scale(i, *span(last), scaled[:])
             store(i, S - CHUNK, scaled)
 
-        for i in range(EARLY_ROWS, ROWS):
-            whole = i < ROWS - SINGLE_ROWS
-            if EARLY_ROWS < i < ROWS - 1:
-                round_up_into(gpsimd_round, i + 1, i + 2, rounded[:, 0:P, :])
-                quantize_up(i + 1, i + 2)
-            if whole:
-                scaled = staged("scaled", S)
+        def open_and_close(i, j0, j1):
+            if (i, j0) not in y_bank:
+                w4_passes(i, j0, j1)
+            up_pass(i, j0, j1)
+
+        def leave(i, j0, j1, width):
+            scaled = staged("scaled", j1 - j0)
+            for j in range(j0, j1, width):
+                open_and_close(i, j, j + width)
+                scale(i, j, j + width, scaled[:, j - j0 : j - j0 + width])
+            store(i, j0, scaled)
+
+        def leave_by_gpsimd(i, c):
+            open_and_close(i, *span(c))
+            sums = keep.tile([P, CHUNK], F32, name="sums%d" % i, align_bytes=ALIGN)
+            nc.scalar.copy(sums[:], y_bank[i, c * CHUNK][:])
+            nc.gpsimd.tensor_tensor(spent[:, 1, :], sums[:], ts_cols[c], MULT)
+            result = keep.tile([P, CHUNK], F32, name="result%d" % i, align_bytes=ALIGN)
+            nc.gpsimd.tensor_scalar(result[:], spent[:, 1, :], 1.0, bias[:, i : i + 1], MULT, ADD)
+            nc.gpsimd.dma_start(out[i * P : (i + 1) * P, slice(*span(c))], result[:])
+
+        leave(2, 0, last * CHUNK, CHUNK)
+        row2 = staged("scaled", CHUNK)
+        open_and_close(2, *span(last))
+        scale(2, *span(last), row2[:])
+        round_up_into(gpsimd_round, ROWS // 2, ROWS, spent[:, 1:3, :].rearrange("p a w -> p (a w)").bitcast(BF16).rearrange("p (n t) -> p n t", t=PACK))
+        quantize_up(ROWS // 2, ROWS)
+        leave_by_gpsimd(3, 0)
+        store(2, last * CHUNK, row2)
+        leave(3, CHUNK, S, CHUNK)
+        leave_by_gpsimd(4, 0)
+        for c in range(1, CHUNKS):
+            leave(4, *span(c), CHUNK)
+        for i in (5, 6):
             for c in range(CHUNKS):
-                width = CHUNK // 2 if i == ROWS - 1 and c >= CHUNKS - 2 else CHUNK
-                for j0 in range(*span(c), width):
-                    if (i, j0) not in y_bank:
-                        w4_passes(i, j0, j0 + width)
-                    up_pass(i, j0, j0 + width)
-                    if whole:
-                        scale(i, j0, j0 + width, scaled[:, j0 : j0 + width])
-                    else:
-                        scaled = staged("scaled", width)
-                        scale(i, j0, j0 + width, scaled[:])
-                        store(i, j0, scaled)
-            if whole:
-                store(i, 0, scaled)
+                leave(i, *span(c), CHUNK)
+        leave(7, *span(0), CHUNK)
+        for j0 in range(CHUNK, S, CHUNK // 2):
+            leave(7, j0, j0 + CHUNK // 2, CHUNK // 2)

@@ -142,8 +142,9 @@ def tile_list_tabts_bias_kernel(
         gather_scales(0)
         gather_scales(1)
         load_down(0, 0, P)
+        load_tab(1, 0, HEAD)
         move_scales(0, 0, 1)
-        load_tab(1, 0, T)
+        load_tab(1, HEAD, T)
         load_w4_words(0)
         move_scales(0, 1, PASSES)
         load_down(1, 0, P // 2)

import math
from contextlib import ExitStack

import concourse.mybir as mybir
from concourse.masks import make_identity

K, M, T, S, R = 1024, 1024, 4096, 1536, 512
FLOPS = 2 * S * (K * M + K * R + R * M)

F32 = mybir.dt.float32
BF16 = mybir.dt.bfloat16
I32 = mybir.dt.int32
U32 = mybir.dt.uint32
U16 = mybir.dt.uint16
U8 = mybir.dt.uint8
FP8X4 = mybir.dt.float8_e4m3fn_x4
FP4X4 = mybir.dt.float4_e2m1fn_x4
MULT = mybir.AluOpType.mult
ADD = mybir.AluOpType.add
IDENT = mybir.ActivationFunctionType.Identity

P = 128
PACK = 4
PASSES = K // (P * PACK)
GROUP = 16
QUADRANT = 32
CHUNK = 512
CHUNKS = S // CHUNK
SUB = 128
SUBS = CHUNK // SUB
ROWS = M // P
BANKS = 8
EARLY_ROWS = 2
EARLY_CHUNKS = 2
EARLY_COLS = EARLY_ROWS * P
HALF = M // 2
HEAD = T // 4
WIDE_STAGE = 2
STAGE = 8
ALIGN = 256
WORD_LEAD = ALIGN // 2
SCALE_LEAD = ALIGN // 4


def tile_list_tabts_bias_kernel(
    tc, tab_words, tab_scales, w4_words, w4_scales, down, up, ts, b, offs, out
):
    nc = tc.nc
    with ExitStack() as ctx:
        keep = ctx.enter_context(tc.tile_pool(name="keep", bufs=1))
        wide = ctx.enter_context(tc.tile_pool(name="wide", bufs=WIDE_STAGE))
        stage = ctx.enter_context(tc.tile_pool(name="stage", bufs=STAGE))
        psum = ctx.enter_context(tc.psum_pool(name="psum", bufs=1))

        def stationary(shape, dtype, name, lead):
            padded = keep.tile([P, lead + math.prod(shape)], dtype, name=name, align_bytes=ALIGN)
            return padded[:, lead:].rearrange("p (a w) -> p a w", a=shape[0])

        offsets = keep.tile([P, S // GROUP], U16, name="offsets")
        tab = [keep.tile([P, T], I32, name="tab%d" % a, align_bytes=ALIGN) for a in range(PASSES)]

        def load_tab(a, t0, t1):
            words = tab_words[a].rearrange("p t i -> p (t i)").bitcast(I32)
            nc.sync.dma_start(tab[a][:, t0:t1], words[:, t0:t1])

        ts_row = keep.tile([P, T // P], F32, name="ts_row")
        load_tab(0, 0, HEAD)
        nc.sync.dma_start(offsets[:], offs)
        nc.sync.dma_start(ts_row[:], ts[0].rearrange("(q c) -> q c", q=P))
        tab_rows = keep.tile([P, T // 4], I32, name="tab_rows", align_bytes=ALIGN)
        nc.vector.memset(tab_rows[:], 0)
        nc.sync.dma_start(tab_rows[0:P:4, :], tab_scales.rearrange("a s t -> s a t").bitcast(I32))
        identity = keep.tile([P, P], F32, name="identity")
        make_identity(nc, identity[:])
        w4_cols = [(0, EARLY_COLS), (EARLY_COLS, M)]
        w4_plane = [
            stationary([PASSES, (n1 - n0) // 4], I32, "w4_plane%d" % n0, SCALE_LEAD // 4) for n0, n1 in w4_cols
        ]
        w4_codes = [
            stationary([PASSES, (n1 - n0) // 2], I32, "w4_codes%d" % n0, WORD_LEAD // 4) for n0, n1 in w4_cols
        ]
        w4_pairs = w4_words.bitcast(I32).rearrange("a p w -> p a w")

        def load_w4_scales(queue, g):
            n0, n1 = w4_cols[g]
            cols = w4_scales[:, :, n0:n1].bitcast(I32)
            for r in range(4):
                queue.dma_start(w4_plane[g][r:P:QUADRANT, :, :], cols.rearrange("a (q r) n -> r q a n", r=4)[r])

        def load_w4_words(g):
            n0, n1 = w4_cols[g]
            nc.sync.dma_start(w4_codes[g], w4_pairs[:, :, n0 // 2 : n1 // 2])

        nc.gpsimd.memset(w4_plane[0][:], 0)
        load_w4_scales(nc.gpsimd, 0)
        b_rows = keep.tile([P, P], F32, name="b_rows")
        nc.vector.memset(b_rows[:], 0.0)
        nc.scalar.dma_start(b_rows[0:ROWS, :], b.rearrange("(i p) -> i p", p=P))
        runs = [(0, EARLY_CHUNKS), (EARLY_CHUNKS, CHUNKS)]
        v_plane = [
            keep.tile([P, PASSES, (c1 - c0) * CHUNK // 4], I32, name="v_plane%d" % c0, align_bytes=ALIGN)
            for c0, c1 in runs
        ]
        for plane in v_plane:
            nc.vector.memset(plane[:], 0)
        nc.vector.memset(w4_plane[1][:], 0)

        down_raw = {}

        def load_down(a, m0, m1):
            raw = keep.tile([P, PACK, PACK * (m1 - m0)], F32, name="down_raw%d_%d" % (a, m0), align_bytes=ALIGN)
            rows = down[a * P * PACK : (a + 1) * P * PACK, PACK * m0 : PACK * m1]
            nc.sync.dma_start(raw[:], rows.rearrange("(p j) r -> p j r", j=PACK))
            down_raw[a, m0] = raw

        def entries(c0, c1):
            return offsets[:, c0 * CHUNK // GROUP : c1 * CHUNK // GROUP]

        picked = {}

        def gather_scales(g):
            c0, c1 = runs[g]
            picked[g] = keep.tile([P, (c1 - c0) * CHUNK], U8, name="picked%d" % g, align_bytes=ALIGN)
            nc.vector.tensor_copy(picked[g][:], tab_rows[:].bitcast(U8).indirect(entries(c0, c1)))

        def move_scales(g, a0, a1):
            for q in (0, 2, 1, 3):
                p0 = QUADRANT * q
                step = 4 * PASSES // (a1 - a0)
                rows = picked[g][p0 + 4 * a0 : p0 + QUADRANT : step, :].bitcast(I32)
                nc.sync.dma_start(v_plane[g][p0 : p0 + 4, a0:a1, :], rows)

        up_raw = {}

        def load_up(g):
            raw = keep.tile([P, PACK, HALF], F32, name="up_raw%d" % g, align_bytes=ALIGN)
            cols = up[:, g * HALF : (g + 1) * HALF]
            nc.sync.dma_start(raw[:], cols.rearrange("(p t) n -> p t n", t=PACK))
            up_raw[g] = raw

        load_tab(0, HEAD, T)
        gather_scales(0)
        gather_scales(1)
        load_down(0, 0, P)
        load_tab(1, 0, HEAD)
        move_scales(0, 0, 1)
        load_tab(1, HEAD, T)
        load_w4_words(0)
        move_scales(0, 1, PASSES)
        load_down(1, 0, P // 2)
        load_down(1, P // 2, P)
        load_up(0)
        move_scales(1, 0, PASSES)
        load_w4_words(1)
        load_w4_scales(nc.sync, 1)
        load_up(1)

        ts_all = keep.tile([P, T], F32, name="ts_all", align_bytes=ALIGN)
        ts_view = ts_all[:].rearrange("p (q c) -> p q c", q=P)
        for c0 in range(0, T // P, 4):
            bank = psum.tile([P, 4, P], F32, name="bank%d" % (c0 // 4))
            for j in range(4):
                column = ts_row[:, c0 + j : c0 + j + 1].to_broadcast([P, P])
                nc.tensor.transpose(bank[:, j, :], column, identity[:])
            nc.scalar.copy(ts_view[:, :, c0 : c0 + 4], bank[:].rearrange("p j q -> p q j"))
        bias = keep.tile([P, ROWS], F32, name="bias")
        bank = psum.tile([P, P], F32, name="bank0")
        nc.tensor.transpose(bank[:], b_rows[:], identity[:])
        nc.scalar.copy(bias[:], bank[:, 0:ROWS])

        v_codes, ts_cols = {}, {}

        def v_scales(a, c):
            g = 0 if c < EARLY_CHUNKS else 1
            j0 = (c - runs[g][0]) * CHUNK
            return v_plane[g][:, a, :].bitcast(U8)[:, j0 : j0 + CHUNK]

        def gather_codes(a, c0, c1, tag):
            words = keep.tile([P, (c1 - c0) * CHUNK], U32, name="v_codes", tag=tag, align_bytes=ALIGN)
            nc.vector.tensor_copy(words[:], tab[a][:].bitcast(U32).indirect(entries(c0, c1)))
            for c in range(c0, c1):
                v_codes[a, c] = words[:, (c - c0) * CHUNK : (c - c0 + 1) * CHUNK]

        def gather_ts(c0, c1, tag):
            cols = keep.tile([P, (c1 - c0) * CHUNK], F32, name="ts_cols", tag=tag, align_bytes=ALIGN)
            nc.vector.tensor_copy(cols[:], ts_all[:].indirect(entries(c0, c1)))
            for c in range(c0, c1):
                ts_cols[c] = cols[:, (c - c0) * CHUNK : (c - c0 + 1) * CHUNK]

        y_bank = {}
        turn = (4, 5, 6, 7, 0, 1, 2, 3)

        def bank_of(n):
            return n if n < len(early) else turn[(n - len(early)) % BANKS]

        early = [(i, c) for c in range(EARLY_CHUNKS) for i in range(EARLY_ROWS)]

        def span(c):
            return c * CHUNK, (c + 1) * CHUNK

        def in_chunk(j0, j1):
            c, j = divmod(j0, CHUNK)
            return c, slice(j, j + j1 - j0)

        def w4_pass(i, j0, j1, a):
            if a == 0:
                y_bank[i, j0] = psum.tile([P, j1 - j0], F32, name="bank%d" % bank_of(len(y_bank)))
            c, cols = in_chunk(j0, j1)
            g = 0 if i < EARLY_ROWS else 1
            n = i * P - w4_cols[g][0]
            nc.tensor.matmul_mx(
                out=y_bank[i, j0][:],
                lhsT=w4_codes[g][:, a, :].bitcast(U8)[:, 2 * n : 2 * (n + P)].bitcast(FP4X4),
                lhsT_scale=w4_plane[g][:, a, :].bitcast(U8)[:, n : n + P],
                rhs=v_codes[a, c][:, cols].bitcast(FP8X4),
                rhs_scale=v_scales(a, c)[:, cols],
                start=(a == 0),
                stop=False,
            )

        def w4_passes(i, j0, j1):
            for a in range(PASSES):
                w4_pass(i, j0, j1, a)

        down_bf = [
            keep.tile([P, PACK, P, PACK], BF16, name="down_bf%d" % a, align_bytes=ALIGN) for a in range(PASSES)
        ]
        down_codes = stationary([PASSES, R], U32, "down_codes", WORD_LEAD // 4)
        down_scales = stationary([PASSES, R], U8, "down_scales", SCALE_LEAD)

        def round_down(copy, a, m0, m1, t0, t1):
            src = down_raw[a, m0][:].rearrange("p j (m t) -> p m j t", t=PACK)
            dst = down_bf[a][:].rearrange("p t m j -> p m j t")
            copy(dst[:, m0:m1, :, t0:t1], src[:, :, :, t0:t1])

        def quantize_down(a, t0, t1):
            nc.vector.quantize_mx(
                out=down_codes[:, a, t0 * P : t1 * P].bitcast(FP8X4),
                scales=down_scales[:, a, t0 * P : t1 * P],
                in_=down_bf[a][:, t0:t1].rearrange("p t m j -> p (t m j)"),
            )

        up_bf = {}
        up_codes = stationary([1, M], U32, "up_codes", WORD_LEAD // 4)[:, 0, :]
        up_scales = stationary([1, M], U8, "up_scales", SCALE_LEAD)[:, 0, :]

        def up_cols(i0, i1):
            place = (5, 6, 0, 7, 0, 1, 2, 3)
            return slice(place[i0] * P, (place[i0] + i1 - i0) * P)

        def round_up(copy, i0, i1, tag):
            rounded = keep.tile([P, (i1 - i0) * P, PACK], BF16, name="up_bf", tag=tag, align_bytes=ALIGN)
            round_up_into(copy, i0, i1, rounded[:])

        def round_up_into(copy, i0, i1, rounded):
            up_bf[i0] = rounded
            g, n = divmod(i0 * P, HALF)
            copy(rounded, up_raw[g][:, :, n : n + (i1 - i0) * P].rearrange("p t n -> p n t"))

        def gpsimd_round(dst, src):
            nc.gpsimd.tensor_scalar(dst, src, 1.0, 0.0, MULT, ADD)

        def quantize_up(i0, i1, part=None):
            nc.vector.quantize_mx(
                out=up_codes[:, up_cols(i0, i1)].bitcast(FP8X4),
                scales=up_scales[:, up_cols(i0, i1)],
                in_=(up_bf[i0] if part is None else part).rearrange("p n t -> p (n t)"),
            )

        h_bf = [keep.tile([P, CHUNK, PACK], BF16, name="h_bf%d" % c, align_bytes=ALIGN) for c in range(CHUNKS)]
        h_codes = keep.tile([P, S], U32, name="h_codes", align_bytes=ALIGN)
        h_scales = keep.tile([P, S], U8, name="h_scales", align_bytes=ALIGN)
        h_bank = {}

        def h_pass(c, s, a, t):
            if (a, t) == (0, 0):
                h_bank[c, s] = psum.tile([P, PACK, SUB], F32, name="bank%d" % (BANKS - SUBS + s))
            cols = slice(s * SUB, (s + 1) * SUB)
            nc.tensor.matmul_mx(
                out=h_bank[c, s][:, t, :],
                lhsT=down_codes[:, a, t * P : (t + 1) * P].bitcast(FP8X4),
                lhsT_scale=down_scales[:, a, t * P : (t + 1) * P],
                rhs=v_codes[a, c][:, cols].bitcast(FP8X4),
                rhs_scale=v_scales(a, c)[:, cols],
                start=(a, t) == (0, 0),
                stop=(a, t) == (PASSES - 1, PACK - 1),
            )

        def round_h(c, s):
            nc.scalar.copy(h_bf[c][:, s * SUB : (s + 1) * SUB, :], h_bank[c, s][:].rearrange("p t n -> p n t"))

        def make_h(c, s0, s1):
            for s in range(s0, s1):
                for a in range(PASSES):
                    for t in range(PACK):
                        h_pass(c, s, a, t)
                round_h(c, s)

        def quantize_h(c):
            nc.vector.quantize_mx(
                out=h_codes[:, c * CHUNK : (c + 1) * CHUNK].bitcast(FP8X4),
                scales=h_scales[:, c * CHUNK : (c + 1) * CHUNK],
                in_=h_bf[c][:].rearrange("p n t -> p (n t)"),
            )

        def up_pass(i, j0, j1):
            rows = up_cols(i, i + 1)
            nc.tensor.matmul_mx(
                out=y_bank[i, j0][:],
                lhsT=up_codes[:, rows].bitcast(FP8X4),
                lhsT_scale=up_scales[:, rows],
                rhs=h_codes[:, j0:j1].bitcast(FP8X4),
                rhs_scale=h_scales[:, j0:j1],
                start=False,
                stop=True,
            )

        def staged(name, width):
            pool = wide if width > CHUNK else stage
            return pool.tile([P, width], F32, name=name, align_bytes=ALIGN)

        def scale(i, j0, j1, scaled):
            c, cols = in_chunk(j0, j1)
            nc.vector.tensor_tensor(scaled, y_bank[i, j0][:], ts_cols[c][:, cols], MULT)

        def store(i, j0, scaled):
            width = scaled.shape[1]
            result = staged("result", width)
            nc.scalar.activation(result[:], scaled[:], IDENT, bias=bias[:, i : i + 1])
            nc.sync.dma_start(out[i * P : (i + 1) * P, j0 : j0 + width], result[:])

        gather_codes(0, 0, CHUNKS, "v_codes0")
        round_down(nc.scalar.copy, 0, 0, P, 0, PACK)
        quantize_down(0, 0, PACK)
        gather_ts(0, 1, "down_bf0")
        for i, c in early:
            w4_pass(i, *span(c), 0)
        for s in range(SUBS):
            for t in range(PACK):
                h_pass(0, s, 0, t)
        for c in range(EARLY_CHUNKS):
            gather_codes(1, c, c + 1, "v_codes1%d" % c)
        for i, c in early:
            w4_pass(i, *span(c), 1)

        round_down(nc.scalar.copy, 1, 0, P // 2, 0, PACK)
        round_down(nc.vector.tensor_copy, 1, P // 2, P, 0, PACK // 2)
        round_down(nc.scalar.copy, 1, P // 2, P, PACK // 2, PACK)
        for t in range(PACK):
            quantize_down(1, t, t + 1)
        for t in range(PACK):
            for s in range(SUBS // 2):
                h_pass(0, s, 1, t)
        for s in range(SUBS // 2, SUBS):
            for t in range(PACK):
                h_pass(0, s, 1, t)
        for s in range(SUBS):
            round_h(0, s)
        gather_codes(1, EARLY_CHUNKS, CHUNKS, "down_bf1")

        last = CHUNKS - 1
        round_up(nc.vector.tensor_copy, 0, EARLY_ROWS, "up_bf0")
        quantize_up(0, EARLY_ROWS)
        quantize_h(0)
        gather_ts(1, EARLY_CHUNKS, "h_bf0")
        make_h(1, 0, SUBS)
        early_scaled = {}

        def close_early(c, tag):
            both = keep.tile([P, EARLY_ROWS, CHUNK], F32, name="early_scaled", tag=tag, align_bytes=ALIGN)
            for i in range(EARLY_ROWS):
                up_pass(i, *span(c))
                scale(i, *span(c), both[:, i, :])
                early_scaled[i, c] = both[:, i, :]

        quantize_h(1)
        spent = keep.tile([P, 3, CHUNK], F32, name="spent", tag="h_bf1", align_bytes=ALIGN)
        ts_cols[last] = spent[:, 0, :]
        nc.vector.tensor_copy(ts_cols[last], ts_all[:].indirect(entries(last, CHUNKS)))
        make_h(last, 0, SUBS)
        quantize_h(last)
        close_early(0, "early_scaled")
        rounded = spent[:, 1, :].bitcast(BF16).rearrange("p (n t) -> p n t", t=PACK)
        round_up_into(nc.scalar.copy, EARLY_ROWS, 2 * EARLY_ROWS, rounded)
        for i in (2, 3):
            quantize_up(i, i + 1, rounded[:, (i - 2) * P : (i - 1) * P, :])
        close_early(1, "h_bf2")
        for i in range(EARLY_ROWS):
            w4_passes(i, *span(last))

        for i, c in early:
            store(i, c * CHUNK, early_scaled[i, c])
        for c in range(EARLY_CHUNKS):
            w4_passes(EARLY_ROWS, *span(c))
        for i in range(EARLY_ROWS):
            up_pass(i, *span(last))
            scaled = staged("scaled", CHUNK)
            scale(i, *span(last), scaled[:])
            store(i, S - CHUNK, scaled)

        def open_and_close(i, j0, j1):
            if (i, j0) not in y_bank:
                w4_passes(i, j0, j1)
            up_pass(i, j0, j1)

        def leave(i, j0, j1, width):
            scaled = staged("scaled", j1 - j0)
            for j in range(j0, j1, width):
                open_and_close(i, j, j + width)
                scale(i, j, j + width, scaled[:, j - j0 : j - j0 + width])
            store(i, j0, scaled)

        def leave_by_gpsimd(i, c):
            open_and_close(i, *span(c))
            sums = keep.tile([P, CHUNK], F32, name="sums%d" % i, align_bytes=ALIGN)
            nc.scalar.copy(sums[:], y_bank[i, c * CHUNK][:])
            nc.gpsimd.tensor_tensor(spent[:, 1, :], sums[:], ts_cols[c], MULT)
            result = keep.tile([P, CHUNK], F32, name="result%d" % i, align_bytes=ALIGN)
            nc.gpsimd.tensor_scalar(result[:], spent[:, 1, :], 1.0, bias[:, i : i + 1], MULT, ADD)
            nc.gpsimd.dma_start(out[i * P : (i + 1) * P, slice(*span(c))], result[:])

        leave(2, 0, last * CHUNK, CHUNK)
        row2 = staged("scaled", CHUNK)
        open_and_close(2, *span(last))
        scale(2, *span(last), row2[:])
        round_up_into(gpsimd_round, ROWS // 2, ROWS, spent[:, 1:3, :].rearrange("p a w -> p (a w)").bitcast(BF16).rearrange("p (n t) -> p n t", t=PACK))
        quantize_up(ROWS // 2, ROWS)
        leave_by_gpsimd(3, 0)
        store(2, last * CHUNK, row2)
        leave(3, CHUNK, S, CHUNK)
        leave_by_gpsimd(4, 0)
        for c in range(1, CHUNKS):
            leave(4, *span(c), CHUNK)
        for i in (5, 6):
            for c in range(CHUNKS):
                leave(i, *span(c), CHUNK)
        leave(7, *span(0), CHUNK)
        for j0 in range(CHUNK, S, CHUNK // 2):
            leave(7, j0, j0 + CHUNK // 2, CHUNK // 2)
